import numpy as np
import ml_dtypes


def mxq(x, axis, fmt="e4m3"):
    dtype, down = {"e4m3": (ml_dtypes.float8_e4m3fn, 7), "e5m2": (ml_dtypes.float8_e5m2, 14)}[fmt]
    v = np.moveaxis(np.asarray(x, np.float32).astype(ml_dtypes.bfloat16).astype(np.float64), axis, -1)
    blocks = v.reshape(v.shape[:-1] + (-1, 32))
    amax = np.abs(blocks).max(-1, keepdims=True)
    byte = np.maximum(np.where(amax > 0, np.frexp(amax)[1] - 1 + 127, 0) - down, 1)
    scale = np.exp2(byte - 127.0)
    codes = (blocks / scale).astype(np.float32).astype(dtype).astype(np.float64)
    return np.moveaxis((codes * scale).reshape(v.shape), -1, axis)


WIDE = False


def mx_kscale(k):
    if not WIDE:
        return np.ones(k)
    levels = np.array([10, -10, 5, -5, 0])
    if k % 512:
        return np.exp2(np.random.permutation(np.resize(levels, k // 32))).repeat(32)
    a = np.empty((k // 512, 16))
    for p in range(k // 512):
        a[p, :8] = np.random.permutation(np.resize(levels, 8))
        for g in range(8):
            far = levels[np.abs(levels - a[p, g]) >= 10]
            a[p, g + 8] = far[np.random.randint(len(far))]
    return np.exp2(a.ravel()).repeat(32)


def f64(x):
    return np.asarray(x).astype(np.float64)


def striped(idx):
    return np.tile(idx.reshape(-1, 16).T, (8, 1)).astype(np.uint16)


def unstriped(offs):
    return offs[:16].T.reshape(-1).astype(np.int64)


E2M1 = np.array([0.0, 0.5, 1.0, 1.5, 2.0, 3.0, 4.0, 6.0, -0.0, -0.5, -1.0, -1.5, -2.0, -3.0, -4.0, -6.0])


def pack_weight(w, fmt):
    k, n = w.shape
    w = f64(np.asarray(w, np.float32).astype(ml_dtypes.bfloat16)).reshape(k // 32, 32, n)
    amax = np.abs(w).max(1)
    if fmt == "e4m3":
        byte = np.frexp(amax)[1] - 1 + 127 - 7
    else:
        mant, ex = np.frexp(amax / 6.0)
        byte = np.where(mant > 0.5, ex, ex - 1) + 127
    byte = np.clip(np.where(amax > 0, byte, 1), 1, 254)
    scaled = (w * np.exp2(127.0 - byte)[:, None, :]).reshape(k, n).astype(np.float32)
    by_word = np.ascontiguousarray(scaled.reshape(k // 512, 128, 4, n).transpose(0, 1, 3, 2))
    if fmt == "e4m3":
        words = by_word.astype(ml_dtypes.float8_e4m3fn).view(np.uint8)
    else:
        c = by_word.astype(ml_dtypes.float4_e2m1fn).view(np.uint8) & 0xF
        words = (c[..., 0::2] | (c[..., 1::2] << 4)).reshape(k // 512, 128, 2 * n)
    return np.ascontiguousarray(words), np.ascontiguousarray(byte.astype(np.uint8).reshape(k // 512, 16, n))


def unpack_weight(words, scales, fmt):
    g, _, n = scales.shape
    words = np.ascontiguousarray(words).reshape(g, 128, n, -1)
    if fmt == "e4m3":
        vals = words.view(ml_dtypes.float8_e4m3fn).astype(np.float64)
    else:
        nib = np.empty((g, 128, n, 4), np.uint8)
        nib[..., 0::2] = words & 0xF
        nib[..., 1::2] = words >> 4
        vals = E2M1[nib]
    vals = vals * np.repeat(np.exp2(scales.astype(np.float64) - 127.0), 8, axis=1)[..., None]
    return vals.transpose(0, 1, 3, 2).reshape(g * 512, n)


K, T, E, C = 512, 512, 8, 128


def deal():
    first = np.random.permutation(np.repeat(np.arange(E), T // E))
    second = (first + 1 + np.random.permutation(np.repeat(np.arange(E - 1), -(-T // (E - 1)))[:T])) % E
    while np.bincount(second, minlength=E).max() != T // E:
        load = np.bincount(second, minlength=E); hi, lo = int(load.argmax()), int(load.argmin())
        t = np.flatnonzero((second == hi) & (first != lo))[0]; second[t] = lo
    slot_token = np.empty(E * C, np.int64); pos = np.empty((2, T), np.int64); fill = np.zeros(E, np.int64)
    place = np.stack([np.random.permutation(C) for _ in range(E)])
    for r, deal in enumerate((first, second)):
        for t in np.random.permutation(T):
            e = deal[t]; j = e * C + place[e, fill[e]]; fill[e] += 1; slot_token[j] = t; pos[r, t] = j
    g = np.random.uniform(0.2, 0.8, T)
    return slot_token, pos, np.stack([g, 1.0 - g])


def by_expert(wq, xq):
    return np.concatenate([wq[e].T @ xq[:, e * C:(e + 1) * C] for e in range(E)], axis=1)


def setup_inputs():
    n = np.random.standard_normal
    s = mx_kscale(K)
    slots1, pos1, g1 = deal()
    slots2, pos2, g2 = deal()
    x = pack_weight(n((K, T)) * s[:, None], "e4m3")
    w = [pack_weight(m, "e2m1") for m in n((E, K, K)) / np.sqrt(K) / s[None, :, None] * s]
    return {
        "x_words": x[0],
        "x_scales": x[1],
        "w_words": np.stack([m[0] for m in w]),
        "w_scales": np.stack([m[1] for m in w]),
        "gate1": (np.stack([np.tile(r, (128, 1)) for r in g1])).astype(np.float32),
        "gate2": (np.stack([np.tile(r, (128, 1)) for r in g2])).astype(np.float32),
        "offs": striped(slots1),
        "pos1": striped(pos1[0]),
        "pos2": striped(pos1[1]),
        "offs2": striped(slots2),
        "pos3": striped(pos2[0]),
        "pos4": striped(pos2[1]),
    }


def reference(x_words, x_scales, w_words, w_scales, gate1, gate2, offs, pos1, pos2, offs2, pos3, pos4):
    w = np.stack([unpack_weight(w_words[e], w_scales[e], "e2m1") for e in range(E)])
    idx, idx2 = unstriped(offs), unstriped(offs2)
    y = by_expert(w, unpack_weight(x_words, x_scales, "e4m3")[:, idx])
    c = sum(f64(gate1[r, :1]) * y[:, unstriped(p)] for r, p in enumerate((pos1, pos2)))
    z = by_expert(w, mxq(c[:, idx2], 0, "e4m3"))
    out = sum(f64(gate2[r, :1]) * z[:, unstriped(p)] for r, p in enumerate((pos3, pos4)))
    return out

@@ -1,0 +1,243 @@
+from contextlib import ExitStack
+
+import concourse.mybir as mybir
+from concourse.masks import make_identity
+
+K, T, E, C = 512, 512, 8, 128
+S = E * C
+P = 128
+PACK = 4
+FLOPS = 2 * 2 * K * K * S
+
+F32 = mybir.dt.float32
+BF16 = mybir.dt.bfloat16
+I32 = mybir.dt.int32
+U32 = mybir.dt.uint32
+U16 = mybir.dt.uint16
+U8 = mybir.dt.uint8
+FP8X4 = mybir.dt.float8_e4m3fn_x4
+FP4X4 = mybir.dt.float4_e2m1fn_x4
+MULT = mybir.AluOpType.mult
+ADD = mybir.AluOpType.add
+COPY = mybir.ActivationFunctionType.Copy
+
+
+def cols(first, last):
+    return slice(first // 16, last // 16)
+
+
+def tile_moe_uni_none_kernel(
+    tc, x_words, x_scales, w_words, w_scales, gate1, gate2, offs, pos1, pos2, offs2, pos3, pos4, out
+):
+    nc = tc.nc
+    with ExitStack() as ctx:
+        lists = ctx.enter_context(tc.tile_pool(name="lists", bufs=1))
+        held = ctx.enter_context(tc.tile_pool(name="held", bufs=1))
+        psum = ctx.enter_context(tc.psum_pool(name="psum", bufs=1))
+
+        offs_sb = lists.tile([P, S // 16], U16, name="offs_sb")
+        offs2_sb = lists.tile([P, S // 16], U16, name="offs2_sb")
+        pos_sb = [lists.tile([P, T // 16], U16, name="pos%d_sb" % r) for r in range(4)]
+
+        xw = held.tile([P, T], I32, name="xw", align_bytes=64)
+        xs = held.tile([P, T // 4], I32, name="xs", align_bytes=64)
+        ww = held.tile([P, E * 2 * K // 4], I32, name="ww", align_bytes=64)
+        ws = held.tile([P, E * K // 4], I32, name="ws", align_bytes=64)
+        gates = [held.tile([P, 2, T], F32, name="gate%d_sb" % s) for s in range(2)]
+        ident = held.tile([P, P], F32, name="ident")
+        banks = [psum.tile([P, 512], F32, name="bank%d" % b) for b in range(8)]
+
+        nc.gpsimd.memset(xs[:], 0)
+        nc.gpsimd.memset(ws[:, :512], 0)
+        nc.vector.memset(ws[:, 512:], 0)
+        make_identity(nc, ident[:])
+
+        nc.sync.dma_start(offs_sb[:], offs)
+        nc.sync.dma_start(xw[:], x_words[0].rearrange("p t d -> p (t d)").bitcast(I32))
+        for r in range(4):
+            nc.sync.dma_start(xs[r:P:32, :], x_scales[0, r:16:4, :].bitcast(I32))
+        ww3 = ww[:].rearrange("p (e n) -> p e n", e=E)
+        w_rows = w_words[:, 0, :, :].rearrange("e p n -> p e n").bitcast(I32)
+        nc.sync.dma_start(ww3[:, :2, :], w_rows[:, :2, :])
+        for r in range(4):
+            nc.sync.dma_start(
+                ws[r:P:32, :].rearrange("q (e n) -> q e n", e=E),
+                w_scales[:, 0, r:16:4, :].rearrange("e q n -> q e n").bitcast(I32),
+            )
+        nc.sync.dma_start(ww3[:, 2:, :], w_rows[:, 2:, :])
+        nc.sync.dma_start(pos_sb[0][:], pos1)
+        nc.sync.dma_start(pos_sb[1][:], pos2)
+        nc.sync.dma_start(gates[0][:], gate1.rearrange("r p t -> p r t"))
+        nc.sync.dma_start(offs2_sb[:], offs2)
+        nc.sync.dma_start(pos_sb[2][:], pos3)
+        nc.sync.dma_start(pos_sb[3][:], pos4)
+        nc.sync.dma_start(gates[1][:], gate2.rearrange("r p t -> p r t"))
+
+        w_bytes = ww[:].bitcast(U8)
+        w_scale = ws[:].bitcast(U8)
+
+        xg = held.tile([P, S], U32, name="xg", align_bytes=64)
+        xgs = held.tile([P, S], U8, name="xgs", align_bytes=64)
+        for s0, s1 in ((0, 128), (128, 256), (256, 512), (512, 768), (768, 896), (896, 1024)):
+            nc.vector.tensor_copy(xg[:, s0:s1], xw[:].bitcast(U32).indirect(offs_sb[:, cols(s0, s1)]))
+            nc.vector.tensor_copy(xgs[:, s0:s1], xs[:].bitcast(U8).indirect(offs_sb[:, cols(s0, s1)]))
+
+        ys = held.tile([P, E, PACK, P], F32, name="ys")
+        y = [held.tile([P, S], F32, name="y%d" % d) for d in range(PACK)]
+
+        def multiply1(e):
+            bank = banks[e % 3]
+            nc.tensor.matmul_mx(
+                bank[:],
+                lhsT=xg[:, e * C : (e + 1) * C].bitcast(FP8X4),
+                lhsT_scale=xgs[:, e * C : (e + 1) * C],
+                rhs=w_bytes[:, e * 2 * K : (e + 1) * 2 * K].bitcast(FP4X4),
+                rhs_scale=w_scale[:, e * K : (e + 1) * K],
+                start=True,
+                stop=True,
+            )
+            return bank[:].rearrange("s (p d) -> s d p", d=PACK)
+
+        def turn(d, e0, e1, bank):
+            for e in range(e0, e1):
+                nc.tensor.transpose(bank[:, (e - e0) * C : (e - e0 + 1) * C], ys[:, e, d, :], ident[:])
+            return bank[:, : (e1 - e0) * C]
+
+        for e in range(E - 1):
+            sums = multiply1(e)
+            if e == 0:
+                nc.scalar.activation(ys[:, e, :, :], sums, COPY)
+            else:
+                nc.scalar.copy(ys[:, e, :, :], sums)
+            if e == 3:
+                turned_first = turn(0, 0, 4, banks[3])
+        nc.vector.tensor_copy(y[0][:, : 4 * C], turned_first)
+        sums = multiply1(E - 1)
+        nc.vector.tensor_copy(ys[:, E - 1, 0, :], sums[:, 0, :])
+        nc.scalar.copy(ys[:, E - 1, 1:, :], sums[:, 1:, :])
+        nc.vector.tensor_copy(y[0][:, 4 * C : 7 * C], turn(0, 4, 7, banks[4]))
+        nc.scalar.copy(y[0][:, 7 * C :], turn(0, 7, 8, banks[5]))
+        for d, (b0, b1) in ((1, (6, 7)), (2, (3, 4)), (3, (5, 6))):
+            nc.scalar.copy(y[d][:, : 4 * C], turn(d, 0, 4, banks[b0]))
+            nc.scalar.copy(y[d][:, 4 * C :], turn(d, 4, 8, banks[b1]))
+
+        def weigh(dst, rows, step, r, t0, t1):
+            nc.vector.tensor_tensor(
+                dst[:, t0:t1], rows[:].indirect(pos_sb[2 * step + r][:, cols(t0, t1)]), gates[step][:, r, t0:t1], MULT
+            )
+
+        prod = [held.tile([P, PACK, T], F32, name="prod%d" % r) for r in range(2)]
+        c_plane = [held.tile([P, T], BF16, name="c%d" % d) for d in range(2)]
+        c_pair = held.tile([P, T, 2], BF16, name="c_pair")
+
+        def add_plane(d):
+            nc.vector.tensor_tensor(c_plane[d][:], prod[0][:, d, :], prod[1][:, d, :], ADD)
+
+        weigh(prod[0][:, 0, :], y[0], 0, 0, 0, T)
+        weigh(prod[1][:, 0, :], y[0], 0, 1, 0, T)
+        weigh(prod[0][:, 1, :], y[1], 0, 0, 0, T)
+        add_plane(0)
+        weigh(prod[1][:, 1, :], y[1], 0, 1, 0, T)
+        weigh(prod[0][:, 2, :], y[2], 0, 0, 0, T)
+        add_plane(1)
+        weigh(prod[1][:, 2, :], y[2], 0, 1, 0, T)
+        weigh(prod[0][:, 3, :], y[3], 0, 0, 0, T)
+        weigh(prod[1][:, 3, :], y[3], 0, 1, 0, T // 2)
+        weigh(prod[1][:, 3, :], y[3], 0, 1, T // 2, T)
+        for t0 in (0, T // 2):
+            tok = slice(t0, t0 + T // 2)
+            nc.vector.tensor_tensor(
+                c_pair[:, tok, :],
+                prod[0][:, 2:, tok].rearrange("p d t -> p t d"),
+                prod[1][:, 2:, tok].rearrange("p d t -> p t d"),
+                ADD,
+            )
+
+        STAGED = 6 * C
+        staged = held.tile([P, 2, STAGED, 2], BF16, name="staged", align_bytes=64)
+        grouped = held.tile([P, S, PACK], BF16, name="grouped", align_bytes=64)
+        codes = held.tile([P, S], U32, name="codes", align_bytes=64)
+        scales = held.tile([P, S], U8, name="scales", align_bytes=64)
+        for d in range(2):
+            for e in range(E):
+                slots = slice(e * C, (e + 1) * C)
+                dst = staged[:, 0, slots, d] if (e + 1) * C <= STAGED else grouped[:, slots, d]
+                nc.scalar.activation(dst, c_plane[d][:].indirect(offs2_sb[:, cols(e * C, (e + 1) * C)]), COPY)
+
+        pair_window = c_pair[:].rearrange("p t d -> p (t d)").bitcast(U32)
+        staged_flat = staged[:].rearrange("p u s d -> p (u s d)")
+        grouped_flat = grouped[:].rearrange("p s d -> p (s d)")
+
+        def gather_pairs(s0, s1):
+            if s1 <= STAGED:
+                dst = staged_flat.bitcast(U32)[:, STAGED + s0 : STAGED + s1]
+            else:
+                dst = grouped_flat.bitcast(U32)[:, 2 * s0 + 1 : 2 * s1 : 2]
+            nc.vector.tensor_copy(dst, pair_window.indirect(offs2_sb[:, cols(s0, s1)]))
+            if s1 <= STAGED:
+                nc.scalar.copy(
+                    grouped_flat.bitcast(F32).rearrange("p (s u) -> p s u", u=2)[:, s0:s1, :],
+                    staged_flat.bitcast(F32).rearrange("p (u s) -> p s u", u=2)[:, s0:s1, :],
+                )
+
+        def quantize(s0, s1):
+            nc.vector.quantize_mx(
+                out=codes[:, s0:s1].bitcast(FP8X4), scales=scales[:, s0:s1], in_=grouped_flat[:, PACK * s0 : PACK * s1]
+            )
+
+        gather_pairs(0, 256)
+        gather_pairs(256, 512)
+        gather_pairs(512, 768)
+        quantize(0, 256)
+        gather_pairs(768, 1024)
+        quantize(256, 512)
+        quantize(512, 768)
+        quantize(768, 1024)
+
+        z = [held.tile([P, S], F32, name="z%d" % t) for t in range(PACK)]
+
+        def multiply2(t, e0, e1, bank):
+            for e in range(e0, e1):
+                col = e * K + t * P
+                nc.tensor.matmul_mx(
+                    bank[:, (e - e0) * C : (e - e0 + 1) * C],
+                    lhsT=w_bytes[:, 2 * col : 2 * (col + P)].bitcast(FP4X4),
+                    lhsT_scale=w_scale[:, col : col + P],
+                    rhs=codes[:, e * C : (e + 1) * C].bitcast(FP8X4),
+                    rhs_scale=scales[:, e * C : (e + 1) * C],
+                    start=True,
+                    stop=True,
+                )
+            nc.scalar.copy(z[t][:, e0 * C : e1 * C], bank[:, : (e1 - e0) * C])
+
+        multiply2(0, 0, 4, banks[0])
+        multiply2(0, 4, 6, banks[4])
+        multiply2(0, 6, 8, banks[5])
+        for t, (b0, b1) in ((1, (1, 6)), (2, (2, 7)), (3, (3, 0))):
+            multiply2(t, 0, 4, banks[b0])
+            multiply2(t, 4, 8, banks[b1])
+
+        prod2 = [held.tile([P, PACK, T], F32, name="prod2_%d" % r) for r in range(2)]
+        result = held.tile([P, PACK, T], F32, name="result")
+
+        def finish(t, t0, t1):
+            nc.vector.tensor_tensor(result[:, t, t0:t1], prod2[0][:, t, t0:t1], prod2[1][:, t, t0:t1], ADD)
+            nc.sync.dma_start(out[t * P : (t + 1) * P, t0:t1], result[:, t, t0:t1])
+
+        weigh(prod2[0][:, 0, :], z[0], 1, 0, 0, T)
+        weigh(prod2[1][:, 0, :], z[0], 1, 1, 0, T)
+        weigh(prod2[0][:, 1, :], z[1], 1, 0, 0, T)
+        finish(0, 0, T)
+        weigh(prod2[1][:, 1, :], z[1], 1, 1, 0, T)
+        weigh(prod2[0][:, 2, :], z[2], 1, 0, 0, T)
+        finish(1, 0, T)
+        weigh(prod2[1][:, 2, :], z[2], 1, 1, 0, T)
+        weigh(prod2[0][:, 3, :], z[3], 1, 0, 0, 256)
+        finish(2, 0, T)
+        weigh(prod2[1][:, 3, :], z[3], 1, 1, 0, 256)
+        weigh(prod2[0][:, 3, :], z[3], 1, 0, 256, 512)
+        finish(3, 0, 256)
+        weigh(prod2[1][:, 3, :], z[3], 1, 1, 256, 384)
+        weigh(prod2[1][:, 3, :], z[3], 1, 1, 384, 512)
+        finish(3, 256, 384)
+        finish(3, 384, 512)

@@ -33,6 +33,7 @@ def tile_moe_uni_none_kernel(
     with ExitStack() as ctx:
         lists = ctx.enter_context(tc.tile_pool(name="lists", bufs=1))
         held = ctx.enter_context(tc.tile_pool(name="held", bufs=1))
+        ring = ctx.enter_context(tc.tile_pool(name="ring", bufs=4))
         psum = ctx.enter_context(tc.psum_pool(name="psum", bufs=1))
 
         offs_sb = lists.tile([P, S // 16], U16, name="offs_sb")
@@ -64,7 +65,8 @@ def tile_moe_uni_none_kernel(
                 ws[r:P:32, :].rearrange("q (e n) -> q e n", e=E),
                 w_scales[:, 0, r:16:4, :].rearrange("e q n -> q e n").bitcast(I32),
             )
-        nc.sync.dma_start(ww3[:, 2:, :], w_rows[:, 2:, :])
+        nc.sync.dma_start(ww3[:, 2:4, :], w_rows[:, 2:4, :])
+        nc.sync.dma_start(ww3[:, 4:, :], w_rows[:, 4:, :])
         nc.sync.dma_start(pos_sb[0][:], pos1)
         nc.sync.dma_start(pos_sb[1][:], pos2)
         nc.sync.dma_start(gates[0][:], gate1.rearrange("r p t -> p r t"))
@@ -76,20 +78,34 @@ def tile_moe_uni_none_kernel(
         w_bytes = ww[:].bitcast(U8)
         w_scale = ws[:].bitcast(U8)
 
-        xg = held.tile([P, S], U32, name="xg", align_bytes=64)
         xgs = held.tile([P, S], U8, name="xgs", align_bytes=64)
-        for s0, s1 in ((0, 128), (128, 256), (256, 512), (512, 768), (768, 896), (896, 1024)):
-            nc.vector.tensor_copy(xg[:, s0:s1], xw[:].bitcast(U32).indirect(offs_sb[:, cols(s0, s1)]))
+
+        def gather_words(e):
+            xg = ring.tile([P, C], U32, name="xg", align_bytes=64)
+            nc.vector.tensor_copy(xg[:], xw[:].bitcast(U32).indirect(offs_sb[:, cols(e * C, (e + 1) * C)]))
+            return xg
+
+        def gather_scales(s0, s1):
             nc.vector.tensor_copy(xgs[:, s0:s1], xs[:].bitcast(U8).indirect(offs_sb[:, cols(s0, s1)]))
 
-        ys = held.tile([P, E, PACK, P], F32, name="ys")
+        whole = held.tile([P, 3, PACK, P], F32, name="whole")
+        early = held.tile([P, E - 3, 2, P], F32, name="early")
+        last_early = held.tile([P, P], F32, name="last_early", tag="shared")
+
+        def staged_sums(e, d):
+            if (e, d) == (E - 1, 0):
+                return last_early[:]
+            if e < 3:
+                return whole[:, e, d, :]
+            return early[:, e - 3, d, :] if d < 2 else late_rest[:, e - 3, d - 2, :]
+
         y = [held.tile([P, S], F32, name="y%d" % d) for d in range(PACK)]
 
-        def multiply1(e):
-            bank = banks[e % 3]
+        def multiply1(e, xg):
+            bank = banks[e]
             nc.tensor.matmul_mx(
                 bank[:],
-                lhsT=xg[:, e * C : (e + 1) * C].bitcast(FP8X4),
+                lhsT=xg[:].bitcast(FP8X4),
                 lhsT_scale=xgs[:, e * C : (e + 1) * C],
                 rhs=w_bytes[:, e * 2 * K : (e + 1) * 2 * K].bitcast(FP4X4),
                 rhs_scale=w_scale[:, e * K : (e + 1) * K],
@@ -100,26 +116,36 @@ def tile_moe_uni_none_kernel(
 
         def turn(d, e0, e1, bank):
             for e in range(e0, e1):
-                nc.tensor.transpose(bank[:, (e - e0) * C : (e - e0 + 1) * C], ys[:, e, d, :], ident[:])
+                nc.tensor.transpose(bank[:, (e - e0) * C : (e - e0 + 1) * C], staged_sums(e, d), ident[:])
             return bank[:, : (e1 - e0) * C]
 
-        for e in range(E - 1):
-            sums = multiply1(e)
-            if e == 0:
-                nc.scalar.activation(ys[:, e, :, :], sums, COPY)
-            else:
-                nc.scalar.copy(ys[:, e, :, :], sums)
-            if e == 3:
-                turned_first = turn(0, 0, 4, banks[3])
-        nc.vector.tensor_copy(y[0][:, : 4 * C], turned_first)
-        sums = multiply1(E - 1)
-        nc.vector.tensor_copy(ys[:, E - 1, 0, :], sums[:, 0, :])
-        nc.scalar.copy(ys[:, E - 1, 1:, :], sums[:, 1:, :])
-        nc.vector.tensor_copy(y[0][:, 4 * C : 7 * C], turn(0, 4, 7, banks[4]))
-        nc.scalar.copy(y[0][:, 7 * C :], turn(0, 7, 8, banks[5]))
-        for d, (b0, b1) in ((1, (6, 7)), (2, (3, 4)), (3, (5, 6))):
-            nc.scalar.copy(y[d][:, : 4 * C], turn(d, 0, 4, banks[b0]))
-            nc.scalar.copy(y[d][:, 4 * C :], turn(d, 4, 8, banks[b1]))
+        sums = []
+        for e in range(E):
+            xg = gather_words(e)
+            if e < 2:
+                gather_scales(e * C, (e + 1) * C)
+            elif e % 2 == 0:
+                gather_scales(e * C, (e + 2) * C)
+            sums.append(multiply1(e, xg))
+        nc.scalar.activation(whole[:, 0, :, :], sums[0], COPY)
+        nc.scalar.copy(whole[:, 1, :, :], sums[1])
+        nc.scalar.copy(whole[:, 2, :, :], sums[2])
+        for e in range(3, E - 1):
+            nc.scalar.copy(early[:, e - 3, :, :], sums[e][:, :2, :])
+        nc.scalar.copy(last_early[:], sums[E - 1][:, 0, :])
+        nc.vector.tensor_copy(y[0][:, : 4 * C], turn(0, 0, 4, banks[0]))
+        nc.scalar.copy(y[0][:, 4 * C : 6 * C], turn(0, 4, 6, banks[1]))
+        nc.vector.tensor_copy(y[0][:, 6 * C :], turn(0, 6, 8, banks[2]))
+        nc.scalar.copy(staged_sums(E - 1, 1), sums[E - 1][:, 1, :])
+        late_rest = held.tile([P, E - 3, 2, P], F32, name="late_rest", tag="shared")
+        nc.scalar.copy(late_rest[:, 0, :, :], sums[3][:, 2:, :])
+        nc.scalar.copy(y[1][:, : 4 * C], turn(1, 0, 4, banks[2]))
+        nc.scalar.copy(y[1][:, 4 * C :], turn(1, 4, 8, banks[3]))
+        for e in range(4, E):
+            nc.scalar.copy(late_rest[:, e - 3, :, :], sums[e][:, 2:, :])
+        for d in range(2, PACK):
+            nc.scalar.copy(y[d][:, : 4 * C], turn(d, 0, 4, banks[2 * d]))
+            nc.scalar.copy(y[d][:, 4 * C :], turn(d, 4, 8, banks[2 * d + 1]))
 
         def weigh(dst, rows, step, r, t0, t1):
             nc.vector.tensor_tensor(
@@ -192,7 +218,8 @@ def tile_moe_uni_none_kernel(
         gather_pairs(768, 1024)
         quantize(256, 512)
         quantize(512, 768)
-        quantize(768, 1024)
+        quantize(768, 896)
+        quantize(896, 1024)
 
         z = [held.tile([P, S], F32, name="z%d" % t) for t in range(PACK)]
 
@@ -212,10 +239,15 @@ def tile_moe_uni_none_kernel(
 
         multiply2(0, 0, 4, banks[0])
         multiply2(0, 4, 6, banks[4])
-        multiply2(0, 6, 8, banks[5])
-        for t, (b0, b1) in ((1, (1, 6)), (2, (2, 7)), (3, (3, 0))):
-            multiply2(t, 0, 4, banks[b0])
-            multiply2(t, 4, 8, banks[b1])
+        multiply2(0, 6, 7, banks[5])
+        multiply2(0, 7, 8, banks[6])
+
+        def multiply_plane(t):
+            multiply2(t, 0, 4, banks[0])
+            multiply2(t, 4, 8, banks[6])
+
+        for t in range(1, PACK):
+            multiply_plane(t)
 
         prod2 = [held.tile([P, PACK, T], F32, name="prod2_%d" % r) for r in range(2)]
         result = held.tile([P, PACK, T], F32, name="result")
@@ -224,20 +256,40 @@ def tile_moe_uni_none_kernel(
             nc.vector.tensor_tensor(result[:, t, t0:t1], prod2[0][:, t, t0:t1], prod2[1][:, t, t0:t1], ADD)
             nc.sync.dma_start(out[t * P : (t + 1) * P, t0:t1], result[:, t, t0:t1])
 
+        turned = held.tile([P, 2, T], F32, name="turned")
+
+        def finish_on_tensor(t, j0, j1, bank_sum, bank_back):
+            width = (j1 - j0) * P
+            for r in range(2):
+                for j in range(j0, j1):
+                    nc.tensor.matmul(
+                        bank_sum[:, (j - j0) * P : (j - j0 + 1) * P],
+                        lhsT=prod2[r][:, t, j * P : (j + 1) * P],
+                        rhs=ident[:],
+                        start=(r == 0 and j == j0),
+                        stop=(r == 1 and j == j1 - 1),
+                        is_transpose=True,
+                    )
+            nc.scalar.copy(turned[:, t, j0 * P : j1 * P], bank_sum[:, :width])
+            for j in range(j0, j1):
+                nc.tensor.transpose(
+                    bank_back[:, (j - j0) * P : (j - j0 + 1) * P], turned[:, t, j * P : (j + 1) * P], ident[:]
+                )
+            nc.scalar.copy(result[:, t, j0 * P : j1 * P], bank_back[:, :width])
+            nc.sync.dma_start(out[t * P : (t + 1) * P, j0 * P : j1 * P], result[:, t, j0 * P : j1 * P])
+
         weigh(prod2[0][:, 0, :], z[0], 1, 0, 0, T)
         weigh(prod2[1][:, 0, :], z[0], 1, 1, 0, T)
+        finish_on_tensor(0, 0, 4, banks[1], banks[2])
         weigh(prod2[0][:, 1, :], z[1], 1, 0, 0, T)
-        finish(0, 0, T)
         weigh(prod2[1][:, 1, :], z[1], 1, 1, 0, T)
+        finish_on_tensor(1, 0, 4, banks[3], banks[4])
         weigh(prod2[0][:, 2, :], z[2], 1, 0, 0, T)
-        finish(1, 0, T)
         weigh(prod2[1][:, 2, :], z[2], 1, 1, 0, T)
         weigh(prod2[0][:, 3, :], z[3], 1, 0, 0, 256)
         finish(2, 0, T)
         weigh(prod2[1][:, 3, :], z[3], 1, 1, 0, 256)
         weigh(prod2[0][:, 3, :], z[3], 1, 0, 256, 512)
         finish(3, 0, 256)
-        weigh(prod2[1][:, 3, :], z[3], 1, 1, 256, 384)
-        weigh(prod2[1][:, 3, :], z[3], 1, 1, 384, 512)
-        finish(3, 256, 384)
-        finish(3, 384, 512)
+        weigh(prod2[1][:, 3, :], z[3], 1, 1, 256, 512)
+        finish(3, 256, 512)

@@ -53,8 +53,8 @@ def tile_moe_uni_none_kernel(
         nc.vector.memset(ws[:, 512:], 0)
         make_identity(nc, ident[:])
 
-        nc.sync.dma_start(offs_sb[:], offs)
         nc.sync.dma_start(xw[:], x_words[0].rearrange("p t d -> p (t d)").bitcast(I32))
+        nc.sync.dma_start(offs_sb[:], offs)
         for r in range(4):
             nc.sync.dma_start(xs[r:P:32, :], x_scales[0, r:16:4, :].bitcast(I32))
         ww3 = ww[:].rearrange("p (e n) -> p e n", e=E)
@@ -90,6 +90,7 @@ def tile_moe_uni_none_kernel(
 
         whole = held.tile([P, 3, PACK, P], F32, name="whole")
         early = held.tile([P, E - 3, 2, P], F32, name="early")
+        late_free = held.tile([P, 3, 2, P], F32, name="late_free")
         last_early = held.tile([P, P], F32, name="last_early", tag="shared")
 
         def staged_sums(e, d):
@@ -97,7 +98,9 @@ def tile_moe_uni_none_kernel(
                 return last_early[:]
             if e < 3:
                 return whole[:, e, d, :]
-            return early[:, e - 3, d, :] if d < 2 else late_rest[:, e - 3, d - 2, :]
+            if d < 2:
+                return early[:, e - 3, d, :]
+            return late_free[:, e - 3, d - 2, :] if e < 6 else late_rest[:, e - 6, d - 2, :]
 
         y = [held.tile([P, S], F32, name="y%d" % d) for d in range(PACK)]
 
@@ -135,17 +138,18 @@ def tile_moe_uni_none_kernel(
         nc.scalar.copy(last_early[:], sums[E - 1][:, 0, :])
         nc.vector.tensor_copy(y[0][:, : 4 * C], turn(0, 0, 4, banks[0]))
         nc.scalar.copy(y[0][:, 4 * C : 6 * C], turn(0, 4, 6, banks[1]))
-        nc.vector.tensor_copy(y[0][:, 6 * C :], turn(0, 6, 8, banks[2]))
-        nc.scalar.copy(staged_sums(E - 1, 1), sums[E - 1][:, 1, :])
-        late_rest = held.tile([P, E - 3, 2, P], F32, name="late_rest", tag="shared")
-        nc.scalar.copy(late_rest[:, 0, :, :], sums[3][:, 2:, :])
+        nc.scalar.copy(y[0][:, 6 * C :], turn(0, 6, 8, banks[2]))
+        nc.vector.tensor_copy(staged_sums(E - 1, 1), sums[E - 1][:, 1, :])
+        for e in range(3, 6):
+            nc.vector.tensor_copy(late_free[:, e - 3, :, :], sums[e][:, 2:, :])
+        late_rest = held.tile([P, 2, 2, P], F32, name="late_rest", tag="shared")
+        nc.scalar.copy(late_rest[:, 0, :, :], sums[6][:, 2:, :])
         nc.scalar.copy(y[1][:, : 4 * C], turn(1, 0, 4, banks[2]))
-        nc.scalar.copy(y[1][:, 4 * C :], turn(1, 4, 8, banks[3]))
-        for e in range(4, E):
-            nc.scalar.copy(late_rest[:, e - 3, :, :], sums[e][:, 2:, :])
-        for d in range(2, PACK):
-            nc.scalar.copy(y[d][:, : 4 * C], turn(d, 0, 4, banks[2 * d]))
-            nc.scalar.copy(y[d][:, 4 * C :], turn(d, 4, 8, banks[2 * d + 1]))
+        nc.scalar.copy(y[1][:, 4 * C :], turn(1, 4, 8, banks[6]))
+        nc.scalar.copy(late_rest[:, 1, :, :], sums[7][:, 2:, :])
+        for d, (b0, b1) in ((2, (7, 2)), (3, (6, 7))):
+            nc.scalar.copy(y[d][:, : 4 * C], turn(d, 0, 4, banks[b0]))
+            nc.scalar.copy(y[d][:, 4 * C :], turn(d, 4, 8, banks[b1]))
 
         def weigh(dst, rows, step, r, t0, t1):
             nc.vector.tensor_tensor(
@@ -156,13 +160,31 @@ def tile_moe_uni_none_kernel(
         c_plane = [held.tile([P, T], BF16, name="c%d" % d) for d in range(2)]
         c_pair = held.tile([P, T, 2], BF16, name="c_pair")
 
+        def add_on_tensor(dst, first, second, bank_sum, bank_back):
+            blocks = [slice(j * P, (j + 1) * P) for j in range(T // P)]
+            for r, src in enumerate((first, second)):
+                for j, block in enumerate(blocks):
+                    nc.tensor.matmul(
+                        bank_sum[:, block],
+                        lhsT=src[:, block],
+                        rhs=ident[:],
+                        start=(r == 0 and j == 0),
+                        stop=(r == 1 and j == len(blocks) - 1),
+                        is_transpose=True,
+                    )
+            turned = ring.tile([P, T], F32, name="turned", bufs=2)
+            nc.scalar.copy(turned[:], bank_sum[:])
+            for block in blocks:
+                nc.tensor.transpose(bank_back[:, block], turned[:, block], ident[:])
+            nc.scalar.copy(dst, bank_back[:])
+
         def add_plane(d):
             nc.vector.tensor_tensor(c_plane[d][:], prod[0][:, d, :], prod[1][:, d, :], ADD)
 
         weigh(prod[0][:, 0, :], y[0], 0, 0, 0, T)
         weigh(prod[1][:, 0, :], y[0], 0, 1, 0, T)
+        add_on_tensor(c_plane[0][:], prod[0][:, 0, :], prod[1][:, 0, :], banks[0], banks[1])
         weigh(prod[0][:, 1, :], y[1], 0, 0, 0, T)
-        add_plane(0)
         weigh(prod[1][:, 1, :], y[1], 0, 1, 0, T)
         weigh(prod[0][:, 2, :], y[2], 0, 0, 0, T)
         add_plane(1)
@@ -173,9 +195,9 @@ def tile_moe_uni_none_kernel(
         for t0 in (0, T // 2):
             tok = slice(t0, t0 + T // 2)
             nc.vector.tensor_tensor(
-                c_pair[:, tok, :],
-                prod[0][:, 2:, tok].rearrange("p d t -> p t d"),
-                prod[1][:, 2:, tok].rearrange("p d t -> p t d"),
+                c_pair[:, tok, :].rearrange("p (g i) d -> p g d i", i=4),
+                prod[0][:, 2:, tok].rearrange("p d (g i) -> p g d i", i=4),
+                prod[1][:, 2:, tok].rearrange("p d (g i) -> p g d i", i=4),
                 ADD,
             )
 
@@ -184,11 +206,12 @@ def tile_moe_uni_none_kernel(
         grouped = held.tile([P, S, PACK], BF16, name="grouped", align_bytes=64)
         codes = held.tile([P, S], U32, name="codes", align_bytes=64)
         scales = held.tile([P, S], U8, name="scales", align_bytes=64)
-        for d in range(2):
-            for e in range(E):
-                slots = slice(e * C, (e + 1) * C)
-                dst = staged[:, 0, slots, d] if (e + 1) * C <= STAGED else grouped[:, slots, d]
-                nc.scalar.activation(dst, c_plane[d][:].indirect(offs2_sb[:, cols(e * C, (e + 1) * C)]), COPY)
+        for experts in (range(6), range(6, E)):
+            for d in range(2):
+                for e in experts:
+                    slots = slice(e * C, (e + 1) * C)
+                    dst = staged[:, 0, slots, d] if (e + 1) * C <= STAGED else grouped[:, slots, d]
+                    nc.scalar.activation(dst, c_plane[d][:].indirect(offs2_sb[:, cols(e * C, (e + 1) * C)]), COPY)
 
         pair_window = c_pair[:].rearrange("p t d -> p (t d)").bitcast(U32)
         staged_flat = staged[:].rearrange("p u s d -> p (u s d)")
@@ -241,13 +264,9 @@ def tile_moe_uni_none_kernel(
         multiply2(0, 4, 6, banks[4])
         multiply2(0, 6, 7, banks[5])
         multiply2(0, 7, 8, banks[6])
-
-        def multiply_plane(t):
-            multiply2(t, 0, 4, banks[0])
-            multiply2(t, 4, 8, banks[6])
-
-        for t in range(1, PACK):
-            multiply_plane(t)
+        for t, (b0, b1) in ((1, (0, 6)), (2, (5, 0)), (3, (6, 5))):
+            multiply2(t, 0, 4, banks[b0])
+            multiply2(t, 4, 8, banks[b1])
 
         prod2 = [held.tile([P, PACK, T], F32, name="prod2_%d" % r) for r in range(2)]
         result = held.tile([P, PACK, T], F32, name="result")
@@ -256,34 +275,16 @@ def tile_moe_uni_none_kernel(
             nc.vector.tensor_tensor(result[:, t, t0:t1], prod2[0][:, t, t0:t1], prod2[1][:, t, t0:t1], ADD)
             nc.sync.dma_start(out[t * P : (t + 1) * P, t0:t1], result[:, t, t0:t1])
 
-        turned = held.tile([P, 2, T], F32, name="turned")
-
-        def finish_on_tensor(t, j0, j1, bank_sum, bank_back):
-            width = (j1 - j0) * P
-            for r in range(2):
-                for j in range(j0, j1):
-                    nc.tensor.matmul(
-                        bank_sum[:, (j - j0) * P : (j - j0 + 1) * P],
-                        lhsT=prod2[r][:, t, j * P : (j + 1) * P],
-                        rhs=ident[:],
-                        start=(r == 0 and j == j0),
-                        stop=(r == 1 and j == j1 - 1),
-                        is_transpose=True,
-                    )
-            nc.scalar.copy(turned[:, t, j0 * P : j1 * P], bank_sum[:, :width])
-            for j in range(j0, j1):
-                nc.tensor.transpose(
-                    bank_back[:, (j - j0) * P : (j - j0 + 1) * P], turned[:, t, j * P : (j + 1) * P], ident[:]
-                )
-            nc.scalar.copy(result[:, t, j0 * P : j1 * P], bank_back[:, :width])
-            nc.sync.dma_start(out[t * P : (t + 1) * P, j0 * P : j1 * P], result[:, t, j0 * P : j1 * P])
+        def finish_on_tensor(t, bank_sum, bank_back):
+            add_on_tensor(result[:, t, :], prod2[0][:, t, :], prod2[1][:, t, :], bank_sum, bank_back)
+            nc.sync.dma_start(out[t * P : (t + 1) * P, :], result[:, t, :])
 
         weigh(prod2[0][:, 0, :], z[0], 1, 0, 0, T)
         weigh(prod2[1][:, 0, :], z[0], 1, 1, 0, T)
-        finish_on_tensor(0, 0, 4, banks[1], banks[2])
+        finish_on_tensor(0, banks[1], banks[2])
         weigh(prod2[0][:, 1, :], z[1], 1, 0, 0, T)
         weigh(prod2[1][:, 1, :], z[1], 1, 1, 0, T)
-        finish_on_tensor(1, 0, 4, banks[3], banks[4])
+        finish_on_tensor(1, banks[3], banks[4])
         weigh(prod2[0][:, 2, :], z[2], 1, 0, 0, T)
         weigh(prod2[1][:, 2, :], z[2], 1, 1, 0, T)
         weigh(prod2[0][:, 3, :], z[3], 1, 0, 0, 256)

@@ -7,7 +7,18 @@ K, T, E, C = 512, 512, 8, 128
 S = E * C
 P = 128
 PACK = 4
+ROW_TILES = K // P
+BANK = 512
+PER_COLUMN = 16
+SCALE_ROWS = K // 32
+HALF_E, HALF_T = E // 2, T // 2
 FLOPS = 2 * 2 * K * K * S
+
+WHOLE, HELD = 3, 6
+LAST = E - 1
+WORD_RING = 4
+STAGED = 6
+ZEROED_BY_GPSIMD = 512
 
 F32 = mybir.dt.float32
 BF16 = mybir.dt.bfloat16
@@ -22,8 +33,12 @@ ADD = mybir.AluOpType.add
 COPY = mybir.ActivationFunctionType.Copy
 
 
-def cols(first, last):
-    return slice(first // 16, last // 16)
+def entries(first, last):
+    return slice(first // PER_COLUMN, last // PER_COLUMN)
+
+
+def slots(e0, e1):
+    return slice(e0 * C, e1 * C)
 
 
 def tile_moe_uni_none_kernel(
@@ -33,40 +48,40 @@ def tile_moe_uni_none_kernel(
     with ExitStack() as ctx:
         lists = ctx.enter_context(tc.tile_pool(name="lists", bufs=1))
         held = ctx.enter_context(tc.tile_pool(name="held", bufs=1))
-        ring = ctx.enter_context(tc.tile_pool(name="ring", bufs=4))
+        ring = ctx.enter_context(tc.tile_pool(name="ring", bufs=WORD_RING))
         psum = ctx.enter_context(tc.psum_pool(name="psum", bufs=1))
 
-        offs_sb = lists.tile([P, S // 16], U16, name="offs_sb")
-        offs2_sb = lists.tile([P, S // 16], U16, name="offs2_sb")
-        pos_sb = [lists.tile([P, T // 16], U16, name="pos%d_sb" % r) for r in range(4)]
+        offs_sb = lists.tile([P, S // PER_COLUMN], U16, name="offs_sb")
+        offs2_sb = lists.tile([P, S // PER_COLUMN], U16, name="offs2_sb")
+        pos_sb = [lists.tile([P, T // PER_COLUMN], U16, name="pos%d_sb" % (n + 1)) for n in range(4)]
 
-        xw = held.tile([P, T], I32, name="xw", align_bytes=64)
-        xs = held.tile([P, T // 4], I32, name="xs", align_bytes=64)
-        ww = held.tile([P, E * 2 * K // 4], I32, name="ww", align_bytes=64)
-        ws = held.tile([P, E * K // 4], I32, name="ws", align_bytes=64)
-        gates = [held.tile([P, 2, T], F32, name="gate%d_sb" % s) for s in range(2)]
+        x_words_sb = held.tile([P, T], I32, name="x_words_sb", align_bytes=64)
+        x_scales_sb = held.tile([P, T // 4], I32, name="x_scales_sb", align_bytes=64)
+        w_words_sb = held.tile([P, E * 2 * K // 4], I32, name="w_words_sb", align_bytes=64)
+        w_scales_sb = held.tile([P, E * K // 4], I32, name="w_scales_sb", align_bytes=64)
+        gates = [held.tile([P, 2, T], F32, name="gate%d_sb" % (step + 1)) for step in range(2)]
         ident = held.tile([P, P], F32, name="ident")
-        banks = [psum.tile([P, 512], F32, name="bank%d" % b) for b in range(8)]
+        banks = [psum.tile([P, BANK], F32, name="bank%d" % b) for b in range(8)]
 
-        nc.gpsimd.memset(xs[:], 0)
-        nc.gpsimd.memset(ws[:, :512], 0)
-        nc.vector.memset(ws[:, 512:], 0)
+        nc.gpsimd.memset(x_scales_sb[:], 0)
+        nc.gpsimd.memset(w_scales_sb[:, :ZEROED_BY_GPSIMD], 0)
+        nc.vector.memset(w_scales_sb[:, ZEROED_BY_GPSIMD:], 0)
         make_identity(nc, ident[:])
 
-        nc.sync.dma_start(xw[:], x_words[0].rearrange("p t d -> p (t d)").bitcast(I32))
+        nc.sync.dma_start(x_words_sb[:], x_words[0].rearrange("p t d -> p (t d)").bitcast(I32))
         nc.sync.dma_start(offs_sb[:], offs)
         for r in range(4):
-            nc.sync.dma_start(xs[r:P:32, :], x_scales[0, r:16:4, :].bitcast(I32))
-        ww3 = ww[:].rearrange("p (e n) -> p e n", e=E)
-        w_rows = w_words[:, 0, :, :].rearrange("e p n -> p e n").bitcast(I32)
-        nc.sync.dma_start(ww3[:, :2, :], w_rows[:, :2, :])
+            nc.sync.dma_start(x_scales_sb[r:P:32, :], x_scales[0, r:SCALE_ROWS:4, :].bitcast(I32))
+        w_words_by_expert = w_words_sb[:].rearrange("p (e n) -> p e n", e=E)
+        w_words_hbm = w_words[:, 0, :, :].rearrange("e p n -> p e n").bitcast(I32)
+        nc.sync.dma_start(w_words_by_expert[:, :2, :], w_words_hbm[:, :2, :])
         for r in range(4):
             nc.sync.dma_start(
-                ws[r:P:32, :].rearrange("q (e n) -> q e n", e=E),
-                w_scales[:, 0, r:16:4, :].rearrange("e q n -> q e n").bitcast(I32),
+                w_scales_sb[r:P:32, :].rearrange("q (e n) -> q e n", e=E),
+                w_scales[:, 0, r:SCALE_ROWS:4, :].rearrange("e q n -> q e n").bitcast(I32),
             )
-        nc.sync.dma_start(ww3[:, 2:4, :], w_rows[:, 2:4, :])
-        nc.sync.dma_start(ww3[:, 4:, :], w_rows[:, 4:, :])
+        nc.sync.dma_start(w_words_by_expert[:, 2:HALF_E, :], w_words_hbm[:, 2:HALF_E, :])
+        nc.sync.dma_start(w_words_by_expert[:, HALF_E:, :], w_words_hbm[:, HALF_E:, :])
         nc.sync.dma_start(pos_sb[0][:], pos1)
         nc.sync.dma_start(pos_sb[1][:], pos2)
         nc.sync.dma_start(gates[0][:], gate1.rearrange("r p t -> p r t"))
@@ -75,222 +90,219 @@ def tile_moe_uni_none_kernel(
         nc.sync.dma_start(pos_sb[3][:], pos4)
         nc.sync.dma_start(gates[1][:], gate2.rearrange("r p t -> p r t"))
 
-        w_bytes = ww[:].bitcast(U8)
-        w_scale = ws[:].bitcast(U8)
+        w_word_bytes = w_words_sb[:].bitcast(U8)
+        w_scale_bytes = w_scales_sb[:].bitcast(U8)
 
-        xgs = held.tile([P, S], U8, name="xgs", align_bytes=64)
+        slot_scales = held.tile([P, S], U8, name="slot_scales", align_bytes=64)
 
         def gather_words(e):
-            xg = ring.tile([P, C], U32, name="xg", align_bytes=64)
-            nc.vector.tensor_copy(xg[:], xw[:].bitcast(U32).indirect(offs_sb[:, cols(e * C, (e + 1) * C)]))
-            return xg
+            slot_words = ring.tile([P, C], U32, name="slot_words", align_bytes=64)
+            window = x_words_sb[:].bitcast(U32)
+            nc.vector.tensor_copy(slot_words[:], window.indirect(offs_sb[:, entries(e * C, (e + 1) * C)]))
+            return slot_words
 
-        def gather_scales(s0, s1):
-            nc.vector.tensor_copy(xgs[:, s0:s1], xs[:].bitcast(U8).indirect(offs_sb[:, cols(s0, s1)]))
+        def gather_scales(e0, e1):
+            window = x_scales_sb[:].bitcast(U8)
+            nc.vector.tensor_copy(slot_scales[:, slots(e0, e1)], window.indirect(offs_sb[:, entries(e0 * C, e1 * C)]))
 
-        whole = held.tile([P, 3, PACK, P], F32, name="whole")
-        early = held.tile([P, E - 3, 2, P], F32, name="early")
-        late_free = held.tile([P, 3, 2, P], F32, name="late_free")
-        last_early = held.tile([P, P], F32, name="last_early", tag="shared")
+        all_planes = held.tile([P, WHOLE, PACK, P], F32, name="all_planes")
+        low_planes = held.tile([P, E - WHOLE, 2, P], F32, name="low_planes")
+        high_planes = held.tile([P, HELD - WHOLE, 2, P], F32, name="high_planes")
+        last_plane0 = held.tile([P, P], F32, name="last_plane0", tag="after_plane0")
 
-        def staged_sums(e, d):
-            if (e, d) == (E - 1, 0):
-                return last_early[:]
-            if e < 3:
-                return whole[:, e, d, :]
+        def unturned(e, d):
+            if (e, d) == (LAST, 0):
+                return last_plane0[:]
+            if e < WHOLE:
+                return all_planes[:, e, d, :]
             if d < 2:
-                return early[:, e - 3, d, :]
-            return late_free[:, e - 3, d - 2, :] if e < 6 else late_rest[:, e - 6, d - 2, :]
+                return low_planes[:, e - WHOLE, d, :]
+            return high_planes[:, e - WHOLE, d - 2, :] if e < HELD else held_high_planes[:, e - HELD, d - 2, :]
 
         y = [held.tile([P, S], F32, name="y%d" % d) for d in range(PACK)]
 
-        def multiply1(e, xg):
-            bank = banks[e]
+        def multiply_step1(e, slot_words):
             nc.tensor.matmul_mx(
-                bank[:],
-                lhsT=xg[:].bitcast(FP8X4),
-                lhsT_scale=xgs[:, e * C : (e + 1) * C],
-                rhs=w_bytes[:, e * 2 * K : (e + 1) * 2 * K].bitcast(FP4X4),
-                rhs_scale=w_scale[:, e * K : (e + 1) * K],
+                banks[e][:],
+                lhsT=slot_words[:].bitcast(FP8X4),
+                lhsT_scale=slot_scales[:, slots(e, e + 1)],
+                rhs=w_word_bytes[:, e * 2 * K : (e + 1) * 2 * K].bitcast(FP4X4),
+                rhs_scale=w_scale_bytes[:, e * K : (e + 1) * K],
                 start=True,
                 stop=True,
             )
-            return bank[:].rearrange("s (p d) -> s d p", d=PACK)
+            return banks[e][:].rearrange("s (p d) -> s d p", d=PACK)
 
-        def turn(d, e0, e1, bank):
+        def turn(copy, d, e0, e1, bank):
             for e in range(e0, e1):
-                nc.tensor.transpose(bank[:, (e - e0) * C : (e - e0 + 1) * C], staged_sums(e, d), ident[:])
-            return bank[:, : (e1 - e0) * C]
+                nc.tensor.transpose(bank[:, slots(e - e0, e - e0 + 1)], unturned(e, d), ident[:])
+            copy(y[d][:, slots(e0, e1)], bank[:, slots(0, e1 - e0)])
 
         sums = []
         for e in range(E):
-            xg = gather_words(e)
+            slot_words = gather_words(e)
             if e < 2:
-                gather_scales(e * C, (e + 1) * C)
+                gather_scales(e, e + 1)
             elif e % 2 == 0:
-                gather_scales(e * C, (e + 2) * C)
-            sums.append(multiply1(e, xg))
-        nc.scalar.activation(whole[:, 0, :, :], sums[0], COPY)
-        nc.scalar.copy(whole[:, 1, :, :], sums[1])
-        nc.scalar.copy(whole[:, 2, :, :], sums[2])
-        for e in range(3, E - 1):
-            nc.scalar.copy(early[:, e - 3, :, :], sums[e][:, :2, :])
-        nc.scalar.copy(last_early[:], sums[E - 1][:, 0, :])
-        nc.vector.tensor_copy(y[0][:, : 4 * C], turn(0, 0, 4, banks[0]))
-        nc.scalar.copy(y[0][:, 4 * C : 6 * C], turn(0, 4, 6, banks[1]))
-        nc.scalar.copy(y[0][:, 6 * C :], turn(0, 6, 8, banks[2]))
-        nc.vector.tensor_copy(staged_sums(E - 1, 1), sums[E - 1][:, 1, :])
-        for e in range(3, 6):
-            nc.vector.tensor_copy(late_free[:, e - 3, :, :], sums[e][:, 2:, :])
-        late_rest = held.tile([P, 2, 2, P], F32, name="late_rest", tag="shared")
-        nc.scalar.copy(late_rest[:, 0, :, :], sums[6][:, 2:, :])
-        nc.scalar.copy(y[1][:, : 4 * C], turn(1, 0, 4, banks[2]))
-        nc.scalar.copy(y[1][:, 4 * C :], turn(1, 4, 8, banks[6]))
-        nc.scalar.copy(late_rest[:, 1, :, :], sums[7][:, 2:, :])
-        for d, (b0, b1) in ((2, (7, 2)), (3, (6, 7))):
-            nc.scalar.copy(y[d][:, : 4 * C], turn(d, 0, 4, banks[b0]))
-            nc.scalar.copy(y[d][:, 4 * C :], turn(d, 4, 8, banks[b1]))
+                gather_scales(e, e + 2)
+            sums.append(multiply_step1(e, slot_words))
 
-        def weigh(dst, rows, step, r, t0, t1):
-            nc.vector.tensor_tensor(
-                dst[:, t0:t1], rows[:].indirect(pos_sb[2 * step + r][:, cols(t0, t1)]), gates[step][:, r, t0:t1], MULT
-            )
+        nc.scalar.activation(all_planes[:, 0, :, :], sums[0], COPY)
+        for e in range(1, WHOLE):
+            nc.scalar.copy(all_planes[:, e, :, :], sums[e])
+        for e in range(WHOLE, LAST):
+            nc.scalar.copy(low_planes[:, e - WHOLE, :, :], sums[e][:, :2, :])
+        nc.scalar.copy(last_plane0[:], sums[LAST][:, 0, :])
 
-        prod = [held.tile([P, PACK, T], F32, name="prod%d" % r) for r in range(2)]
-        c_plane = [held.tile([P, T], BF16, name="c%d" % d) for d in range(2)]
+        turn(nc.vector.tensor_copy, 0, 0, HALF_E, banks[0])
+        turn(nc.scalar.copy, 0, HALF_E, HELD, banks[1])
+        turn(nc.scalar.copy, 0, HELD, E, banks[2])
+        nc.vector.tensor_copy(unturned(LAST, 1), sums[LAST][:, 1, :])
+        for e in range(WHOLE, HELD):
+            nc.vector.tensor_copy(high_planes[:, e - WHOLE, :, :], sums[e][:, 2:, :])
+
+        held_high_planes = held.tile([P, E - HELD, 2, P], F32, name="held_high_planes", tag="after_plane0")
+        nc.scalar.copy(held_high_planes[:, 0, :, :], sums[HELD][:, 2:, :])
+        turn(nc.scalar.copy, 1, 0, HALF_E, banks[2])
+        turn(nc.scalar.copy, 1, HALF_E, E, banks[6])
+        nc.scalar.copy(held_high_planes[:, 1, :, :], sums[LAST][:, 2:, :])
+        for d, (first_half, second_half) in ((2, (7, 2)), (3, (6, 7))):
+            turn(nc.scalar.copy, d, 0, HALF_E, banks[first_half])
+            turn(nc.scalar.copy, d, HALF_E, E, banks[second_half])
+
+        def weigh(step, r, rows, terms, n, t0=0, t1=T):
+            picked = rows[n][:].indirect(pos_sb[2 * step + r][:, entries(t0, t1)])
+            nc.vector.tensor_tensor(terms[r][:, n, t0:t1], picked, gates[step][:, r, t0:t1], MULT)
+
+        c_terms = [held.tile([P, PACK, T], F32, name="c_terms%d" % r) for r in range(2)]
+        c_plane = [held.tile([P, T], BF16, name="c_plane%d" % d) for d in range(2)]
         c_pair = held.tile([P, T, 2], BF16, name="c_pair")
 
-        def add_on_tensor(dst, first, second, bank_sum, bank_back):
+        def add_on_tensor(dst, terms, n, bank_sum, bank_back):
             blocks = [slice(j * P, (j + 1) * P) for j in range(T // P)]
-            for r, src in enumerate((first, second)):
+            for r in range(2):
                 for j, block in enumerate(blocks):
                     nc.tensor.matmul(
                         bank_sum[:, block],
-                        lhsT=src[:, block],
+                        lhsT=terms[r][:, n, block],
                         rhs=ident[:],
                         start=(r == 0 and j == 0),
                         stop=(r == 1 and j == len(blocks) - 1),
                         is_transpose=True,
                     )
-            turned = ring.tile([P, T], F32, name="turned", bufs=2)
-            nc.scalar.copy(turned[:], bank_sum[:])
+            turned_sum = ring.tile([P, T], F32, name="turned_sum", bufs=2)
+            nc.scalar.copy(turned_sum[:], bank_sum[:])
             for block in blocks:
-                nc.tensor.transpose(bank_back[:, block], turned[:, block], ident[:])
+                nc.tensor.transpose(bank_back[:, block], turned_sum[:, block], ident[:])
             nc.scalar.copy(dst, bank_back[:])
 
-        def add_plane(d):
-            nc.vector.tensor_tensor(c_plane[d][:], prod[0][:, d, :], prod[1][:, d, :], ADD)
-
-        weigh(prod[0][:, 0, :], y[0], 0, 0, 0, T)
-        weigh(prod[1][:, 0, :], y[0], 0, 1, 0, T)
-        add_on_tensor(c_plane[0][:], prod[0][:, 0, :], prod[1][:, 0, :], banks[0], banks[1])
-        weigh(prod[0][:, 1, :], y[1], 0, 0, 0, T)
-        weigh(prod[1][:, 1, :], y[1], 0, 1, 0, T)
-        weigh(prod[0][:, 2, :], y[2], 0, 0, 0, T)
-        add_plane(1)
-        weigh(prod[1][:, 2, :], y[2], 0, 1, 0, T)
-        weigh(prod[0][:, 3, :], y[3], 0, 0, 0, T)
-        weigh(prod[1][:, 3, :], y[3], 0, 1, 0, T // 2)
-        weigh(prod[1][:, 3, :], y[3], 0, 1, T // 2, T)
-        for t0 in (0, T // 2):
-            tok = slice(t0, t0 + T // 2)
+        weigh(0, 0, y, c_terms, 0)
+        weigh(0, 1, y, c_terms, 0)
+        add_on_tensor(c_plane[0][:], c_terms, 0, banks[0], banks[1])
+        weigh(0, 0, y, c_terms, 1)
+        weigh(0, 1, y, c_terms, 1)
+        weigh(0, 0, y, c_terms, 2)
+        nc.vector.tensor_tensor(c_plane[1][:], c_terms[0][:, 1, :], c_terms[1][:, 1, :], ADD)
+        weigh(0, 1, y, c_terms, 2)
+        weigh(0, 0, y, c_terms, 3)
+        weigh(0, 1, y, c_terms, 3, 0, HALF_T)
+        weigh(0, 1, y, c_terms, 3, HALF_T, T)
+        for t0 in (0, HALF_T):
+            tokens = slice(t0, t0 + HALF_T)
             nc.vector.tensor_tensor(
-                c_pair[:, tok, :].rearrange("p (g i) d -> p g d i", i=4),
-                prod[0][:, 2:, tok].rearrange("p d (g i) -> p g d i", i=4),
-                prod[1][:, 2:, tok].rearrange("p d (g i) -> p g d i", i=4),
+                c_pair[:, tokens, :].rearrange("p (g i) d -> p g d i", i=4),
+                c_terms[0][:, 2:, tokens].rearrange("p d (g i) -> p g d i", i=4),
+                c_terms[1][:, 2:, tokens].rearrange("p d (g i) -> p g d i", i=4),
                 ADD,
             )
 
-        STAGED = 6 * C
-        staged = held.tile([P, 2, STAGED, 2], BF16, name="staged", align_bytes=64)
+        staged = held.tile([P, 2, STAGED * C, 2], BF16, name="staged", align_bytes=64)
         grouped = held.tile([P, S, PACK], BF16, name="grouped", align_bytes=64)
-        codes = held.tile([P, S], U32, name="codes", align_bytes=64)
-        scales = held.tile([P, S], U8, name="scales", align_bytes=64)
-        for experts in (range(6), range(6, E)):
+        c_words = held.tile([P, S], U32, name="c_words", align_bytes=64)
+        c_scales = held.tile([P, S], U8, name="c_scales", align_bytes=64)
+
+        for experts in (range(STAGED), range(STAGED, E)):
             for d in range(2):
                 for e in experts:
-                    slots = slice(e * C, (e + 1) * C)
-                    dst = staged[:, 0, slots, d] if (e + 1) * C <= STAGED else grouped[:, slots, d]
-                    nc.scalar.activation(dst, c_plane[d][:].indirect(offs2_sb[:, cols(e * C, (e + 1) * C)]), COPY)
+                    dst = staged[:, 0, slots(e, e + 1), d] if e < STAGED else grouped[:, slots(e, e + 1), d]
+                    picked = c_plane[d][:].indirect(offs2_sb[:, entries(e * C, (e + 1) * C)])
+                    nc.scalar.activation(dst, picked, COPY)
 
-        pair_window = c_pair[:].rearrange("p t d -> p (t d)").bitcast(U32)
+        c_pair_words = c_pair[:].rearrange("p t d -> p (t d)").bitcast(U32)
         staged_flat = staged[:].rearrange("p u s d -> p (u s d)")
         grouped_flat = grouped[:].rearrange("p s d -> p (s d)")
 
-        def gather_pairs(s0, s1):
-            if s1 <= STAGED:
-                dst = staged_flat.bitcast(U32)[:, STAGED + s0 : STAGED + s1]
-            else:
-                dst = grouped_flat.bitcast(U32)[:, 2 * s0 + 1 : 2 * s1 : 2]
-            nc.vector.tensor_copy(dst, pair_window.indirect(offs2_sb[:, cols(s0, s1)]))
-            if s1 <= STAGED:
+        def gather_pairs(e0, e1):
+            picked = c_pair_words.indirect(offs2_sb[:, entries(e0 * C, e1 * C)])
+            if e1 <= STAGED:
+                nc.vector.tensor_copy(staged_flat.bitcast(U32)[:, slots(STAGED + e0, STAGED + e1)], picked)
                 nc.scalar.copy(
-                    grouped_flat.bitcast(F32).rearrange("p (s u) -> p s u", u=2)[:, s0:s1, :],
-                    staged_flat.bitcast(F32).rearrange("p (u s) -> p s u", u=2)[:, s0:s1, :],
+                    grouped_flat.bitcast(F32).rearrange("p (s u) -> p s u", u=2)[:, slots(e0, e1), :],
+                    staged_flat.bitcast(F32).rearrange("p (u s) -> p s u", u=2)[:, slots(e0, e1), :],
                 )
+            else:
+                nc.vector.tensor_copy(grouped_flat.bitcast(U32)[:, 2 * e0 * C + 1 : 2 * e1 * C : 2], picked)
 
-        def quantize(s0, s1):
+        def quantize(e0, e1):
             nc.vector.quantize_mx(
-                out=codes[:, s0:s1].bitcast(FP8X4), scales=scales[:, s0:s1], in_=grouped_flat[:, PACK * s0 : PACK * s1]
+                out=c_words[:, slots(e0, e1)].bitcast(FP8X4),
+                scales=c_scales[:, slots(e0, e1)],
+                in_=grouped_flat[:, slots(PACK * e0, PACK * e1)],
             )
 
-        gather_pairs(0, 256)
-        gather_pairs(256, 512)
-        gather_pairs(512, 768)
-        quantize(0, 256)
-        gather_pairs(768, 1024)
-        quantize(256, 512)
-        quantize(512, 768)
-        quantize(768, 896)
-        quantize(896, 1024)
+        gather_pairs(0, 2)
+        gather_pairs(2, 4)
+        gather_pairs(4, 6)
+        quantize(0, 2)
+        gather_pairs(6, 8)
+        quantize(2, 4)
+        quantize(4, 6)
+        quantize(6, 7)
+        quantize(7, 8)
 
-        z = [held.tile([P, S], F32, name="z%d" % t) for t in range(PACK)]
+        z = [held.tile([P, S], F32, name="z%d" % m) for m in range(ROW_TILES)]
 
-        def multiply2(t, e0, e1, bank):
+        def multiply_step2(m, e0, e1, bank):
             for e in range(e0, e1):
-                col = e * K + t * P
+                column = e * K + m * P
                 nc.tensor.matmul_mx(
-                    bank[:, (e - e0) * C : (e - e0 + 1) * C],
-                    lhsT=w_bytes[:, 2 * col : 2 * (col + P)].bitcast(FP4X4),
-                    lhsT_scale=w_scale[:, col : col + P],
-                    rhs=codes[:, e * C : (e + 1) * C].bitcast(FP8X4),
-                    rhs_scale=scales[:, e * C : (e + 1) * C],
+                    bank[:, slots(e - e0, e - e0 + 1)],
+                    lhsT=w_word_bytes[:, 2 * column : 2 * (column + P)].bitcast(FP4X4),
+                    lhsT_scale=w_scale_bytes[:, column : column + P],
+                    rhs=c_words[:, slots(e, e + 1)].bitcast(FP8X4),
+                    rhs_scale=c_scales[:, slots(e, e + 1)],
                     start=True,
                     stop=True,
                 )
-            nc.scalar.copy(z[t][:, e0 * C : e1 * C], bank[:, : (e1 - e0) * C])
+            nc.scalar.copy(z[m][:, slots(e0, e1)], bank[:, slots(0, e1 - e0)])
 
-        multiply2(0, 0, 4, banks[0])
-        multiply2(0, 4, 6, banks[4])
-        multiply2(0, 6, 7, banks[5])
-        multiply2(0, 7, 8, banks[6])
-        for t, (b0, b1) in ((1, (0, 6)), (2, (5, 0)), (3, (6, 5))):
-            multiply2(t, 0, 4, banks[b0])
-            multiply2(t, 4, 8, banks[b1])
+        for e0, e1, b in ((0, 4, 0), (4, 6, 4), (6, 7, 5), (7, 8, 6)):
+            multiply_step2(0, e0, e1, banks[b])
+        for m in range(1, ROW_TILES):
+            multiply_step2(m, 0, HALF_E, banks[0])
+            multiply_step2(m, HALF_E, E, banks[6])
 
-        prod2 = [held.tile([P, PACK, T], F32, name="prod2_%d" % r) for r in range(2)]
-        result = held.tile([P, PACK, T], F32, name="result")
+        out_terms = [held.tile([P, ROW_TILES, T], F32, name="out_terms%d" % r) for r in range(2)]
+        result = held.tile([P, ROW_TILES, T], F32, name="result")
 
-        def finish(t, t0, t1):
-            nc.vector.tensor_tensor(result[:, t, t0:t1], prod2[0][:, t, t0:t1], prod2[1][:, t, t0:t1], ADD)
-            nc.sync.dma_start(out[t * P : (t + 1) * P, t0:t1], result[:, t, t0:t1])
+        def finish_on_vector(m, t0, t1):
+            nc.vector.tensor_tensor(result[:, m, t0:t1], out_terms[0][:, m, t0:t1], out_terms[1][:, m, t0:t1], ADD)
+            nc.sync.dma_start(out[m * P : (m + 1) * P, t0:t1], result[:, m, t0:t1])
 
-        def finish_on_tensor(t, bank_sum, bank_back):
-            add_on_tensor(result[:, t, :], prod2[0][:, t, :], prod2[1][:, t, :], bank_sum, bank_back)
-            nc.sync.dma_start(out[t * P : (t + 1) * P, :], result[:, t, :])
+        def finish_on_tensor(m, bank_sum, bank_back):
+            add_on_tensor(result[:, m, :], out_terms, m, bank_sum, bank_back)
+            nc.sync.dma_start(out[m * P : (m + 1) * P, :], result[:, m, :])
 
-        weigh(prod2[0][:, 0, :], z[0], 1, 0, 0, T)
-        weigh(prod2[1][:, 0, :], z[0], 1, 1, 0, T)
-        finish_on_tensor(0, banks[1], banks[2])
-        weigh(prod2[0][:, 1, :], z[1], 1, 0, 0, T)
-        weigh(prod2[1][:, 1, :], z[1], 1, 1, 0, T)
-        finish_on_tensor(1, banks[3], banks[4])
-        weigh(prod2[0][:, 2, :], z[2], 1, 0, 0, T)
-        weigh(prod2[1][:, 2, :], z[2], 1, 1, 0, T)
-        weigh(prod2[0][:, 3, :], z[3], 1, 0, 0, 256)
-        finish(2, 0, T)
-        weigh(prod2[1][:, 3, :], z[3], 1, 1, 0, 256)
-        weigh(prod2[0][:, 3, :], z[3], 1, 0, 256, 512)
-        finish(3, 0, 256)
-        weigh(prod2[1][:, 3, :], z[3], 1, 1, 256, 512)
-        finish(3, 256, 512)
+        for m, (bank_sum, bank_back) in enumerate(((1, 2), (3, 4))):
+            weigh(1, 0, z, out_terms, m)
+            weigh(1, 1, z, out_terms, m)
+            finish_on_tensor(m, banks[bank_sum], banks[bank_back])
+        weigh(1, 0, z, out_terms, 2)
+        weigh(1, 1, z, out_terms, 2)
+        weigh(1, 0, z, out_terms, 3, 0, HALF_T)
+        finish_on_vector(2, 0, T)
+        weigh(1, 1, z, out_terms, 3, 0, HALF_T)
+        weigh(1, 0, z, out_terms, 3, HALF_T, T)
+        finish_on_vector(3, 0, HALF_T)
+        weigh(1, 1, z, out_terms, 3, HALF_T, T)
+        finish_on_vector(3, HALF_T, T)

@@ -14,7 +14,7 @@ SCALE_ROWS = K // 32
 HALF_E, HALF_T = E // 2, T // 2
 FLOPS = 2 * 2 * K * K * S
 
-WHOLE, HELD = 3, 6
+WHOLE = 3
 LAST = E - 1
 WORD_RING = 4
 STAGED = 6
@@ -56,7 +56,7 @@ def tile_moe_uni_none_kernel(
         pos_sb = [lists.tile([P, T // PER_COLUMN], U16, name="pos%d_sb" % (n + 1)) for n in range(4)]
 
         x_words_sb = held.tile([P, T], I32, name="x_words_sb", align_bytes=64)
-        x_scales_sb = held.tile([P, T // 4], I32, name="x_scales_sb", align_bytes=64)
+        x_scales_sb = held.tile([P, T // 4], I32, name="x_scales_sb", tag="after_scales", align_bytes=64)
         w_words_sb = held.tile([P, E * 2 * K // 4], I32, name="w_words_sb", align_bytes=64)
         w_scales_sb = held.tile([P, E * K // 4], I32, name="w_scales_sb", align_bytes=64)
         gates = [held.tile([P, 2, T], F32, name="gate%d_sb" % (step + 1)) for step in range(2)]
@@ -95,36 +95,32 @@ def tile_moe_uni_none_kernel(
 
         slot_scales = held.tile([P, S], U8, name="slot_scales", align_bytes=64)
 
-        def gather_words(e):
-            slot_words = ring.tile([P, C], U32, name="slot_words", align_bytes=64)
+        def gather_words(dst, e0, e1):
             window = x_words_sb[:].bitcast(U32)
-            nc.vector.tensor_copy(slot_words[:], window.indirect(offs_sb[:, entries(e * C, (e + 1) * C)]))
-            return slot_words
+            nc.vector.tensor_copy(dst, window.indirect(offs_sb[:, entries(e0 * C, e1 * C)]))
 
         def gather_scales(e0, e1):
             window = x_scales_sb[:].bitcast(U8)
             nc.vector.tensor_copy(slot_scales[:, slots(e0, e1)], window.indirect(offs_sb[:, entries(e0 * C, e1 * C)]))
 
         all_planes = held.tile([P, WHOLE, PACK, P], F32, name="all_planes")
-        low_planes = held.tile([P, E - WHOLE, 2, P], F32, name="low_planes")
-        high_planes = held.tile([P, HELD - WHOLE, 2, P], F32, name="high_planes")
-        last_plane0 = held.tile([P, P], F32, name="last_plane0", tag="after_plane0")
+        plane0 = held.tile([P, E - WHOLE, P], F32, name="plane0")
+        plane1 = held.tile([P, E - WHOLE, P], F32, name="plane1")
+        high_planes = held.tile([P, E - WHOLE, 2, P], F32, name="high_planes")
 
-        def unturned(e, d):
-            if (e, d) == (LAST, 0):
-                return last_plane0[:]
+        def plane(e, d):
             if e < WHOLE:
                 return all_planes[:, e, d, :]
-            if d < 2:
-                return low_planes[:, e - WHOLE, d, :]
-            return high_planes[:, e - WHOLE, d - 2, :] if e < HELD else held_high_planes[:, e - HELD, d - 2, :]
+            if d >= 2:
+                return high_planes[:, e - WHOLE, d - 2, :]
+            return (plane0, plane1)[d][:, e - WHOLE, :]
 
         y = [held.tile([P, S], F32, name="y%d" % d) for d in range(PACK)]
 
         def multiply_step1(e, slot_words):
             nc.tensor.matmul_mx(
                 banks[e][:],
-                lhsT=slot_words[:].bitcast(FP8X4),
+                lhsT=slot_words.bitcast(FP8X4),
                 lhsT_scale=slot_scales[:, slots(e, e + 1)],
                 rhs=w_word_bytes[:, e * 2 * K : (e + 1) * 2 * K].bitcast(FP4X4),
                 rhs_scale=w_scale_bytes[:, e * K : (e + 1) * K],
@@ -135,40 +131,51 @@ def tile_moe_uni_none_kernel(
 
         def turn(copy, d, e0, e1, bank):
             for e in range(e0, e1):
-                nc.tensor.transpose(bank[:, slots(e - e0, e - e0 + 1)], unturned(e, d), ident[:])
+                nc.tensor.transpose(bank[:, slots(e - e0, e - e0 + 1)], plane(e, d), ident[:])
             copy(y[d][:, slots(e0, e1)], bank[:, slots(0, e1 - e0)])
 
-        sums = []
-        for e in range(E):
-            slot_words = gather_words(e)
-            if e < 2:
-                gather_scales(e, e + 1)
-            elif e % 2 == 0:
-                gather_scales(e, e + 2)
-            sums.append(multiply_step1(e, slot_words))
+        first_words = held.tile([P, 2 * C], U32, name="first_words", align_bytes=64)
+        gather_words(first_words[:], 0, 2)
+        gather_scales(0, 2)
+        for n in range(3):
+            nc.tensor.matmul_mx(
+                banks[LAST][:, : 2 * C],
+                lhsT=first_words[:, slots(0, 1)].bitcast(FP8X4),
+                lhsT_scale=slot_scales[:, slots(0, 1)],
+                rhs=w_word_bytes[:, : 4 * C].bitcast(FP4X4),
+                rhs_scale=slot_scales[:, slots(0, 2)],
+                start=True,
+                stop=True,
+            )
+        sums = [multiply_step1(e, first_words[:, slots(e, e + 1)]) for e in range(2)]
+        gather_scales(2, 5)
+        gather_scales(5, 8)
+        later_words = held.tile([P, (E - 2) * C], U32, name="later_words", tag="after_scales", align_bytes=64)
+        for e in range(2, E):
+            gather_words(later_words[:, slots(e - 2, e - 1)], e, e + 1)
+            sums.append(multiply_step1(e, later_words[:, slots(e - 2, e - 1)]))
 
         nc.scalar.activation(all_planes[:, 0, :, :], sums[0], COPY)
         for e in range(1, WHOLE):
             nc.scalar.copy(all_planes[:, e, :, :], sums[e])
-        for e in range(WHOLE, LAST):
-            nc.scalar.copy(low_planes[:, e - WHOLE, :, :], sums[e][:, :2, :])
-        nc.scalar.copy(last_plane0[:], sums[LAST][:, 0, :])
+        for e in range(WHOLE, LAST - 1):
+            nc.scalar.copy(plane(e, 0), sums[e][:, 0, :])
+        for e in (LAST - 1, LAST):
+            nc.vector.tensor_copy(plane(e, 0), sums[e][:, 0, :])
 
-        turn(nc.vector.tensor_copy, 0, 0, HALF_E, banks[0])
-        turn(nc.scalar.copy, 0, HALF_E, HELD, banks[1])
-        turn(nc.scalar.copy, 0, HELD, E, banks[2])
-        nc.vector.tensor_copy(unturned(LAST, 1), sums[LAST][:, 1, :])
-        for e in range(WHOLE, HELD):
-            nc.vector.tensor_copy(high_planes[:, e - WHOLE, :, :], sums[e][:, 2:, :])
-
-        held_high_planes = held.tile([P, E - HELD, 2, P], F32, name="held_high_planes", tag="after_plane0")
-        nc.scalar.copy(held_high_planes[:, 0, :, :], sums[HELD][:, 2:, :])
-        turn(nc.scalar.copy, 1, 0, HALF_E, banks[2])
-        turn(nc.scalar.copy, 1, HALF_E, E, banks[6])
-        nc.scalar.copy(held_high_planes[:, 1, :, :], sums[LAST][:, 2:, :])
-        for d, (first_half, second_half) in ((2, (7, 2)), (3, (6, 7))):
-            turn(nc.scalar.copy, d, 0, HALF_E, banks[first_half])
-            turn(nc.scalar.copy, d, HALF_E, E, banks[second_half])
+        turn(nc.vector.tensor_copy, 0, 0, WHOLE, banks[0])
+        turn(nc.scalar.copy, 0, WHOLE, LAST - 1, banks[1])
+        turn(nc.vector.tensor_copy, 0, LAST - 1, E, banks[2])
+        for e in range(WHOLE, E):
+            nc.scalar.copy(plane(e, 1), sums[e][:, 1, :])
+        turn(nc.scalar.copy, 1, 0, HALF_E, banks[0])
+        turn(nc.scalar.copy, 1, HALF_E, E, banks[1])
+        for e in range(WHOLE, E):
+            nc.scalar.copy(high_planes[:, e - WHOLE, :, :], sums[e][:, 2:, :])
+        turn(nc.scalar.copy, 2, 0, HALF_E, banks[2])
+        turn(nc.scalar.copy, 2, HALF_E, E, banks[0])
+        turn(nc.scalar.copy, 3, 0, HALF_E, banks[3])
+        turn(nc.scalar.copy, 3, HALF_E, E, banks[4])
 
         def weigh(step, r, rows, terms, n, t0=0, t1=T):
             picked = rows[n][:].indirect(pos_sb[2 * step + r][:, entries(t0, t1)])
@@ -196,13 +203,11 @@ def tile_moe_uni_none_kernel(
                 nc.tensor.transpose(bank_back[:, block], turned_sum[:, block], ident[:])
             nc.scalar.copy(dst, bank_back[:])
 
-        weigh(0, 0, y, c_terms, 0)
-        weigh(0, 1, y, c_terms, 0)
-        add_on_tensor(c_plane[0][:], c_terms, 0, banks[0], banks[1])
-        weigh(0, 0, y, c_terms, 1)
-        weigh(0, 1, y, c_terms, 1)
+        for d, (bank_sum, bank_back) in enumerate(((0, 5), (6, 7))):
+            weigh(0, 0, y, c_terms, d)
+            weigh(0, 1, y, c_terms, d)
+            add_on_tensor(c_plane[d][:], c_terms, d, banks[bank_sum], banks[bank_back])
         weigh(0, 0, y, c_terms, 2)
-        nc.vector.tensor_tensor(c_plane[1][:], c_terms[0][:, 1, :], c_terms[1][:, 1, :], ADD)
         weigh(0, 1, y, c_terms, 2)
         weigh(0, 0, y, c_terms, 3)
         weigh(0, 1, y, c_terms, 3, 0, HALF_T)
@@ -221,12 +226,10 @@ def tile_moe_uni_none_kernel(
         c_words = held.tile([P, S], U32, name="c_words", align_bytes=64)
         c_scales = held.tile([P, S], U8, name="c_scales", align_bytes=64)
 
-        for experts in (range(STAGED), range(STAGED, E)):
-            for d in range(2):
-                for e in experts:
-                    dst = staged[:, 0, slots(e, e + 1), d] if e < STAGED else grouped[:, slots(e, e + 1), d]
-                    picked = c_plane[d][:].indirect(offs2_sb[:, entries(e * C, (e + 1) * C)])
-                    nc.scalar.activation(dst, picked, COPY)
+        for e0, e1, d in ((0, 3, 0), (3, 6, 0), (0, 3, 1), (3, 6, 1), (6, 8, 0), (6, 8, 1)):
+            dst = staged[:, 0, slots(e0, e1), d] if e1 <= STAGED else grouped[:, slots(e0, e1), d]
+            picked = c_plane[d][:].indirect(offs2_sb[:, entries(e0 * C, e1 * C)])
+            nc.scalar.activation(dst, picked, COPY)
 
         c_pair_words = c_pair[:].rearrange("p t d -> p (t d)").bitcast(U32)
         staged_flat = staged[:].rearrange("p u s d -> p (u s d)")

@@ -56,7 +56,7 @@ def tile_moe_uni_none_kernel(
         pos_sb = [lists.tile([P, T // PER_COLUMN], U16, name="pos%d_sb" % (n + 1)) for n in range(4)]
 
         x_words_sb = held.tile([P, T], I32, name="x_words_sb", align_bytes=64)
-        x_scales_sb = held.tile([P, T // 4], I32, name="x_scales_sb", tag="after_scales", align_bytes=64)
+        x_scales_sb = held.tile([P, T // 4], I32, name="x_scales_sb", align_bytes=64)
         w_words_sb = held.tile([P, E * 2 * K // 4], I32, name="w_words_sb", align_bytes=64)
         w_scales_sb = held.tile([P, E * K // 4], I32, name="w_scales_sb", align_bytes=64)
         gates = [held.tile([P, 2, T], F32, name="gate%d_sb" % (step + 1)) for step in range(2)]
@@ -134,26 +134,15 @@ def tile_moe_uni_none_kernel(
                 nc.tensor.transpose(bank[:, slots(e - e0, e - e0 + 1)], plane(e, d), ident[:])
             copy(y[d][:, slots(e0, e1)], bank[:, slots(0, e1 - e0)])
 
-        first_words = held.tile([P, 2 * C], U32, name="first_words", align_bytes=64)
-        gather_words(first_words[:], 0, 2)
-        gather_scales(0, 2)
-        for n in range(3):
-            nc.tensor.matmul_mx(
-                banks[LAST][:, : 2 * C],
-                lhsT=first_words[:, slots(0, 1)].bitcast(FP8X4),
-                lhsT_scale=slot_scales[:, slots(0, 1)],
-                rhs=w_word_bytes[:, : 4 * C].bitcast(FP4X4),
-                rhs_scale=slot_scales[:, slots(0, 2)],
-                start=True,
-                stop=True,
-            )
-        sums = [multiply_step1(e, first_words[:, slots(e, e + 1)]) for e in range(2)]
-        gather_scales(2, 5)
-        gather_scales(5, 8)
-        later_words = held.tile([P, (E - 2) * C], U32, name="later_words", tag="after_scales", align_bytes=64)
-        for e in range(2, E):
-            gather_words(later_words[:, slots(e - 2, e - 1)], e, e + 1)
-            sums.append(multiply_step1(e, later_words[:, slots(e - 2, e - 1)]))
+        sums = []
+        for e in range(E):
+            slot_words = ring.tile([P, C], U32, name="slot_words", align_bytes=64)
+            gather_words(slot_words[:], e, e + 1)
+            if e < 2:
+                gather_scales(e, e + 1)
+            elif e % 2 == 0:
+                gather_scales(e, e + 2)
+            sums.append(multiply_step1(e, slot_words[:]))
 
         nc.scalar.activation(all_planes[:, 0, :, :], sums[0], COPY)
         for e in range(1, WHOLE):
@@ -185,8 +174,8 @@ def tile_moe_uni_none_kernel(
         c_plane = [held.tile([P, T], BF16, name="c_plane%d" % d) for d in range(2)]
         c_pair = held.tile([P, T, 2], BF16, name="c_pair")
 
-        def add_on_tensor(dst, terms, n, bank_sum, bank_back):
-            blocks = [slice(j * P, (j + 1) * P) for j in range(T // P)]
+        def add_on_tensor(dst, terms, n, bank_sum, bank_back, t0=0, t1=T):
+            blocks = [slice(j * P, (j + 1) * P) for j in range(t0 // P, t1 // P)]
             for r in range(2):
                 for j, block in enumerate(blocks):
                     nc.tensor.matmul(
@@ -197,11 +186,11 @@ def tile_moe_uni_none_kernel(
                         stop=(r == 1 and j == len(blocks) - 1),
                         is_transpose=True,
                     )
-            turned_sum = ring.tile([P, T], F32, name="turned_sum", bufs=2)
-            nc.scalar.copy(turned_sum[:], bank_sum[:])
+            turned_sum = ring.tile([P, T], F32, name="turned_sum")
+            nc.scalar.copy(turned_sum[:, t0:t1], bank_sum[:, t0:t1])
             for block in blocks:
                 nc.tensor.transpose(bank_back[:, block], turned_sum[:, block], ident[:])
-            nc.scalar.copy(dst, bank_back[:])
+            nc.scalar.copy(dst, bank_back[:, t0:t1])
 
         for d, (bank_sum, bank_back) in enumerate(((0, 5), (6, 7))):
             weigh(0, 0, y, c_terms, d)
@@ -226,10 +215,15 @@ def tile_moe_uni_none_kernel(
         c_words = held.tile([P, S], U32, name="c_words", align_bytes=64)
         c_scales = held.tile([P, S], U8, name="c_scales", align_bytes=64)
 
-        for e0, e1, d in ((0, 3, 0), (3, 6, 0), (0, 3, 1), (3, 6, 1), (6, 8, 0), (6, 8, 1)):
+        def gather_plane(d, e0, e1):
             dst = staged[:, 0, slots(e0, e1), d] if e1 <= STAGED else grouped[:, slots(e0, e1), d]
             picked = c_plane[d][:].indirect(offs2_sb[:, entries(e0 * C, e1 * C)])
             nc.scalar.activation(dst, picked, COPY)
+
+        for d in range(2):
+            gather_plane(d, 0, STAGED // 2)
+            gather_plane(d, STAGED // 2, STAGED)
+        gather_plane(0, STAGED, E)
 
         c_pair_words = c_pair[:].rearrange("p t d -> p (t d)").bitcast(U32)
         staged_flat = staged[:].rearrange("p u s d -> p (u s d)")
@@ -256,6 +250,8 @@ def tile_moe_uni_none_kernel(
         gather_pairs(0, 2)
         gather_pairs(2, 4)
         gather_pairs(4, 6)
+        gather_plane(1, 6, 7)
+        gather_plane(1, 7, 8)
         quantize(0, 2)
         gather_pairs(6, 8)
         quantize(2, 4)
@@ -292,18 +288,19 @@ def tile_moe_uni_none_kernel(
             nc.vector.tensor_tensor(result[:, m, t0:t1], out_terms[0][:, m, t0:t1], out_terms[1][:, m, t0:t1], ADD)
             nc.sync.dma_start(out[m * P : (m + 1) * P, t0:t1], result[:, m, t0:t1])
 
-        def finish_on_tensor(m, bank_sum, bank_back):
-            add_on_tensor(result[:, m, :], out_terms, m, bank_sum, bank_back)
-            nc.sync.dma_start(out[m * P : (m + 1) * P, :], result[:, m, :])
+        def finish_on_tensor(m, bank_sum, bank_back, t0=0, t1=T):
+            add_on_tensor(result[:, m, t0:t1], out_terms, m, bank_sum, bank_back, t0, t1)
+            nc.scalar.dma_start(out[m * P : (m + 1) * P, t0:t1], result[:, m, t0:t1])
 
         for m, (bank_sum, bank_back) in enumerate(((1, 2), (3, 4))):
             weigh(1, 0, z, out_terms, m)
             weigh(1, 1, z, out_terms, m)
             finish_on_tensor(m, banks[bank_sum], banks[bank_back])
         weigh(1, 0, z, out_terms, 2)
-        weigh(1, 1, z, out_terms, 2)
+        for t0, bank_sum, bank_back in ((0, 5, 7), (HALF_T, 1, 2)):
+            weigh(1, 1, z, out_terms, 2, t0, t0 + HALF_T)
+            finish_on_tensor(2, banks[bank_sum], banks[bank_back], t0, t0 + HALF_T)
         weigh(1, 0, z, out_terms, 3, 0, HALF_T)
-        finish_on_vector(2, 0, T)
         weigh(1, 1, z, out_terms, 3, 0, HALF_T)
         weigh(1, 0, z, out_terms, 3, HALF_T, T)
         finish_on_vector(3, 0, HALF_T)

@@ -103,17 +103,7 @@ def tile_moe_uni_none_kernel(
             window = x_scales_sb[:].bitcast(U8)
             nc.vector.tensor_copy(slot_scales[:, slots(e0, e1)], window.indirect(offs_sb[:, entries(e0 * C, e1 * C)]))
 
-        all_planes = held.tile([P, WHOLE, PACK, P], F32, name="all_planes")
-        plane0 = held.tile([P, E - WHOLE, P], F32, name="plane0")
-        plane1 = held.tile([P, E - WHOLE, P], F32, name="plane1")
-        high_planes = held.tile([P, E - WHOLE, 2, P], F32, name="high_planes")
-
-        def plane(e, d):
-            if e < WHOLE:
-                return all_planes[:, e, d, :]
-            if d >= 2:
-                return high_planes[:, e - WHOLE, d - 2, :]
-            return (plane0, plane1)[d][:, e - WHOLE, :]
+        unturned = held.tile([P, E, PACK, P], F32, name="unturned")
 
         y = [held.tile([P, S], F32, name="y%d" % d) for d in range(PACK)]
 
@@ -131,7 +121,7 @@ def tile_moe_uni_none_kernel(
 
         def turn(copy, d, e0, e1, bank):
             for e in range(e0, e1):
-                nc.tensor.transpose(bank[:, slots(e - e0, e - e0 + 1)], plane(e, d), ident[:])
+                nc.tensor.transpose(bank[:, slots(e - e0, e - e0 + 1)], unturned[:, e, d, :], ident[:])
             copy(y[d][:, slots(e0, e1)], bank[:, slots(0, e1 - e0)])
 
         sums = []
@@ -144,27 +134,29 @@ def tile_moe_uni_none_kernel(
                 gather_scales(e, e + 2)
             sums.append(multiply_step1(e, slot_words[:]))
 
-        nc.scalar.activation(all_planes[:, 0, :, :], sums[0], COPY)
+        def empty(copy, e, d0, d1):
+            copy(unturned[:, e, d0:d1, :], sums[e][:, d0:d1, :])
+
+        nc.scalar.activation(unturned[:, 0, :, :], sums[0], COPY)
         for e in range(1, WHOLE):
-            nc.scalar.copy(all_planes[:, e, :, :], sums[e])
+            empty(nc.scalar.copy, e, 0, PACK)
         for e in range(WHOLE, LAST - 1):
-            nc.scalar.copy(plane(e, 0), sums[e][:, 0, :])
-        for e in (LAST - 1, LAST):
-            nc.vector.tensor_copy(plane(e, 0), sums[e][:, 0, :])
+            empty(nc.scalar.copy, e, 0, 1)
+        empty(nc.vector.tensor_copy, LAST - 1, 0, 2)
+        empty(nc.vector.tensor_copy, LAST, 0, 1)
 
         turn(nc.vector.tensor_copy, 0, 0, WHOLE, banks[0])
         turn(nc.scalar.copy, 0, WHOLE, LAST - 1, banks[1])
+        empty(nc.vector.tensor_copy, LAST, 1, PACK)
         turn(nc.vector.tensor_copy, 0, LAST - 1, E, banks[2])
-        for e in range(WHOLE, E):
-            nc.scalar.copy(plane(e, 1), sums[e][:, 1, :])
+        for e in range(WHOLE, LAST - 1):
+            empty(nc.scalar.copy, e, 1, 2)
         turn(nc.scalar.copy, 1, 0, HALF_E, banks[0])
         turn(nc.scalar.copy, 1, HALF_E, E, banks[1])
-        for e in range(WHOLE, E):
-            nc.scalar.copy(high_planes[:, e - WHOLE, :, :], sums[e][:, 2:, :])
+        for e in range(WHOLE, LAST):
+            empty(nc.scalar.copy, e, 2, PACK)
         turn(nc.scalar.copy, 2, 0, HALF_E, banks[2])
         turn(nc.scalar.copy, 2, HALF_E, E, banks[0])
-        turn(nc.scalar.copy, 3, 0, HALF_E, banks[3])
-        turn(nc.scalar.copy, 3, HALF_E, E, banks[4])
 
         def weigh(step, r, rows, terms, n, t0=0, t1=T):
             picked = rows[n][:].indirect(pos_sb[2 * step + r][:, entries(t0, t1)])
@@ -192,10 +184,14 @@ def tile_moe_uni_none_kernel(
                 nc.tensor.transpose(bank_back[:, block], turned_sum[:, block], ident[:])
             nc.scalar.copy(dst, bank_back[:, t0:t1])
 
-        for d, (bank_sum, bank_back) in enumerate(((0, 5), (6, 7))):
-            weigh(0, 0, y, c_terms, d)
-            weigh(0, 1, y, c_terms, d)
-            add_on_tensor(c_plane[d][:], c_terms, d, banks[bank_sum], banks[bank_back])
+        weigh(0, 0, y, c_terms, 0)
+        weigh(0, 1, y, c_terms, 0)
+        add_on_tensor(c_plane[0][:], c_terms, 0, banks[6], banks[5])
+        turn(nc.scalar.copy, 3, 0, HALF_E, banks[2])
+        turn(nc.scalar.copy, 3, HALF_E, E, banks[0])
+        weigh(0, 0, y, c_terms, 1)
+        weigh(0, 1, y, c_terms, 1)
+        add_on_tensor(c_plane[1][:], c_terms, 1, banks[2], banks[3])
         weigh(0, 0, y, c_terms, 2)
         weigh(0, 1, y, c_terms, 2)
         weigh(0, 0, y, c_terms, 3)
@@ -261,7 +257,7 @@ def tile_moe_uni_none_kernel(
 
         z = [held.tile([P, S], F32, name="z%d" % m) for m in range(ROW_TILES)]
 
-        def multiply_step2(m, e0, e1, bank):
+        def multiply_step2(m, e0, e1, bank, copy=nc.scalar.copy):
             for e in range(e0, e1):
                 column = e * K + m * P
                 nc.tensor.matmul_mx(
@@ -273,9 +269,10 @@ def tile_moe_uni_none_kernel(
                     start=True,
                     stop=True,
                 )
-            nc.scalar.copy(z[m][:, slots(e0, e1)], bank[:, slots(0, e1 - e0)])
+            copy(z[m][:, slots(e0, e1)], bank[:, slots(0, e1 - e0)])
 
-        for e0, e1, b in ((0, 4, 0), (4, 6, 4), (6, 7, 5), (7, 8, 6)):
+        multiply_step2(0, 0, HALF_E, banks[0], nc.vector.tensor_copy)
+        for e0, e1, b in ((4, 6, 4), (6, 7, 5), (7, 8, 6)):
             multiply_step2(0, e0, e1, banks[b])
         for m in range(1, ROW_TILES):
             multiply_step2(m, 0, HALF_E, banks[0])

@@ -67,6 +67,8 @@ def tile_moe_uni_none_kernel(
         nc.gpsimd.memset(w_scales_sb[:, :ZEROED_BY_GPSIMD], 0)
         nc.vector.memset(w_scales_sb[:, ZEROED_BY_GPSIMD:], 0)
         make_identity(nc, ident[:])
+        ident_bf16 = held.tile([P, P], BF16, name="ident_bf16")
+        make_identity(nc, ident_bf16[:])
 
         nc.sync.dma_start(x_words_sb[:], x_words[0].rearrange("p t d -> p (t d)").bitcast(I32))
         nc.sync.dma_start(offs_sb[:], offs)
@@ -166,7 +168,7 @@ def tile_moe_uni_none_kernel(
         c_plane = [held.tile([P, T], BF16, name="c_plane%d" % d) for d in range(2)]
         c_pair = held.tile([P, T, 2], BF16, name="c_pair")
 
-        def add_on_tensor(dst, terms, n, bank_sum, bank_back, t0=0, t1=T):
+        def add_on_tensor(dst, terms, n, bank_sum, bank_back, t0=0, t1=T, rounded=False):
             blocks = [slice(j * P, (j + 1) * P) for j in range(t0 // P, t1 // P)]
             for r in range(2):
                 for j, block in enumerate(blocks):
@@ -178,20 +180,25 @@ def tile_moe_uni_none_kernel(
                         stop=(r == 1 and j == len(blocks) - 1),
                         is_transpose=True,
                     )
-            turned_sum = ring.tile([P, T], F32, name="turned_sum")
+            if rounded:
+                turned_sum = ring.tile([P, T], BF16, name="rounded_sum")
+                back, unit = bank_back[:].bitcast(BF16), ident_bf16
+            else:
+                turned_sum = ring.tile([P, T], F32, name="turned_sum")
+                back, unit = bank_back[:], ident
             nc.scalar.copy(turned_sum[:, t0:t1], bank_sum[:, t0:t1])
             for block in blocks:
-                nc.tensor.transpose(bank_back[:, block], turned_sum[:, block], ident[:])
-            nc.scalar.copy(dst, bank_back[:, t0:t1])
+                nc.tensor.transpose(back[:, block], turned_sum[:, block], unit[:])
+            nc.scalar.copy(dst, back[:, t0:t1])
 
         weigh(0, 0, y, c_terms, 0)
         weigh(0, 1, y, c_terms, 0)
-        add_on_tensor(c_plane[0][:], c_terms, 0, banks[6], banks[5])
+        add_on_tensor(c_plane[0][:], c_terms, 0, banks[6], banks[5], rounded=True)
         turn(nc.scalar.copy, 3, 0, HALF_E, banks[2])
         turn(nc.scalar.copy, 3, HALF_E, E, banks[0])
         weigh(0, 0, y, c_terms, 1)
         weigh(0, 1, y, c_terms, 1)
-        add_on_tensor(c_plane[1][:], c_terms, 1, banks[2], banks[3])
+        add_on_tensor(c_plane[1][:], c_terms, 1, banks[2], banks[3], rounded=True)
         weigh(0, 0, y, c_terms, 2)
         weigh(0, 1, y, c_terms, 2)
         weigh(0, 0, y, c_terms, 3)

@@ -16,7 +16,7 @@ FLOPS = 2 * 2 * K * K * S
 
 WHOLE = 3
 LAST = E - 1
-WORD_RING = 4
+RING = 4
 STAGED = 6
 ZEROED_BY_GPSIMD = 512
 
@@ -48,7 +48,7 @@ def tile_moe_uni_none_kernel(
     with ExitStack() as ctx:
         lists = ctx.enter_context(tc.tile_pool(name="lists", bufs=1))
         held = ctx.enter_context(tc.tile_pool(name="held", bufs=1))
-        ring = ctx.enter_context(tc.tile_pool(name="ring", bufs=WORD_RING))
+        ring = ctx.enter_context(tc.tile_pool(name="ring", bufs=RING))
         psum = ctx.enter_context(tc.psum_pool(name="psum", bufs=1))
 
         offs_sb = lists.tile([P, S // PER_COLUMN], U16, name="offs_sb")
@@ -149,10 +149,10 @@ def tile_moe_uni_none_kernel(
 
         turn(nc.vector.tensor_copy, 0, 0, WHOLE, banks[0])
         turn(nc.scalar.copy, 0, WHOLE, LAST - 1, banks[1])
-        empty(nc.vector.tensor_copy, LAST, 1, PACK)
         turn(nc.vector.tensor_copy, 0, LAST - 1, E, banks[2])
         for e in range(WHOLE, LAST - 1):
             empty(nc.scalar.copy, e, 1, 2)
+        empty(nc.scalar.copy, LAST, 1, PACK)
         turn(nc.scalar.copy, 1, 0, HALF_E, banks[0])
         turn(nc.scalar.copy, 1, HALF_E, E, banks[1])
         for e in range(WHOLE, LAST):
@@ -250,17 +250,16 @@ def tile_moe_uni_none_kernel(
                 in_=grouped_flat[:, slots(PACK * e0, PACK * e1)],
             )
 
-        gather_pairs(0, 2)
-        gather_pairs(2, 4)
-        gather_pairs(4, 6)
-        gather_plane(1, 6, 7)
-        gather_plane(1, 7, 8)
+        for e in range(0, STAGED, 2):
+            gather_pairs(e, e + 2)
+        for e in range(STAGED, E):
+            gather_plane(1, e, e + 1)
         quantize(0, 2)
-        gather_pairs(6, 8)
-        quantize(2, 4)
-        quantize(4, 6)
-        quantize(6, 7)
-        quantize(7, 8)
+        gather_pairs(STAGED, E)
+        for e in range(2, STAGED, 2):
+            quantize(e, e + 2)
+        for e in range(STAGED, E):
+            quantize(e, e + 1)
 
         z = [held.tile([P, S], F32, name="z%d" % m) for m in range(ROW_TILES)]
 
@@ -279,7 +278,7 @@ def tile_moe_uni_none_kernel(
             copy(z[m][:, slots(e0, e1)], bank[:, slots(0, e1 - e0)])
 
         multiply_step2(0, 0, HALF_E, banks[0], nc.vector.tensor_copy)
-        for e0, e1, b in ((4, 6, 4), (6, 7, 5), (7, 8, 6)):
+        for e0, e1, b in ((HALF_E, STAGED, 4), (STAGED, LAST, 5), (LAST, E, 6)):
             multiply_step2(0, e0, e1, banks[b])
         for m in range(1, ROW_TILES):
             multiply_step2(m, 0, HALF_E, banks[0])

@@ -12,12 +12,13 @@ BANK = 512
 PER_COLUMN = 16
 SCALE_ROWS = K // 32
 HALF_E, HALF_T = E // 2, T // 2
+BLOCKS = T // P
+PAIRS = K // 2
 FLOPS = 2 * 2 * K * K * S
-
-WHOLE = 3
 LAST = E - 1
-RING = 4
 STAGED = 6
+DIRECT = 2
+WINDOW = 704
 ZEROED_BY_GPSIMD = 512
 
 F32 = mybir.dt.float32
@@ -41,6 +42,10 @@ def slots(e0, e1):
     return slice(e0 * C, e1 * C)
 
 
+def block(j):
+    return slice(j * P, (j + 1) * P)
+
+
 def tile_moe_uni_none_kernel(
     tc, x_words, x_scales, w_words, w_scales, gate1, gate2, offs, pos1, pos2, offs2, pos3, pos4, out
 ):
@@ -48,228 +53,263 @@ def tile_moe_uni_none_kernel(
     with ExitStack() as ctx:
         lists = ctx.enter_context(tc.tile_pool(name="lists", bufs=1))
         held = ctx.enter_context(tc.tile_pool(name="held", bufs=1))
-        ring = ctx.enter_context(tc.tile_pool(name="ring", bufs=RING))
         psum = ctx.enter_context(tc.psum_pool(name="psum", bufs=1))
 
         offs_sb = lists.tile([P, S // PER_COLUMN], U16, name="offs_sb")
         offs2_sb = lists.tile([P, S // PER_COLUMN], U16, name="offs2_sb")
         pos_sb = [lists.tile([P, T // PER_COLUMN], U16, name="pos%d_sb" % (n + 1)) for n in range(4)]
 
-        x_words_sb = held.tile([P, T], I32, name="x_words_sb", align_bytes=64)
-        x_scales_sb = held.tile([P, T // 4], I32, name="x_scales_sb", align_bytes=64)
-        w_words_sb = held.tile([P, E * 2 * K // 4], I32, name="w_words_sb", align_bytes=64)
+        x_words_sb = held.tile([P, WINDOW], I32, name="x_words_sb", align_bytes=64)
+        x_scales_sb = held.tile([P, WINDOW // 4], I32, name="x_scales_sb", tag="scales_then_words", align_bytes=64)
+        groups = ((0, HALF_E), (HALF_E, E))
+        w_words_sb = [
+            held.tile([P, (e1 - e0) * PAIRS], I32, name="w_words_sb%d" % e0, align_bytes=64) for e0, e1 in groups
+        ]
         w_scales_sb = held.tile([P, E * K // 4], I32, name="w_scales_sb", align_bytes=64)
         gates = [held.tile([P, 2, T], F32, name="gate%d_sb" % (step + 1)) for step in range(2)]
+        gate_columns = [
+            [held.tile([P, BLOCKS], F32, name="gate_columns%d%d" % (step, r)) for r in range(2)] for step in range(2)
+        ]
         ident = held.tile([P, P], F32, name="ident")
         banks = [psum.tile([P, BANK], F32, name="bank%d" % b) for b in range(8)]
 
         nc.gpsimd.memset(x_scales_sb[:], 0)
+        nc.gpsimd.memset(x_words_sb[:, T:], 0)
         nc.gpsimd.memset(w_scales_sb[:, :ZEROED_BY_GPSIMD], 0)
         nc.vector.memset(w_scales_sb[:, ZEROED_BY_GPSIMD:], 0)
         make_identity(nc, ident[:])
-        ident_bf16 = held.tile([P, P], BF16, name="ident_bf16")
-        make_identity(nc, ident_bf16[:])
 
-        nc.sync.dma_start(x_words_sb[:], x_words[0].rearrange("p t d -> p (t d)").bitcast(I32))
+        def load_words(g):
+            e0, e1 = groups[g]
+            nc.sync.dma_start(
+                w_words_sb[g][:].rearrange("p (e n) -> p e n", e=e1 - e0),
+                w_words[e0:e1, 0, :, :].rearrange("e p n -> p e n").bitcast(I32),
+            )
+
+        def load_gates(step, gate):
+            nc.sync.dma_start(gates[step][:], gate.rearrange("r p t -> p r t"))
+            with nc.allow_non_contiguous_dma(reason="one gate value a token and partition"):
+                for r in range(2):
+                    nc.sync.dma_start(gate_columns[step][r][:], gate[r, 0, :].rearrange("(j u) -> u j", u=P))
+
+        nc.sync.dma_start(x_words_sb[:, :T], x_words[0].rearrange("p t d -> p (t d)").bitcast(I32))
         nc.sync.dma_start(offs_sb[:], offs)
         for r in range(4):
-            nc.sync.dma_start(x_scales_sb[r:P:32, :], x_scales[0, r:SCALE_ROWS:4, :].bitcast(I32))
-        w_words_by_expert = w_words_sb[:].rearrange("p (e n) -> p e n", e=E)
-        w_words_hbm = w_words[:, 0, :, :].rearrange("e p n -> p e n").bitcast(I32)
-        nc.sync.dma_start(w_words_by_expert[:, :2, :], w_words_hbm[:, :2, :])
+            nc.sync.dma_start(x_scales_sb[r:P:32, : T // 4], x_scales[0, r:SCALE_ROWS:4, :].bitcast(I32))
+        load_words(0)
         for r in range(4):
             nc.sync.dma_start(
                 w_scales_sb[r:P:32, :].rearrange("q (e n) -> q e n", e=E),
                 w_scales[:, 0, r:SCALE_ROWS:4, :].rearrange("e q n -> q e n").bitcast(I32),
             )
-        nc.sync.dma_start(w_words_by_expert[:, 2:HALF_E, :], w_words_hbm[:, 2:HALF_E, :])
-        nc.sync.dma_start(w_words_by_expert[:, HALF_E:, :], w_words_hbm[:, HALF_E:, :])
+        load_words(1)
         nc.sync.dma_start(pos_sb[0][:], pos1)
         nc.sync.dma_start(pos_sb[1][:], pos2)
-        nc.sync.dma_start(gates[0][:], gate1.rearrange("r p t -> p r t"))
+        load_gates(0, gate1)
         nc.sync.dma_start(offs2_sb[:], offs2)
         nc.sync.dma_start(pos_sb[2][:], pos3)
         nc.sync.dma_start(pos_sb[3][:], pos4)
-        nc.sync.dma_start(gates[1][:], gate2.rearrange("r p t -> p r t"))
+        load_gates(1, gate2)
 
-        w_word_bytes = w_words_sb[:].bitcast(U8)
+        def group_of(e, among):
+            return [g for g, (e0, e1) in enumerate(among) if e0 <= e < e1][0]
+
+        word_pieces = ((0, 4), (4, 8))
+        scale_pieces = ((0, 4), (4, 8))
+        early_words = held.tile([P, HALF_E * C], U32, name="early_words", align_bytes=64)
+        slot_scales = [held.tile([P, (b - a) * C], U8, name="slot_scales%d" % a, align_bytes=64) for a, b in scale_pieces]
+
+        def gather_words(dst, a, b):
+            nc.vector.tensor_copy(dst, x_words_sb[:].bitcast(U32).indirect(offs_sb[:, entries(a * C, b * C)]))
+
+        def gather_scales(n):
+            a, b = scale_pieces[n]
+            nc.vector.tensor_copy(slot_scales[n][:], x_scales_sb[:].bitcast(U8).indirect(offs_sb[:, entries(a * C, b * C)]))
+
+        gather_words(early_words[:], 0, HALF_E)
+        gather_scales(0)
+        gather_scales(1)
+        late_words = held.tile([P, HALF_E * C], U32, name="late_words", tag="scales_then_words", align_bytes=64)
+        for a, b in ((4, 6), (6, 7), (7, 8)):
+            gather_words(late_words[:, slots(a - HALF_E, b - HALF_E)], a, b)
+        slot_words = [early_words, late_words]
+
+        pair_words = [held.tile([P, 2, HALF_E, P // 2], U32, name="pair_words%d" % g, align_bytes=64) for g in range(2)]
+        pair_scales = [held.tile([P, 2, HALF_E, P // 2], U16, name="pair_scales%d" % g, align_bytes=64) for g in range(2)]
         w_scale_bytes = w_scales_sb[:].bitcast(U8)
 
-        slot_scales = held.tile([P, S], U8, name="slot_scales", align_bytes=64)
+        def sort_words(g, copy=nc.scalar.copy):
+            pairs = w_words_sb[g][:].bitcast(U32).rearrange("p (e h q u) -> p h u e q", e=HALF_E, h=2, u=2)
+            copy(pair_words[g][:], pairs[:, 1])
 
-        def gather_words(dst, e0, e1):
-            window = x_words_sb[:].bitcast(U32)
-            nc.vector.tensor_copy(dst, window.indirect(offs_sb[:, entries(e0 * C, e1 * C)]))
+        def sort_scales(g, copy=nc.scalar.copy):
+            pairs = w_scales_sb[:].bitcast(U16).rearrange("p (g e h q u) -> p g h u e q", g=2, e=HALF_E, h=2, u=2)
+            copy(pair_scales[g][:], pairs[:, g, 1])
 
-        def gather_scales(e0, e1):
-            window = x_scales_sb[:].bitcast(U8)
-            nc.vector.tensor_copy(slot_scales[:, slots(e0, e1)], window.indirect(offs_sb[:, entries(e0 * C, e1 * C)]))
+        def natural(e, m):
+            g = group_of(e, groups)
+            column = (e - groups[g][0]) * K + m * P
+            words = w_words_sb[g][:].bitcast(U8)[:, 2 * column : 2 * (column + P)]
+            return words.bitcast(FP4X4), w_scale_bytes[:, e * K + m * P : e * K + (m + 1) * P]
 
-        unturned = held.tile([P, E, PACK, P], F32, name="unturned")
+        def sorted_pairs(e, u):
+            g, i = divmod(e, HALF_E)
+            return pair_words[g][:, u, i, :].bitcast(U8).bitcast(FP4X4), pair_scales[g][:, u, i, :].bitcast(U8)
 
-        y = [held.tile([P, S], F32, name="y%d" % d) for d in range(PACK)]
+        y = [held.tile([P, S], F32, name="y%d" % n) for n in range(ROW_TILES)]
 
-        def multiply_step1(e, slot_words):
-            nc.tensor.matmul_mx(
-                banks[e][:],
-                lhsT=slot_words.bitcast(FP8X4),
-                lhsT_scale=slot_scales[:, slots(e, e + 1)],
-                rhs=w_word_bytes[:, e * 2 * K : (e + 1) * 2 * K].bitcast(FP4X4),
-                rhs_scale=w_scale_bytes[:, e * K : (e + 1) * K],
-                start=True,
-                stop=True,
-            )
-            return banks[e][:].rearrange("s (p d) -> s d p", d=PACK)
-
-        def turn(copy, d, e0, e1, bank):
+        def multiply_step1(n, e0, e1, bank, copy=nc.scalar.copy):
             for e in range(e0, e1):
-                nc.tensor.transpose(bank[:, slots(e - e0, e - e0 + 1)], unturned[:, e, d, :], ident[:])
-            copy(y[d][:, slots(e0, e1)], bank[:, slots(0, e1 - e0)])
+                words, scales = natural(e, n) if n < 2 else sorted_pairs(e, n - 2)
+                tw, ts = group_of(e, word_pieces), group_of(e, scale_pieces)
+                ew, es = e - word_pieces[tw][0], e - scale_pieces[ts][0]
+                nc.tensor.matmul_mx(
+                    bank[:, slots(e - e0, e - e0 + 1)],
+                    lhsT=words,
+                    lhsT_scale=scales,
+                    rhs=slot_words[tw][:, slots(ew, ew + 1)].bitcast(FP8X4),
+                    rhs_scale=slot_scales[ts][:, slots(es, es + 1)],
+                    start=True,
+                    stop=True,
+                )
+            copy(y[n][:, slots(e0, e1)], bank[:, slots(0, e1 - e0)])
 
-        sums = []
-        for e in range(E):
-            slot_words = ring.tile([P, C], U32, name="slot_words", align_bytes=64)
-            gather_words(slot_words[:], e, e + 1)
-            if e < 2:
-                gather_scales(e, e + 1)
-            elif e % 2 == 0:
-                gather_scales(e, e + 2)
-            sums.append(multiply_step1(e, slot_words[:]))
+        def first_copy(dst, src):
+            nc.scalar.activation(dst, src, COPY)
 
-        def empty(copy, e, d0, d1):
-            copy(unturned[:, e, d0:d1, :], sums[e][:, d0:d1, :])
-
-        nc.scalar.activation(unturned[:, 0, :, :], sums[0], COPY)
-        for e in range(1, WHOLE):
-            empty(nc.scalar.copy, e, 0, PACK)
-        for e in range(WHOLE, LAST - 1):
-            empty(nc.scalar.copy, e, 0, 1)
-        empty(nc.vector.tensor_copy, LAST - 1, 0, 2)
-        empty(nc.vector.tensor_copy, LAST, 0, 1)
-
-        turn(nc.vector.tensor_copy, 0, 0, WHOLE, banks[0])
-        turn(nc.scalar.copy, 0, WHOLE, LAST - 1, banks[1])
-        turn(nc.vector.tensor_copy, 0, LAST - 1, E, banks[2])
-        for e in range(WHOLE, LAST - 1):
-            empty(nc.scalar.copy, e, 1, 2)
-        empty(nc.scalar.copy, LAST, 1, PACK)
-        turn(nc.scalar.copy, 1, 0, HALF_E, banks[0])
-        turn(nc.scalar.copy, 1, HALF_E, E, banks[1])
-        for e in range(WHOLE, LAST):
-            empty(nc.scalar.copy, e, 2, PACK)
-        turn(nc.scalar.copy, 2, 0, HALF_E, banks[2])
-        turn(nc.scalar.copy, 2, HALF_E, E, banks[0])
+        sort_words(0)
+        sort_scales(0)
+        sort_scales(1)
+        sort_words(1)
+        multiply_step1(0, 0, HALF_E, banks[0], first_copy)
+        multiply_step1(0, HALF_E, LAST, banks[1], nc.vector.tensor_copy)
+        multiply_step1(0, LAST, E, banks[2], nc.vector.tensor_copy)
+        multiply_step1(2, 0, HALF_E, banks[5])
+        multiply_step1(1, 0, HALF_E, banks[3])
+        multiply_step1(2, HALF_E, E, banks[6])
+        multiply_step1(1, HALF_E, E, banks[4])
 
         def weigh(step, r, rows, terms, n, t0=0, t1=T):
             picked = rows[n][:].indirect(pos_sb[2 * step + r][:, entries(t0, t1)])
-            nc.vector.tensor_tensor(terms[r][:, n, t0:t1], picked, gates[step][:, r, t0:t1], MULT)
+            nc.vector.tensor_tensor(terms[r][n][:, t0:t1], picked, gates[step][:, r, t0:t1], MULT)
 
-        c_terms = [held.tile([P, PACK, T], F32, name="c_terms%d" % r) for r in range(2)]
-        c_plane = [held.tile([P, T], BF16, name="c_plane%d" % d) for d in range(2)]
-        c_pair = held.tile([P, T, 2], BF16, name="c_pair")
+        def pick(step, r, rows, terms, n, bank):
+            nc.scalar.activation(terms[r][n][:], rows[n][:].indirect(pos_sb[2 * step + r][:]), COPY)
+            for j in range(BLOCKS):
+                nc.tensor.transpose(bank[:, block(j)], terms[r][n][:, block(j)], ident[:])
 
-        def add_on_tensor(dst, terms, n, bank_sum, bank_back, t0=0, t1=T, rounded=False):
-            blocks = [slice(j * P, (j + 1) * P) for j in range(t0 // P, t1 // P)]
-            for r in range(2):
-                for j, block in enumerate(blocks):
-                    nc.tensor.matmul(
-                        bank_sum[:, block],
-                        lhsT=terms[r][:, n, block],
-                        rhs=ident[:],
-                        start=(r == 0 and j == 0),
-                        stop=(r == 1 and j == len(blocks) - 1),
-                        is_transpose=True,
-                    )
-            if rounded:
-                turned_sum = ring.tile([P, T], BF16, name="rounded_sum")
-                back, unit = bank_back[:].bitcast(BF16), ident_bf16
-            else:
-                turned_sum = ring.tile([P, T], F32, name="turned_sum")
-                back, unit = bank_back[:], ident
-            nc.scalar.copy(turned_sum[:, t0:t1], bank_sum[:, t0:t1])
-            for block in blocks:
-                nc.tensor.transpose(back[:, block], turned_sum[:, block], unit[:])
-            nc.scalar.copy(dst, back[:, t0:t1])
+        def add_turned(bank, parts):
+            for i, (columns, source) in enumerate(parts):
+                nc.tensor.matmul(
+                    bank[:, columns], lhsT=source, rhs=ident[:], start=(i == 0), stop=(i == len(parts) - 1), is_transpose=True
+                )
 
-        weigh(0, 0, y, c_terms, 0)
-        weigh(0, 1, y, c_terms, 0)
-        add_on_tensor(c_plane[0][:], c_terms, 0, banks[6], banks[5], rounded=True)
-        turn(nc.scalar.copy, 3, 0, HALF_E, banks[2])
-        turn(nc.scalar.copy, 3, HALF_E, E, banks[0])
-        weigh(0, 0, y, c_terms, 1)
-        weigh(0, 1, y, c_terms, 1)
-        add_on_tensor(c_plane[1][:], c_terms, 1, banks[2], banks[3], rounded=True)
-        weigh(0, 0, y, c_terms, 2)
-        weigh(0, 1, y, c_terms, 2)
-        weigh(0, 0, y, c_terms, 3)
-        weigh(0, 1, y, c_terms, 3, 0, HALF_T)
-        weigh(0, 1, y, c_terms, 3, HALF_T, T)
-        for t0 in (0, HALF_T):
-            tokens = slice(t0, t0 + HALF_T)
-            nc.vector.tensor_tensor(
-                c_pair[:, tokens, :].rearrange("p (g i) d -> p g d i", i=4),
-                c_terms[0][:, 2:, tokens].rearrange("p d (g i) -> p g d i", i=4),
-                c_terms[1][:, 2:, tokens].rearrange("p d (g i) -> p g d i", i=4),
-                ADD,
+        c_terms = [[held.tile([P, T], F32, name="c_terms%d%d" % (r, n)) for n in range(ROW_TILES)] for r in range(2)]
+        c_turned = held.tile([P, 2, BLOCKS, 2, P], BF16, name="c_turned")
+        c_pair = [held.tile([P, T], F32, name="c_pair%d" % u) for u in range(2)]
+        weighed = held.tile([P, T], F32, name="weighed")
+
+        def turn_back(u, bank):
+            words = c_turned[:, u].rearrange("p j h q -> p (j h q)").bitcast(F32)
+            for j in range(BLOCKS):
+                nc.tensor.transpose(bank[:, block(j)], words[:, block(j)], ident[:])
+            nc.scalar.copy(c_pair[u][:], bank[:])
+
+        def sum_pair0(half, bank):
+            add_turned(
+                bank,
+                [
+                    (block(2 * jj + h), c_terms[r][h][:, block(2 * half + jj)])
+                    for h in range(2)
+                    for r in range(2)
+                    for jj in range(2)
+                ],
+            )
+            nc.scalar.copy(
+                c_turned[:, :, 2 * half : 2 * half + 2, 0, :].rearrange("p u j (q e) -> p u j q e", e=2),
+                bank[:].rearrange("p (j q u e) -> p u j q e", j=2, u=2, e=2),
             )
 
-        staged = held.tile([P, 2, STAGED * C, 2], BF16, name="staged", align_bytes=64)
-        grouped = held.tile([P, S, PACK], BF16, name="grouped", align_bytes=64)
+        def scale_picked(dst, bank, step, r):
+            for j in range(BLOCKS):
+                nc.scalar.activation(dst[:, block(j)], bank[:, block(j)], COPY, scale=gate_columns[step][r][:, j : j + 1])
+
+        def join_tile3(bank):
+            for j in range(BLOCKS):
+                nc.vector.scalar_tensor_tensor(
+                    c_turned[:, 0, j, 1, :], bank[:, block(j)], gate_columns[0][0][:, j : j + 1], weighed[:, block(j)], MULT, ADD
+                )
+
+        def sum_tile2(bank):
+            add_turned(bank, [(block(j), c_terms[r][3][:, block(j)]) for r in range(2) for j in range(BLOCKS)])
+            nc.scalar.copy(c_turned[:, 1, :, 1, :], bank[:].rearrange("p (j q) -> p j q", j=BLOCKS))
+
+        staged = held.tile([P, 2 * STAGED * C], U32, name="staged", align_bytes=64)
+        grouped = [held.tile([P, 2 * C * 2], U32, name="grouped%d" % e, align_bytes=64)[:] for e in (0, 2, 4, 6)]
         c_words = held.tile([P, S], U32, name="c_words", align_bytes=64)
         c_scales = held.tile([P, S], U8, name="c_scales", align_bytes=64)
 
-        def gather_plane(d, e0, e1):
-            dst = staged[:, 0, slots(e0, e1), d] if e1 <= STAGED else grouped[:, slots(e0, e1), d]
-            picked = c_plane[d][:].indirect(offs2_sb[:, entries(e0 * C, e1 * C)])
-            nc.scalar.activation(dst, picked, COPY)
-
-        for d in range(2):
-            gather_plane(d, 0, STAGED // 2)
-            gather_plane(d, STAGED // 2, STAGED)
-        gather_plane(0, STAGED, E)
-
-        c_pair_words = c_pair[:].rearrange("p t d -> p (t d)").bitcast(U32)
-        staged_flat = staged[:].rearrange("p u s d -> p (u s d)")
-        grouped_flat = grouped[:].rearrange("p s d -> p (s d)")
-
-        def gather_pairs(e0, e1):
-            picked = c_pair_words.indirect(offs2_sb[:, entries(e0 * C, e1 * C)])
-            if e1 <= STAGED:
-                nc.vector.tensor_copy(staged_flat.bitcast(U32)[:, slots(STAGED + e0, STAGED + e1)], picked)
-                nc.scalar.copy(
-                    grouped_flat.bitcast(F32).rearrange("p (s u) -> p s u", u=2)[:, slots(e0, e1), :],
-                    staged_flat.bitcast(F32).rearrange("p (u s) -> p s u", u=2)[:, slots(e0, e1), :],
-                )
+        def gather_pairs(u, e0, e1):
+            picked = c_pair[u][:].bitcast(U32).indirect(offs2_sb[:, entries(e0 * C, e1 * C)])
+            if e0 >= DIRECT:
+                nc.vector.tensor_copy(staged[:, slots(u * STAGED + e0 - DIRECT, u * STAGED + e1 - DIRECT)], picked)
             else:
-                nc.vector.tensor_copy(grouped_flat.bitcast(U32)[:, 2 * e0 * C + 1 : 2 * e1 * C : 2], picked)
+                nc.vector.tensor_copy(grouped[e0 // 2][:, u::2], picked)
+
+        def interleave(e0, e1):
+            nc.scalar.copy(
+                grouped[e0 // 2].rearrange("p (s u) -> p s u", u=2)[:, slots(e0 % 2, e0 % 2 + e1 - e0), :],
+                staged[:].rearrange("p (u s) -> p s u", u=2)[:, slots(e0 - DIRECT, e1 - DIRECT), :],
+            )
 
         def quantize(e0, e1):
+            first = e0 % 2 * PACK * C
             nc.vector.quantize_mx(
                 out=c_words[:, slots(e0, e1)].bitcast(FP8X4),
                 scales=c_scales[:, slots(e0, e1)],
-                in_=grouped_flat[:, slots(PACK * e0, PACK * e1)],
+                in_=grouped[e0 // 2].bitcast(BF16)[:, first : first + (e1 - e0) * PACK * C],
             )
 
-        for e in range(0, STAGED, 2):
-            gather_pairs(e, e + 2)
-        for e in range(STAGED, E):
-            gather_plane(1, e, e + 1)
+        for n in range(2):
+            weigh(0, 0, y, c_terms, n)
+            weigh(0, 1, y, c_terms, n)
+        pick(0, 1, y, c_terms, 2, banks[3])
+        pick(0, 0, y, c_terms, 2, banks[4])
+        scale_picked(weighed, banks[3], 0, 1)
+        join_tile3(banks[4])
+        multiply_step1(3, 0, HALF_E, banks[7])
+        multiply_step1(3, HALF_E, E, banks[0])
+        weigh(0, 0, y, c_terms, 3)
+        weigh(0, 1, y, c_terms, 3)
+        sum_pair0(0, banks[1])
+        sum_pair0(1, banks[2])
+        turn_back(0, banks[5])
+        sum_tile2(banks[2])
+        turn_back(1, banks[6])
+        gather_pairs(0, 2, 5)
+        gather_pairs(0, 5, 8)
+        gather_pairs(0, 0, 2)
+        gather_pairs(1, 0, 2)
+        gather_pairs(1, 2, 4)
+        interleave(2, 4)
         quantize(0, 2)
-        gather_pairs(STAGED, E)
-        for e in range(2, STAGED, 2):
-            quantize(e, e + 2)
-        for e in range(STAGED, E):
-            quantize(e, e + 1)
+        gather_pairs(1, 4, 6)
+        interleave(4, 6)
+        quantize(2, 4)
+        gather_pairs(1, 6, 8)
+        interleave(6, 8)
+        quantize(4, 6)
+        quantize(6, 8)
 
         z = [held.tile([P, S], F32, name="z%d" % m) for m in range(ROW_TILES)]
 
         def multiply_step2(m, e0, e1, bank, copy=nc.scalar.copy):
             for e in range(e0, e1):
-                column = e * K + m * P
+                words, scales = natural(e, m)
                 nc.tensor.matmul_mx(
                     bank[:, slots(e - e0, e - e0 + 1)],
-                    lhsT=w_word_bytes[:, 2 * column : 2 * (column + P)].bitcast(FP4X4),
-                    lhsT_scale=w_scale_bytes[:, column : column + P],
+                    lhsT=words,
+                    lhsT_scale=scales,
                     rhs=c_words[:, slots(e, e + 1)].bitcast(FP8X4),
                     rhs_scale=c_scales[:, slots(e, e + 1)],
                     start=True,
@@ -277,35 +317,43 @@ def tile_moe_uni_none_kernel(
                 )
             copy(z[m][:, slots(e0, e1)], bank[:, slots(0, e1 - e0)])
 
-        multiply_step2(0, 0, HALF_E, banks[0], nc.vector.tensor_copy)
-        for e0, e1, b in ((HALF_E, STAGED, 4), (STAGED, LAST, 5), (LAST, E, 6)):
-            multiply_step2(0, e0, e1, banks[b])
-        for m in range(1, ROW_TILES):
-            multiply_step2(m, 0, HALF_E, banks[0])
-            multiply_step2(m, HALF_E, E, banks[6])
+        multiply_step2(0, 0, HALF_E, banks[0])
+        multiply_step2(0, HALF_E, 6, banks[1])
+        multiply_step2(0, 6, E, banks[2], nc.vector.tensor_copy)
+        for m, early, middle, late in ((1, banks[3][:, :256], 0, 5), (2, banks[3][:, 256:], 1, 6), (3, banks[4], 2, 7)):
+            multiply_step2(m, 0, 2, early)
+            multiply_step2(m, 2, 6, banks[middle])
+            multiply_step2(m, 6, E, banks[late])
 
-        out_terms = [held.tile([P, ROW_TILES, T], F32, name="out_terms%d" % r) for r in range(2)]
+        out_terms = [[held.tile([P, T], F32, name="out_terms%d%d" % (r, m)) for m in range(ROW_TILES)] for r in range(2)]
         result = held.tile([P, ROW_TILES, T], F32, name="result")
+        out_weighed = [held.tile([P, T], F32, name="out_weighed%d" % r) for r in range(2)]
 
         def finish_on_vector(m, t0, t1):
-            nc.vector.tensor_tensor(result[:, m, t0:t1], out_terms[0][:, m, t0:t1], out_terms[1][:, m, t0:t1], ADD)
-            nc.sync.dma_start(out[m * P : (m + 1) * P, t0:t1], result[:, m, t0:t1])
+            nc.vector.tensor_tensor(result[:, m, t0:t1], out_terms[0][m][:, t0:t1], out_terms[1][m][:, t0:t1], ADD)
+            nc.sync.dma_start(out[block(m), t0:t1], result[:, m, t0:t1])
 
-        def finish_on_tensor(m, bank_sum, bank_back, t0=0, t1=T):
-            add_on_tensor(result[:, m, t0:t1], out_terms, m, bank_sum, bank_back, t0, t1)
-            nc.scalar.dma_start(out[m * P : (m + 1) * P, t0:t1], result[:, m, t0:t1])
+        def combine_on_scalar(m, banks_turned, banks_back):
+            for r in range(2):
+                pick(1, r, z, out_terms, m, banks_turned[r])
+            for r in range(2):
+                scale_picked(out_weighed[r], banks_turned[r], 1, r)
+            for half, bank in enumerate(banks_back):
+                add_turned(bank, [(block(jj), out_weighed[r][:, block(2 * half + jj)]) for r in range(2) for jj in range(2)])
+                tokens = slice(half * HALF_T, (half + 1) * HALF_T)
+                nc.scalar.copy(result[:, m, tokens], bank[:, :HALF_T])
+                nc.scalar.dma_start(out[block(m), tokens], result[:, m, tokens])
 
-        for m, (bank_sum, bank_back) in enumerate(((1, 2), (3, 4))):
-            weigh(1, 0, z, out_terms, m)
-            weigh(1, 1, z, out_terms, m)
-            finish_on_tensor(m, banks[bank_sum], banks[bank_back])
-        weigh(1, 0, z, out_terms, 2)
-        for t0, bank_sum, bank_back in ((0, 5, 7), (HALF_T, 1, 2)):
-            weigh(1, 1, z, out_terms, 2, t0, t0 + HALF_T)
-            finish_on_tensor(2, banks[bank_sum], banks[bank_back], t0, t0 + HALF_T)
-        weigh(1, 0, z, out_terms, 3, 0, HALF_T)
-        weigh(1, 1, z, out_terms, 3, 0, HALF_T)
-        weigh(1, 0, z, out_terms, 3, HALF_T, T)
-        finish_on_vector(3, 0, HALF_T)
-        weigh(1, 1, z, out_terms, 3, HALF_T, T)
-        finish_on_vector(3, HALF_T, T)
+        combine_on_scalar(3, (banks[3], banks[4]), (banks[5], banks[6]))
+        weigh(1, 0, z, out_terms, 0)
+        weigh(1, 1, z, out_terms, 0)
+        weigh(1, 0, z, out_terms, 1)
+        finish_on_vector(0, 0, T)
+        weigh(1, 1, z, out_terms, 1)
+        weigh(1, 0, z, out_terms, 2, 0, HALF_T)
+        finish_on_vector(1, 0, T)
+        weigh(1, 1, z, out_terms, 2, 0, HALF_T)
+        weigh(1, 0, z, out_terms, 2, HALF_T, T)
+        finish_on_vector(2, 0, HALF_T)
+        weigh(1, 1, z, out_terms, 2, HALF_T, T)
+        finish_on_vector(2, HALF_T, T)

@@ -67,9 +67,7 @@ def tile_moe_uni_none_kernel(
         ]
         w_scales_sb = held.tile([P, E * K // 4], I32, name="w_scales_sb", align_bytes=64)
         gates = [held.tile([P, 2, T], F32, name="gate%d_sb" % (step + 1)) for step in range(2)]
-        gate_columns = [
-            [held.tile([P, BLOCKS], F32, name="gate_columns%d%d" % (step, r)) for r in range(2)] for step in range(2)
-        ]
+        gate_columns = [held.tile([P, 2, BLOCKS], F32, name="gate_columns%d" % step) for step in range(2)]
         ident = held.tile([P, P], F32, name="ident")
         banks = [psum.tile([P, BANK], F32, name="bank%d" % b) for b in range(8)]
 
@@ -88,9 +86,6 @@ def tile_moe_uni_none_kernel(
 
         def load_gates(step, gate):
             nc.sync.dma_start(gates[step][:], gate.rearrange("r p t -> p r t"))
-            with nc.allow_non_contiguous_dma(reason="one gate value a token and partition"):
-                for r in range(2):
-                    nc.sync.dma_start(gate_columns[step][r][:], gate[r, 0, :].rearrange("(j u) -> u j", u=P))
 
         nc.sync.dma_start(x_words_sb[:, :T], x_words[0].rearrange("p t d -> p (t d)").bitcast(I32))
         nc.sync.dma_start(offs_sb[:], offs)
@@ -180,7 +175,7 @@ def tile_moe_uni_none_kernel(
         sort_words(0)
         sort_scales(0)
         sort_scales(1)
-        sort_words(1)
+        sort_words(1, nc.gpsimd.tensor_copy)
         multiply_step1(0, 0, HALF_E, banks[0], first_copy)
         multiply_step1(0, HALF_E, LAST, banks[1], nc.vector.tensor_copy)
         multiply_step1(0, LAST, E, banks[2], nc.vector.tensor_copy)
@@ -197,6 +192,12 @@ def tile_moe_uni_none_kernel(
             nc.scalar.activation(terms[r][n][:], rows[n][:].indirect(pos_sb[2 * step + r][:]), COPY)
             for j in range(BLOCKS):
                 nc.tensor.transpose(bank[:, block(j)], terms[r][n][:, block(j)], ident[:])
+
+        def turn_gates(step, two_banks):
+            for r, bank in enumerate(two_banks):
+                for j in range(BLOCKS):
+                    nc.tensor.transpose(bank[:, block(j)], gates[step][:, r, block(j)], ident[:])
+                nc.scalar.copy(gate_columns[step][:, r, :], bank[:, 0:BANK:P])
 
         def add_turned(bank, parts):
             for i, (columns, source) in enumerate(parts):
@@ -232,12 +233,12 @@ def tile_moe_uni_none_kernel(
 
         def scale_picked(dst, bank, step, r):
             for j in range(BLOCKS):
-                nc.scalar.activation(dst[:, block(j)], bank[:, block(j)], COPY, scale=gate_columns[step][r][:, j : j + 1])
+                nc.scalar.activation(dst[:, block(j)], bank[:, block(j)], COPY, scale=gate_columns[step][:, r, j : j + 1])
 
         def join_tile3(bank):
             for j in range(BLOCKS):
                 nc.vector.scalar_tensor_tensor(
-                    c_turned[:, 0, j, 1, :], bank[:, block(j)], gate_columns[0][0][:, j : j + 1], weighed[:, block(j)], MULT, ADD
+                    c_turned[:, 0, j, 1, :], bank[:, block(j)], gate_columns[0][:, 0, j : j + 1], weighed[:, block(j)], MULT, ADD
                 )
 
         def sum_tile2(bank):
@@ -273,6 +274,7 @@ def tile_moe_uni_none_kernel(
         for n in range(2):
             weigh(0, 0, y, c_terms, n)
             weigh(0, 1, y, c_terms, n)
+        turn_gates(0, (banks[5], banks[6]))
         pick(0, 1, y, c_terms, 2, banks[3])
         pick(0, 0, y, c_terms, 2, banks[4])
         scale_picked(weighed, banks[3], 0, 1)
@@ -286,6 +288,7 @@ def tile_moe_uni_none_kernel(
         turn_back(0, banks[5])
         sum_tile2(banks[2])
         turn_back(1, banks[6])
+        turn_gates(1, (banks[2], banks[6]))
         gather_pairs(0, 2, 5)
         gather_pairs(0, 5, 8)
         gather_pairs(0, 0, 2)

@@ -75,7 +75,9 @@ def tile_moe_uni_none_kernel(
         nc.gpsimd.memset(x_words_sb[:, T:], 0)
         nc.gpsimd.memset(w_scales_sb[:, :ZEROED_BY_GPSIMD], 0)
         nc.vector.memset(w_scales_sb[:, ZEROED_BY_GPSIMD:], 0)
-        make_identity(nc, ident[:])
+        ident_bf16 = held.tile([P, P], BF16, name="ident_bf16")
+        make_identity(nc, ident_bf16[:])
+        nc.scalar.activation(ident[:], ident_bf16[:], COPY)
 
         def load_words(g):
             e0, e1 = groups[g]
@@ -91,12 +93,12 @@ def tile_moe_uni_none_kernel(
         nc.sync.dma_start(offs_sb[:], offs)
         for r in range(4):
             nc.sync.dma_start(x_scales_sb[r:P:32, : T // 4], x_scales[0, r:SCALE_ROWS:4, :].bitcast(I32))
-        load_words(0)
         for r in range(4):
             nc.sync.dma_start(
                 w_scales_sb[r:P:32, :].rearrange("q (e n) -> q e n", e=E),
                 w_scales[:, 0, r:SCALE_ROWS:4, :].rearrange("e q n -> q e n").bitcast(I32),
             )
+        load_words(0)
         load_words(1)
         nc.sync.dma_start(pos_sb[0][:], pos1)
         nc.sync.dma_start(pos_sb[1][:], pos2)
@@ -210,11 +212,11 @@ def tile_moe_uni_none_kernel(
         c_pair = [held.tile([P, T], F32, name="c_pair%d" % u) for u in range(2)]
         weighed = held.tile([P, T], F32, name="weighed")
 
-        def turn_back(u, bank):
+        def turn_back(u, bank, j0=0, j1=BLOCKS):
             words = c_turned[:, u].rearrange("p j h q -> p (j h q)").bitcast(F32)
-            for j in range(BLOCKS):
+            for j in range(j0, j1):
                 nc.tensor.transpose(bank[:, block(j)], words[:, block(j)], ident[:])
-            nc.scalar.copy(c_pair[u][:], bank[:])
+            nc.scalar.copy(c_pair[u][:, j0 * P : j1 * P], bank[:, j0 * P : j1 * P])
 
         def sum_pair0(half, bank):
             add_turned(
@@ -241,9 +243,11 @@ def tile_moe_uni_none_kernel(
                     c_turned[:, 0, j, 1, :], bank[:, block(j)], gate_columns[0][:, 0, j : j + 1], weighed[:, block(j)], MULT, ADD
                 )
 
-        def sum_tile2(bank):
-            add_turned(bank, [(block(j), c_terms[r][3][:, block(j)]) for r in range(2) for j in range(BLOCKS)])
-            nc.scalar.copy(c_turned[:, 1, :, 1, :], bank[:].rearrange("p (j q) -> p j q", j=BLOCKS))
+        def sum_tile2(half, bank):
+            add_turned(bank, [(block(jj), c_terms[r][3][:, block(2 * half + jj)]) for r in range(2) for jj in range(2)])
+            nc.scalar.copy(
+                c_turned[:, 1, 2 * half : 2 * half + 2, 1, :], bank[:, :HALF_T].rearrange("p (j q) -> p j q", j=2)
+            )
 
         staged = held.tile([P, 2 * STAGED * C], U32, name="staged", align_bytes=64)
         grouped = [held.tile([P, 2 * C * 2], U32, name="grouped%d" % e, align_bytes=64)[:] for e in (0, 2, 4, 6)]
@@ -282,13 +286,16 @@ def tile_moe_uni_none_kernel(
         multiply_step1(3, 0, HALF_E, banks[7])
         multiply_step1(3, HALF_E, E, banks[0])
         weigh(0, 0, y, c_terms, 3)
-        weigh(0, 1, y, c_terms, 3)
+        weigh(0, 1, y, c_terms, 3, 0, HALF_T)
+        weigh(0, 1, y, c_terms, 3, HALF_T, T)
         sum_pair0(0, banks[1])
         sum_pair0(1, banks[2])
         turn_back(0, banks[5])
-        sum_tile2(banks[2])
-        turn_back(1, banks[6])
-        turn_gates(1, (banks[2], banks[6]))
+        sum_tile2(0, banks[2])
+        sum_tile2(1, banks[5])
+        turn_back(1, banks[6], 0, 2)
+        turn_back(1, banks[7], 2, 4)
+        turn_gates(1, (banks[5], banks[7]))
         gather_pairs(0, 2, 5)
         gather_pairs(0, 5, 8)
         gather_pairs(0, 0, 2)

@@ -19,6 +19,7 @@ LAST = E - 1
 STAGED = 6
 DIRECT = 2
 WINDOW = 704
+PICKED = 2
 ZEROED_BY_GPSIMD = 512
 
 F32 = mybir.dt.float32
@@ -179,20 +180,21 @@ def tile_moe_uni_none_kernel(
         sort_scales(1)
         sort_words(1, nc.gpsimd.tensor_copy)
         multiply_step1(0, 0, HALF_E, banks[0], first_copy)
-        multiply_step1(0, HALF_E, LAST, banks[1], nc.vector.tensor_copy)
-        multiply_step1(0, LAST, E, banks[2], nc.vector.tensor_copy)
-        multiply_step1(2, 0, HALF_E, banks[5])
+        multiply_step1(0, HALF_E, 6, banks[1])
+        multiply_step1(0, 6, E, banks[2], nc.vector.tensor_copy)
         multiply_step1(1, 0, HALF_E, banks[3])
-        multiply_step1(2, HALF_E, E, banks[6])
         multiply_step1(1, HALF_E, E, banks[4])
+        multiply_step1(2, 0, HALF_E, banks[5])
+        multiply_step1(2, HALF_E, E, banks[6])
 
         def weigh(step, r, rows, terms, n, t0=0, t1=T):
             picked = rows[n][:].indirect(pos_sb[2 * step + r][:, entries(t0, t1)])
             nc.vector.tensor_tensor(terms[r][n][:, t0:t1], picked, gates[step][:, r, t0:t1], MULT)
 
-        def pick(step, r, rows, terms, n, bank):
-            nc.scalar.activation(terms[r][n][:], rows[n][:].indirect(pos_sb[2 * step + r][:]), COPY)
-            for j in range(BLOCKS):
+        def pick(step, r, rows, terms, n, bank, blocks=BLOCKS):
+            picked = rows[n][:].indirect(pos_sb[2 * step + r][:, entries(0, blocks * P)])
+            nc.scalar.activation(terms[r][n][:, : blocks * P], picked, COPY)
+            for j in range(blocks):
                 nc.tensor.transpose(bank[:, block(j)], terms[r][n][:, block(j)], ident[:])
 
         def turn_gates(step, two_banks):
@@ -233,15 +235,21 @@ def tile_moe_uni_none_kernel(
                 bank[:].rearrange("p (j q u e) -> p u j q e", j=2, u=2, e=2),
             )
 
-        def scale_picked(dst, bank, step, r):
-            for j in range(BLOCKS):
+        def scale_picked(dst, bank, step, r, blocks=BLOCKS):
+            for j in range(blocks):
                 nc.scalar.activation(dst[:, block(j)], bank[:, block(j)], COPY, scale=gate_columns[step][:, r, j : j + 1])
 
         def join_tile3(bank):
-            for j in range(BLOCKS):
+            for j in range(PICKED):
                 nc.vector.scalar_tensor_tensor(
                     c_turned[:, 0, j, 1, :], bank[:, block(j)], gate_columns[0][:, 0, j : j + 1], weighed[:, block(j)], MULT, ADD
                 )
+
+        def sum_rest(bank):
+            add_turned(bank, [(block(j), c_terms[r][2][:, block(j)]) for r in range(2) for j in range(PICKED, BLOCKS)])
+            nc.scalar.copy(
+                c_turned[:, 0, PICKED:, 1, :], bank[:, PICKED * P :].rearrange("p (j q) -> p j q", j=BLOCKS - PICKED)
+            )
 
         def sum_tile2(half, bank):
             add_turned(bank, [(block(jj), c_terms[r][3][:, block(2 * half + jj)]) for r in range(2) for jj in range(2)])
@@ -275,13 +283,16 @@ def tile_moe_uni_none_kernel(
                 in_=grouped[e0 // 2].bitcast(BF16)[:, first : first + (e1 - e0) * PACK * C],
             )
 
-        for n in range(2):
-            weigh(0, 0, y, c_terms, n)
-            weigh(0, 1, y, c_terms, n)
+        weigh(0, 0, y, c_terms, 0)
+        weigh(0, 1, y, c_terms, 0)
+        weigh(0, 0, y, c_terms, 1)
+        weigh(0, 1, y, c_terms, 1)
+        weigh(0, 0, y, c_terms, 2, PICKED * P, T)
+        weigh(0, 1, y, c_terms, 2, PICKED * P, T)
         turn_gates(0, (banks[5], banks[6]))
-        pick(0, 1, y, c_terms, 2, banks[3])
-        pick(0, 0, y, c_terms, 2, banks[4])
-        scale_picked(weighed, banks[3], 0, 1)
+        pick(0, 1, y, c_terms, 2, banks[3], PICKED)
+        pick(0, 0, y, c_terms, 2, banks[4], PICKED)
+        scale_picked(weighed, banks[3], 0, 1, PICKED)
         join_tile3(banks[4])
         multiply_step1(3, 0, HALF_E, banks[7])
         multiply_step1(3, HALF_E, E, banks[0])
@@ -290,12 +301,14 @@ def tile_moe_uni_none_kernel(
         weigh(0, 1, y, c_terms, 3, HALF_T, T)
         sum_pair0(0, banks[1])
         sum_pair0(1, banks[2])
-        turn_back(0, banks[5])
-        sum_tile2(0, banks[2])
-        sum_tile2(1, banks[5])
+        sum_rest(banks[3])
+        turn_back(0, banks[5], 0, 2)
+        turn_back(0, banks[4], 2, 4)
+        sum_tile2(0, banks[3])
+        sum_tile2(1, banks[4])
         turn_back(1, banks[6], 0, 2)
         turn_back(1, banks[7], 2, 4)
-        turn_gates(1, (banks[5], banks[7]))
+        turn_gates(1, (banks[4], banks[7]))
         gather_pairs(0, 2, 5)
         gather_pairs(0, 5, 8)
         gather_pairs(0, 0, 2)

@@ -181,7 +181,8 @@ def tile_moe_uni_none_kernel(
         sort_words(1, nc.gpsimd.tensor_copy)
         multiply_step1(0, 0, HALF_E, banks[0], first_copy)
         multiply_step1(0, HALF_E, 6, banks[1])
-        multiply_step1(0, 6, E, banks[2], nc.vector.tensor_copy)
+        multiply_step1(0, 6, LAST, banks[2], nc.vector.tensor_copy)
+        multiply_step1(0, LAST, E, banks[7], nc.vector.tensor_copy)
         multiply_step1(1, 0, HALF_E, banks[3])
         multiply_step1(1, HALF_E, E, banks[4])
         multiply_step1(2, 0, HALF_E, banks[5])
@@ -191,10 +192,10 @@ def tile_moe_uni_none_kernel(
             picked = rows[n][:].indirect(pos_sb[2 * step + r][:, entries(t0, t1)])
             nc.vector.tensor_tensor(terms[r][n][:, t0:t1], picked, gates[step][:, r, t0:t1], MULT)
 
-        def pick(step, r, rows, terms, n, bank, blocks=BLOCKS):
-            picked = rows[n][:].indirect(pos_sb[2 * step + r][:, entries(0, blocks * P)])
-            nc.scalar.activation(terms[r][n][:, : blocks * P], picked, COPY)
-            for j in range(blocks):
+        def pick(step, r, rows, terms, n, bank, j0=0, j1=BLOCKS):
+            picked = rows[n][:].indirect(pos_sb[2 * step + r][:, entries(j0 * P, j1 * P)])
+            nc.scalar.activation(terms[r][n][:, j0 * P : j1 * P], picked, COPY)
+            for j in range(j0, j1):
                 nc.tensor.transpose(bank[:, block(j)], terms[r][n][:, block(j)], ident[:])
 
         def turn_gates(step, two_banks):
@@ -235,8 +236,8 @@ def tile_moe_uni_none_kernel(
                 bank[:].rearrange("p (j q u e) -> p u j q e", j=2, u=2, e=2),
             )
 
-        def scale_picked(dst, bank, step, r, blocks=BLOCKS):
-            for j in range(blocks):
+        def scale_picked(dst, bank, step, r, j0=0, j1=BLOCKS):
+            for j in range(j0, j1):
                 nc.scalar.activation(dst[:, block(j)], bank[:, block(j)], COPY, scale=gate_columns[step][:, r, j : j + 1])
 
         def join_tile3(bank):
@@ -290,9 +291,9 @@ def tile_moe_uni_none_kernel(
         weigh(0, 0, y, c_terms, 2, PICKED * P, T)
         weigh(0, 1, y, c_terms, 2, PICKED * P, T)
         turn_gates(0, (banks[5], banks[6]))
-        pick(0, 1, y, c_terms, 2, banks[3], PICKED)
-        pick(0, 0, y, c_terms, 2, banks[4], PICKED)
-        scale_picked(weighed, banks[3], 0, 1, PICKED)
+        pick(0, 1, y, c_terms, 2, banks[3], 0, PICKED)
+        pick(0, 0, y, c_terms, 2, banks[4], 0, PICKED)
+        scale_picked(weighed, banks[3], 0, 1, 0, PICKED)
         join_tile3(banks[4])
         multiply_step1(3, 0, HALF_E, banks[7])
         multiply_step1(3, HALF_E, E, banks[0])
@@ -322,11 +323,12 @@ def tile_moe_uni_none_kernel(
         gather_pairs(1, 6, 8)
         interleave(6, 8)
         quantize(4, 6)
-        quantize(6, 8)
+        quantize(6, 7)
+        quantize(7, 8)
 
         z = [held.tile([P, S], F32, name="z%d" % m) for m in range(ROW_TILES)]
 
-        def multiply_step2(m, e0, e1, bank, copy=nc.scalar.copy):
+        def multiply_step2(m, e0, e1, bank):
             for e in range(e0, e1):
                 words, scales = natural(e, m)
                 nc.tensor.matmul_mx(
@@ -338,15 +340,29 @@ def tile_moe_uni_none_kernel(
                     start=True,
                     stop=True,
                 )
+
+        def share(m, e0, e1, bank, copy=nc.scalar.copy):
+            multiply_step2(m, e0, e1, bank)
             copy(z[m][:, slots(e0, e1)], bank[:, slots(0, e1 - e0)])
 
-        multiply_step2(0, 0, HALF_E, banks[0])
-        multiply_step2(0, HALF_E, 6, banks[1])
-        multiply_step2(0, 6, E, banks[2], nc.vector.tensor_copy)
-        for m, early, middle, late in ((1, banks[3][:, :256], 0, 5), (2, banks[3][:, 256:], 1, 6), (3, banks[4], 2, 7)):
-            multiply_step2(m, 0, 2, early)
-            multiply_step2(m, 2, 6, banks[middle])
-            multiply_step2(m, 6, E, banks[late])
+        def two_shares(e0, e1, bank):
+            parts = ((1, bank[:, : 2 * C]), (2, bank[:, 2 * C :]))
+            for m, part in parts:
+                multiply_step2(m, e0, e1, part)
+            for m, part in parts:
+                nc.scalar.copy(z[m][:, slots(e0, e1)], part)
+
+        share(0, 0, HALF_E, banks[0])
+        share(0, HALF_E, 6, banks[1])
+        share(0, 6, LAST, banks[2], nc.vector.tensor_copy)
+        share(0, LAST, E, banks[6], nc.vector.tensor_copy)
+        two_shares(0, 2, banks[3])
+        share(1, 2, 6, banks[0])
+        two_shares(6, E, banks[5])
+        share(2, 2, 6, banks[1])
+        share(3, 0, 2, banks[4])
+        share(3, 2, 6, banks[2])
+        share(3, 6, E, banks[7])
 
         out_terms = [[held.tile([P, T], F32, name="out_terms%d%d" % (r, m)) for m in range(ROW_TILES)] for r in range(2)]
         result = held.tile([P, ROW_TILES, T], F32, name="result")
@@ -356,18 +372,21 @@ def tile_moe_uni_none_kernel(
             nc.vector.tensor_tensor(result[:, m, t0:t1], out_terms[0][m][:, t0:t1], out_terms[1][m][:, t0:t1], ADD)
             nc.sync.dma_start(out[block(m), t0:t1], result[:, m, t0:t1])
 
-        def combine_on_scalar(m, banks_turned, banks_back):
-            for r in range(2):
-                pick(1, r, z, out_terms, m, banks_turned[r])
-            for r in range(2):
-                scale_picked(out_weighed[r], banks_turned[r], 1, r)
-            for half, bank in enumerate(banks_back):
-                add_turned(bank, [(block(jj), out_weighed[r][:, block(2 * half + jj)]) for r in range(2) for jj in range(2)])
-                tokens = slice(half * HALF_T, (half + 1) * HALF_T)
-                nc.scalar.copy(result[:, m, tokens], bank[:, :HALF_T])
-                nc.scalar.dma_start(out[block(m), tokens], result[:, m, tokens])
+        def turn_back_sum(m, half, bank):
+            add_turned(bank, [(block(jj), out_weighed[r][:, block(2 * half + jj)]) for r in range(2) for jj in range(2)])
+            tokens = slice(half * HALF_T, (half + 1) * HALF_T)
+            nc.scalar.copy(result[:, m, tokens], bank[:, :HALF_T])
+            nc.scalar.dma_start(out[block(m), tokens], result[:, m, tokens])
 
-        combine_on_scalar(3, (banks[3], banks[4]), (banks[5], banks[6]))
+        pick(1, 0, z, out_terms, 3, banks[3])
+        pick(1, 1, z, out_terms, 3, banks[4], 0, 2)
+        scale_picked(out_weighed[0], banks[3], 1, 0, 0, 2)
+        pick(1, 1, z, out_terms, 3, banks[6], 2, 4)
+        scale_picked(out_weighed[1], banks[4], 1, 1, 0, 2)
+        scale_picked(out_weighed[0], banks[3], 1, 0, 2, 4)
+        scale_picked(out_weighed[1], banks[6], 1, 1, 2, 4)
+        turn_back_sum(3, 0, banks[5])
+        turn_back_sum(3, 1, banks[0])
         weigh(1, 0, z, out_terms, 0)
         weigh(1, 1, z, out_terms, 0)
         weigh(1, 0, z, out_terms, 1)

@@ -252,10 +252,10 @@ def tile_moe_uni_none_kernel(
                 c_turned[:, 0, PICKED:, 1, :], bank[:, PICKED * P :].rearrange("p (j q) -> p j q", j=BLOCKS - PICKED)
             )
 
-        def sum_tile2(half, bank):
-            add_turned(bank, [(block(jj), c_terms[r][3][:, block(2 * half + jj)]) for r in range(2) for jj in range(2)])
+        def sum_tile2(j0, j1, bank):
+            add_turned(bank, [(block(j), c_terms[r][3][:, block(j)]) for r in range(2) for j in range(j0, j1)])
             nc.scalar.copy(
-                c_turned[:, 1, 2 * half : 2 * half + 2, 1, :], bank[:, :HALF_T].rearrange("p (j q) -> p j q", j=2)
+                c_turned[:, 1, j0:j1, 1, :], bank[:, j0 * P : j1 * P].rearrange("p (j q) -> p j q", j=j1 - j0)
             )
 
         staged = held.tile([P, 2 * STAGED * C], U32, name="staged", align_bytes=64)
@@ -298,18 +298,20 @@ def tile_moe_uni_none_kernel(
         multiply_step1(3, 0, HALF_E, banks[7])
         multiply_step1(3, HALF_E, E, banks[0])
         weigh(0, 0, y, c_terms, 3)
-        weigh(0, 1, y, c_terms, 3, 0, HALF_T)
-        weigh(0, 1, y, c_terms, 3, HALF_T, T)
+        weigh(0, 1, y, c_terms, 3, 0, 2 * P)
+        weigh(0, 1, y, c_terms, 3, 2 * P, 3 * P)
+        weigh(0, 1, y, c_terms, 3, 3 * P, T)
         sum_pair0(0, banks[1])
         sum_pair0(1, banks[2])
         sum_rest(banks[3])
         turn_back(0, banks[5], 0, 2)
         turn_back(0, banks[4], 2, 4)
-        sum_tile2(0, banks[3])
-        sum_tile2(1, banks[4])
-        turn_back(1, banks[6], 0, 2)
-        turn_back(1, banks[7], 2, 4)
-        turn_gates(1, (banks[4], banks[7]))
+        sum_tile2(0, 2, banks[3])
+        sum_tile2(2, 3, banks[5])
+        sum_tile2(3, 4, banks[4])
+        turn_back(1, banks[6], 0, 3)
+        turn_back(1, banks[7], 3, 4)
+        turn_gates(1, (banks[6], banks[7]))
         gather_pairs(0, 2, 5)
         gather_pairs(0, 5, 8)
         gather_pairs(0, 0, 2)
@@ -372,6 +374,16 @@ def tile_moe_uni_none_kernel(
             nc.vector.tensor_tensor(result[:, m, t0:t1], out_terms[0][m][:, t0:t1], out_terms[1][m][:, t0:t1], ADD)
             nc.sync.dma_start(out[block(m), t0:t1], result[:, m, t0:t1])
 
+        def finish_on_tensor(m, j0, j1, bank_sum, bank_back):
+            tokens = slice(j0 * P, j1 * P)
+            add_turned(bank_sum, [(block(j), out_terms[r][m][:, block(j)]) for r in range(2) for j in range(j0, j1)])
+            turned_sum = held.tile([P, T], F32, name="turned_sum")
+            nc.scalar.copy(turned_sum[:, tokens], bank_sum[:, tokens])
+            for j in range(j0, j1):
+                nc.tensor.transpose(bank_back[:, block(j)], turned_sum[:, block(j)], ident[:])
+            nc.scalar.copy(result[:, m, tokens], bank_back[:, tokens])
+            nc.scalar.dma_start(out[block(m), tokens], result[:, m, tokens])
+
         def turn_back_sum(m, half, bank):
             add_turned(bank, [(block(jj), out_weighed[r][:, block(2 * half + jj)]) for r in range(2) for jj in range(2)])
             tokens = slice(half * HALF_T, (half + 1) * HALF_T)
@@ -390,12 +402,12 @@ def tile_moe_uni_none_kernel(
         weigh(1, 0, z, out_terms, 0)
         weigh(1, 1, z, out_terms, 0)
         weigh(1, 0, z, out_terms, 1)
-        finish_on_vector(0, 0, T)
+        finish_on_vector(0, 0, HALF_T)
+        finish_on_tensor(0, 2, 4, banks[1], banks[2])
         weigh(1, 1, z, out_terms, 1)
-        weigh(1, 0, z, out_terms, 2, 0, HALF_T)
+        weigh(1, 0, z, out_terms, 2)
         finish_on_vector(1, 0, T)
-        weigh(1, 1, z, out_terms, 2, 0, HALF_T)
-        weigh(1, 0, z, out_terms, 2, HALF_T, T)
-        finish_on_vector(2, 0, HALF_T)
-        weigh(1, 1, z, out_terms, 2, HALF_T, T)
-        finish_on_vector(2, HALF_T, T)
+        weigh(1, 1, z, out_terms, 2, 0, 3 * P)
+        weigh(1, 1, z, out_terms, 2, 3 * P, T)
+        finish_on_vector(2, 0, 3 * P)
+        finish_on_vector(2, 3 * P, T)

@@ -7,17 +7,17 @@ K, T, E, C = 512, 512, 8, 128
 S = E * C
 P = 128
 PACK = 4
-ROW_TILES = K // P
-BANK = 512
+TILES = K // P
 PER_COLUMN = 16
 SCALE_ROWS = K // 32
 HALF_E, HALF_T = E // 2, T // 2
-BLOCKS = T // P
-PAIRS = K // 2
+RUNS = T // P
 FLOPS = 2 * 2 * K * K * S
+
+SINGLY = 6
 LAST = E - 1
-STAGED = 6
 DIRECT = 2
+STAGED = E - DIRECT
 WINDOW = 704
 PICKED = 2
 ZEROED_BY_GPSIMD = 512
@@ -43,8 +43,12 @@ def slots(e0, e1):
     return slice(e0 * C, e1 * C)
 
 
-def block(j):
-    return slice(j * P, (j + 1) * P)
+def runs(j0, j1):
+    return slice(j0 * P, j1 * P)
+
+
+def run(j):
+    return runs(j, j + 1)
 
 
 def tile_moe_uni_none_kernel(
@@ -62,15 +66,13 @@ def tile_moe_uni_none_kernel(
 
         x_words_sb = held.tile([P, WINDOW], I32, name="x_words_sb", align_bytes=64)
         x_scales_sb = held.tile([P, WINDOW // 4], I32, name="x_scales_sb", tag="scales_then_words", align_bytes=64)
-        groups = ((0, HALF_E), (HALF_E, E))
-        w_words_sb = [
-            held.tile([P, (e1 - e0) * PAIRS], I32, name="w_words_sb%d" % e0, align_bytes=64) for e0, e1 in groups
-        ]
+        lower_words = held.tile([P, E * P], I32, name="lower_words", align_bytes=64)
+        upper_words = [held.tile([P, HALF_E * P], I32, name="upper_words%d" % g, align_bytes=64) for g in range(2)]
         w_scales_sb = held.tile([P, E * K // 4], I32, name="w_scales_sb", align_bytes=64)
         gates = [held.tile([P, 2, T], F32, name="gate%d_sb" % (step + 1)) for step in range(2)]
-        gate_columns = [held.tile([P, 2, BLOCKS], F32, name="gate_columns%d" % step) for step in range(2)]
+        gate_columns = [held.tile([P, 2, n], F32, name="gate_columns%d" % n) for n in (PICKED, RUNS)]
         ident = held.tile([P, P], F32, name="ident")
-        banks = [psum.tile([P, BANK], F32, name="bank%d" % b) for b in range(8)]
+        banks = [psum.tile([P, RUNS * P], F32, name="bank%d" % b) for b in range(8)]
 
         nc.gpsimd.memset(x_scales_sb[:], 0)
         nc.gpsimd.memset(x_words_sb[:, T:], 0)
@@ -80,15 +82,11 @@ def tile_moe_uni_none_kernel(
         make_identity(nc, ident_bf16[:])
         nc.scalar.activation(ident[:], ident_bf16[:], COPY)
 
-        def load_words(g):
-            e0, e1 = groups[g]
+        def load_words(dst, e0, e1, h):
             nc.sync.dma_start(
-                w_words_sb[g][:].rearrange("p (e n) -> p e n", e=e1 - e0),
-                w_words[e0:e1, 0, :, :].rearrange("e p n -> p e n").bitcast(I32),
+                dst[:].rearrange("p (e n) -> p e n", e=e1 - e0),
+                w_words[e0:e1, 0, :, h * K : (h + 1) * K].rearrange("e p n -> p e n").bitcast(I32),
             )
-
-        def load_gates(step, gate):
-            nc.sync.dma_start(gates[step][:], gate.rearrange("r p t -> p r t"))
 
         nc.sync.dma_start(x_words_sb[:, :T], x_words[0].rearrange("p t d -> p (t d)").bitcast(I32))
         nc.sync.dma_start(offs_sb[:], offs)
@@ -99,315 +97,270 @@ def tile_moe_uni_none_kernel(
                 w_scales_sb[r:P:32, :].rearrange("q (e n) -> q e n", e=E),
                 w_scales[:, 0, r:SCALE_ROWS:4, :].rearrange("e q n -> q e n").bitcast(I32),
             )
-        load_words(0)
-        load_words(1)
+        load_words(lower_words, 0, E, 0)
+        load_words(upper_words[0], 0, HALF_E, 1)
+        load_words(upper_words[1], HALF_E, E, 1)
         nc.sync.dma_start(pos_sb[0][:], pos1)
         nc.sync.dma_start(pos_sb[1][:], pos2)
-        load_gates(0, gate1)
+        nc.sync.dma_start(gates[0][:], gate1.rearrange("r p t -> p r t"))
         nc.sync.dma_start(offs2_sb[:], offs2)
         nc.sync.dma_start(pos_sb[2][:], pos3)
         nc.sync.dma_start(pos_sb[3][:], pos4)
-        load_gates(1, gate2)
+        nc.sync.dma_start(gates[1][:], gate2.rearrange("r p t -> p r t"))
 
-        def group_of(e, among):
-            return [g for g, (e0, e1) in enumerate(among) if e0 <= e < e1][0]
-
-        word_pieces = ((0, 4), (4, 8))
-        scale_pieces = ((0, 4), (4, 8))
         early_words = held.tile([P, HALF_E * C], U32, name="early_words", align_bytes=64)
-        slot_scales = [held.tile([P, (b - a) * C], U8, name="slot_scales%d" % a, align_bytes=64) for a, b in scale_pieces]
+        slot_scales = [held.tile([P, HALF_E * C], U8, name="slot_scales%d" % g, align_bytes=64) for g in range(2)]
 
-        def gather_words(dst, a, b):
-            nc.vector.tensor_copy(dst, x_words_sb[:].bitcast(U32).indirect(offs_sb[:, entries(a * C, b * C)]))
-
-        def gather_scales(n):
-            a, b = scale_pieces[n]
-            nc.vector.tensor_copy(slot_scales[n][:], x_scales_sb[:].bitcast(U8).indirect(offs_sb[:, entries(a * C, b * C)]))
+        def gather_words(dst, e0, e1):
+            window = x_words_sb[:].bitcast(U32)
+            nc.vector.tensor_copy(dst, window.indirect(offs_sb[:, entries(e0 * C, e1 * C)]))
 
         gather_words(early_words[:], 0, HALF_E)
-        gather_scales(0)
-        gather_scales(1)
+        for g in range(2):
+            listed = offs_sb[:, entries(g * HALF_E * C, (g + 1) * HALF_E * C)]
+            nc.vector.tensor_copy(slot_scales[g][:], x_scales_sb[:].bitcast(U8).indirect(listed))
         late_words = held.tile([P, HALF_E * C], U32, name="late_words", tag="scales_then_words", align_bytes=64)
-        for a, b in ((4, 6), (6, 7), (7, 8)):
-            gather_words(late_words[:, slots(a - HALF_E, b - HALF_E)], a, b)
+        for e0, e1 in ((HALF_E, SINGLY), (SINGLY, LAST), (LAST, E)):
+            gather_words(late_words[:, slots(e0 - HALF_E, e1 - HALF_E)], e0, e1)
         slot_words = [early_words, late_words]
 
         pair_words = [held.tile([P, 2, HALF_E, P // 2], U32, name="pair_words%d" % g, align_bytes=64) for g in range(2)]
         pair_scales = [held.tile([P, 2, HALF_E, P // 2], U16, name="pair_scales%d" % g, align_bytes=64) for g in range(2)]
         w_scale_bytes = w_scales_sb[:].bitcast(U8)
 
-        def sort_words(g, copy=nc.scalar.copy):
-            pairs = w_words_sb[g][:].bitcast(U32).rearrange("p (e h q u) -> p h u e q", e=HALF_E, h=2, u=2)
-            copy(pair_words[g][:], pairs[:, 1])
+        def sort_words(g):
+            pairs = upper_words[g][:].bitcast(U32).rearrange("p (i q u) -> p u i q", i=HALF_E, u=2)
+            nc.gpsimd.tensor_copy(pair_words[g][:], pairs)
 
-        def sort_scales(g, copy=nc.scalar.copy):
-            pairs = w_scales_sb[:].bitcast(U16).rearrange("p (g e h q u) -> p g h u e q", g=2, e=HALF_E, h=2, u=2)
-            copy(pair_scales[g][:], pairs[:, g, 1])
+        def sort_scales(g):
+            pairs = w_scales_sb[:].bitcast(U16).rearrange("p (g i h q u) -> p g h u i q", g=2, i=HALF_E, h=2, u=2)
+            nc.scalar.copy(pair_scales[g][:], pairs[:, g, 1])
 
-        def natural(e, m):
-            g = group_of(e, groups)
-            column = (e - groups[g][0]) * K + m * P
-            words = w_words_sb[g][:].bitcast(U8)[:, 2 * column : 2 * (column + P)]
+        def columns_in_order(e, m):
+            tile, i = (lower_words, e) if m < 2 else (upper_words[e // HALF_E], e % HALF_E)
+            column = (2 * i + m % 2) * P
+            words = tile[:].bitcast(U8)[:, 2 * column : 2 * (column + P)]
             return words.bitcast(FP4X4), w_scale_bytes[:, e * K + m * P : e * K + (m + 1) * P]
 
-        def sorted_pairs(e, u):
+        def columns_sorted(e, u):
             g, i = divmod(e, HALF_E)
             return pair_words[g][:, u, i, :].bitcast(U8).bitcast(FP4X4), pair_scales[g][:, u, i, :].bitcast(U8)
 
-        y = [held.tile([P, S], F32, name="y%d" % n) for n in range(ROW_TILES)]
+        y = [held.tile([P, S], F32, name="y%d" % n) for n in range(TILES)]
 
-        def multiply_step1(n, e0, e1, bank, copy=nc.scalar.copy):
+        def make_y(n, e0, e1, bank, copy=nc.scalar.copy):
             for e in range(e0, e1):
-                words, scales = natural(e, n) if n < 2 else sorted_pairs(e, n - 2)
-                tw, ts = group_of(e, word_pieces), group_of(e, scale_pieces)
-                ew, es = e - word_pieces[tw][0], e - scale_pieces[ts][0]
+                words, scales = columns_in_order(e, n) if n < 2 else columns_sorted(e, n - 2)
+                g, i = divmod(e, HALF_E)
                 nc.tensor.matmul_mx(
                     bank[:, slots(e - e0, e - e0 + 1)],
                     lhsT=words,
                     lhsT_scale=scales,
-                    rhs=slot_words[tw][:, slots(ew, ew + 1)].bitcast(FP8X4),
-                    rhs_scale=slot_scales[ts][:, slots(es, es + 1)],
+                    rhs=slot_words[g][:, slots(i, i + 1)].bitcast(FP8X4),
+                    rhs_scale=slot_scales[g][:, slots(i, i + 1)],
                     start=True,
                     stop=True,
                 )
             copy(y[n][:, slots(e0, e1)], bank[:, slots(0, e1 - e0)])
 
-        def first_copy(dst, src):
-            nc.scalar.activation(dst, src, COPY)
-
         sort_words(0)
         sort_scales(0)
         sort_scales(1)
-        sort_words(1, nc.gpsimd.tensor_copy)
-        multiply_step1(0, 0, HALF_E, banks[0], first_copy)
-        multiply_step1(0, HALF_E, 6, banks[1])
-        multiply_step1(0, 6, LAST, banks[2], nc.vector.tensor_copy)
-        multiply_step1(0, LAST, E, banks[7], nc.vector.tensor_copy)
-        multiply_step1(1, 0, HALF_E, banks[3])
-        multiply_step1(1, HALF_E, E, banks[4])
-        multiply_step1(2, 0, HALF_E, banks[5])
-        multiply_step1(2, HALF_E, E, banks[6])
+        sort_words(1)
+        make_y(0, 0, HALF_E, banks[0])
+        make_y(1, 0, HALF_E, banks[3])
+        make_y(0, HALF_E, SINGLY, banks[1])
+        make_y(0, SINGLY, LAST, banks[2], nc.vector.tensor_copy)
+        make_y(0, LAST, E, banks[7], nc.vector.tensor_copy)
+        make_y(1, HALF_E, E, banks[4])
+        make_y(2, 0, HALF_E, banks[5])
+        make_y(2, HALF_E, E, banks[6])
 
-        def weigh(step, r, rows, terms, n, t0=0, t1=T):
-            picked = rows[n][:].indirect(pos_sb[2 * step + r][:, entries(t0, t1)])
-            nc.vector.tensor_tensor(terms[r][n][:, t0:t1], picked, gates[step][:, r, t0:t1], MULT)
+        def weigh(step, r, rows, terms, n, j0=0, j1=RUNS):
+            gathered = rows[n][:].indirect(pos_sb[2 * step + r][:, entries(j0 * P, j1 * P)])
+            nc.vector.tensor_tensor(terms[r][n][:, runs(j0, j1)], gathered, gates[step][:, r, runs(j0, j1)], MULT)
 
-        def pick(step, r, rows, terms, n, bank, j0=0, j1=BLOCKS):
-            picked = rows[n][:].indirect(pos_sb[2 * step + r][:, entries(j0 * P, j1 * P)])
-            nc.scalar.activation(terms[r][n][:, j0 * P : j1 * P], picked, COPY)
+        def pick(step, r, rows, terms, n, bank, j0, j1):
+            gathered = rows[n][:].indirect(pos_sb[2 * step + r][:, entries(j0 * P, j1 * P)])
+            nc.scalar.activation(terms[r][n][:, runs(j0, j1)], gathered, COPY)
             for j in range(j0, j1):
-                nc.tensor.transpose(bank[:, block(j)], terms[r][n][:, block(j)], ident[:])
+                nc.tensor.transpose(bank[:, run(j)], terms[r][n][:, run(j)], ident[:])
 
-        def turn_gates(step, two_banks):
+        def turn_gates(step, two_banks, count):
             for r, bank in enumerate(two_banks):
-                for j in range(BLOCKS):
-                    nc.tensor.transpose(bank[:, block(j)], gates[step][:, r, block(j)], ident[:])
-                nc.scalar.copy(gate_columns[step][:, r, :], bank[:, 0:BANK:P])
+                for j in range(count):
+                    nc.tensor.transpose(bank[:, run(j)], gates[step][:, r, run(j)], ident[:])
+                nc.scalar.copy(gate_columns[step][:, r, :], bank[:, 0 : count * P : P])
+
+        def weigh_turned(dst, bank, step, r, j0, j1):
+            for j in range(j0, j1):
+                nc.scalar.activation(dst[:, run(j)], bank[:, run(j)], COPY, scale=gate_columns[step][:, r, j : j + 1])
 
         def add_turned(bank, parts):
             for i, (columns, source) in enumerate(parts):
+                first, final = i == 0, i == len(parts) - 1
                 nc.tensor.matmul(
-                    bank[:, columns], lhsT=source, rhs=ident[:], start=(i == 0), stop=(i == len(parts) - 1), is_transpose=True
+                    bank[:, columns], lhsT=source, rhs=ident[:], start=first, stop=final, is_transpose=True
                 )
 
-        c_terms = [[held.tile([P, T], F32, name="c_terms%d%d" % (r, n)) for n in range(ROW_TILES)] for r in range(2)]
-        c_turned = held.tile([P, 2, BLOCKS, 2, P], BF16, name="c_turned")
+        c_terms = [[held.tile([P, T], F32, name="c_terms%d%d" % (r, n)) for n in range(TILES)] for r in range(2)]
+        c_turned = held.tile([P, 2, RUNS, 2, P], BF16, name="c_turned")
         c_pair = [held.tile([P, T], F32, name="c_pair%d" % u) for u in range(2)]
-        weighed = held.tile([P, T], F32, name="weighed")
+        second_term = held.tile([P, T], F32, name="second_term")
 
-        def turn_back(u, bank, j0=0, j1=BLOCKS):
-            words = c_turned[:, u].rearrange("p j h q -> p (j h q)").bitcast(F32)
+        def sum_lower(j0, bank):
+            parts = [
+                (run(2 * j + n), c_terms[r][n][:, run(j0 + j)]) for n in range(2) for r in range(2) for j in range(2)
+            ]
+            add_turned(bank, parts)
+            nc.scalar.copy(
+                c_turned[:, :, j0 : j0 + 2, 0, :].rearrange("a u j (q i) -> a u j q i", i=2),
+                bank[:].rearrange("a (j q u i) -> a u j q i", j=2, u=2, i=2),
+            )
+
+        def sum_upper(u, j0, j1, bank):
+            add_turned(bank, [(run(j), c_terms[r][2 + u][:, run(j)]) for r in range(2) for j in range(j0, j1)])
+            nc.scalar.copy(c_turned[:, u, j0:j1, 1, :], bank[:, runs(j0, j1)].rearrange("a (j q) -> a j q", j=j1 - j0))
+
+        def turn_back(u, j0, j1, bank):
+            pair_view = c_turned[:, u].rearrange("a j h q -> a (j h q)").bitcast(F32)
             for j in range(j0, j1):
-                nc.tensor.transpose(bank[:, block(j)], words[:, block(j)], ident[:])
-            nc.scalar.copy(c_pair[u][:, j0 * P : j1 * P], bank[:, j0 * P : j1 * P])
-
-        def sum_pair0(half, bank):
-            add_turned(
-                bank,
-                [
-                    (block(2 * jj + h), c_terms[r][h][:, block(2 * half + jj)])
-                    for h in range(2)
-                    for r in range(2)
-                    for jj in range(2)
-                ],
-            )
-            nc.scalar.copy(
-                c_turned[:, :, 2 * half : 2 * half + 2, 0, :].rearrange("p u j (q e) -> p u j q e", e=2),
-                bank[:].rearrange("p (j q u e) -> p u j q e", j=2, u=2, e=2),
-            )
-
-        def scale_picked(dst, bank, step, r, j0=0, j1=BLOCKS):
-            for j in range(j0, j1):
-                nc.scalar.activation(dst[:, block(j)], bank[:, block(j)], COPY, scale=gate_columns[step][:, r, j : j + 1])
-
-        def join_tile3(bank):
-            for j in range(PICKED):
-                nc.vector.scalar_tensor_tensor(
-                    c_turned[:, 0, j, 1, :], bank[:, block(j)], gate_columns[0][:, 0, j : j + 1], weighed[:, block(j)], MULT, ADD
-                )
-
-        def sum_rest(bank):
-            add_turned(bank, [(block(j), c_terms[r][2][:, block(j)]) for r in range(2) for j in range(PICKED, BLOCKS)])
-            nc.scalar.copy(
-                c_turned[:, 0, PICKED:, 1, :], bank[:, PICKED * P :].rearrange("p (j q) -> p j q", j=BLOCKS - PICKED)
-            )
-
-        def sum_tile2(j0, j1, bank):
-            add_turned(bank, [(block(j), c_terms[r][3][:, block(j)]) for r in range(2) for j in range(j0, j1)])
-            nc.scalar.copy(
-                c_turned[:, 1, j0:j1, 1, :], bank[:, j0 * P : j1 * P].rearrange("p (j q) -> p j q", j=j1 - j0)
-            )
+                nc.tensor.transpose(bank[:, run(j)], pair_view[:, run(j)], ident[:])
+            nc.scalar.copy(c_pair[u][:, runs(j0, j1)], bank[:, runs(j0, j1)])
 
         staged = held.tile([P, 2 * STAGED * C], U32, name="staged", align_bytes=64)
-        grouped = [held.tile([P, 2 * C * 2], U32, name="grouped%d" % e, align_bytes=64)[:] for e in (0, 2, 4, 6)]
+        grouped = [held.tile([P, 2 * 2 * C], U32, name="grouped%d" % e, align_bytes=64) for e in range(0, E, 2)]
         c_words = held.tile([P, S], U32, name="c_words", align_bytes=64)
         c_scales = held.tile([P, S], U8, name="c_scales", align_bytes=64)
 
-        def gather_pairs(u, e0, e1):
-            picked = c_pair[u][:].bitcast(U32).indirect(offs2_sb[:, entries(e0 * C, e1 * C)])
-            if e0 >= DIRECT:
-                nc.vector.tensor_copy(staged[:, slots(u * STAGED + e0 - DIRECT, u * STAGED + e1 - DIRECT)], picked)
-            else:
-                nc.vector.tensor_copy(grouped[e0 // 2][:, u::2], picked)
+        for n in range(2):
+            weigh(0, 0, y, c_terms, n)
+            weigh(0, 1, y, c_terms, n)
+        weigh(0, 0, y, c_terms, 2, PICKED, RUNS)
+        weigh(0, 1, y, c_terms, 2, PICKED, RUNS)
+        turn_gates(0, (banks[5], banks[6]), PICKED)
+        pick(0, 1, y, c_terms, 2, banks[3], 0, PICKED)
+        pick(0, 0, y, c_terms, 2, banks[4], 0, PICKED)
+        weigh_turned(second_term, banks[3], 0, 1, 0, PICKED)
+        for j in range(PICKED):
+            nc.vector.scalar_tensor_tensor(
+                c_turned[:, 0, j, 1, :],
+                banks[4][:, run(j)],
+                gate_columns[0][:, 0, j : j + 1],
+                second_term[:, run(j)],
+                MULT,
+                ADD,
+            )
+        make_y(3, 0, HALF_E, banks[7])
+        make_y(3, HALF_E, E, banks[0])
+        pieces = ((0, 2), (2, 3), (3, RUNS))
+        weigh(0, 0, y, c_terms, 3)
+        for j0, j1 in pieces:
+            weigh(0, 1, y, c_terms, 3, j0, j1)
+        sum_lower(0, banks[1])
+        sum_lower(2, banks[2])
+        sum_upper(0, PICKED, RUNS, banks[3])
+        turn_back(0, 0, 2, banks[5])
+        turn_back(0, 2, RUNS, banks[4])
+        for (j0, j1), b in zip(pieces, (3, 5, 4)):
+            sum_upper(1, j0, j1, banks[b])
+        turn_back(1, 0, 3, banks[6])
+        turn_back(1, 3, RUNS, banks[7])
+        turn_gates(1, (banks[6], banks[7]), RUNS)
 
-        def interleave(e0, e1):
+        def gather_pairs(u, e0, e1):
+            gathered = c_pair[u][:].bitcast(U32).indirect(offs2_sb[:, entries(e0 * C, e1 * C)])
+            if e0 >= DIRECT:
+                nc.vector.tensor_copy(staged[:, slots(u * STAGED + e0 - DIRECT, u * STAGED + e1 - DIRECT)], gathered)
+            else:
+                nc.vector.tensor_copy(grouped[0][:, u::2], gathered)
+
+        def interleave(e0):
             nc.scalar.copy(
-                grouped[e0 // 2].rearrange("p (s u) -> p s u", u=2)[:, slots(e0 % 2, e0 % 2 + e1 - e0), :],
-                staged[:].rearrange("p (u s) -> p s u", u=2)[:, slots(e0 - DIRECT, e1 - DIRECT), :],
+                grouped[e0 // 2][:].rearrange("p (s u) -> p s u", u=2),
+                staged[:].rearrange("p (u s) -> p s u", u=2)[:, slots(e0 - DIRECT, e0 - DIRECT + 2), :],
             )
 
         def quantize(e0, e1):
-            first = e0 % 2 * PACK * C
+            first = e0 % 2
             nc.vector.quantize_mx(
                 out=c_words[:, slots(e0, e1)].bitcast(FP8X4),
                 scales=c_scales[:, slots(e0, e1)],
-                in_=grouped[e0 // 2].bitcast(BF16)[:, first : first + (e1 - e0) * PACK * C],
+                in_=grouped[e0 // 2][:].bitcast(BF16)[:, slots(PACK * first, PACK * (first + e1 - e0))],
             )
 
-        weigh(0, 0, y, c_terms, 0)
-        weigh(0, 1, y, c_terms, 0)
-        weigh(0, 0, y, c_terms, 1)
-        weigh(0, 1, y, c_terms, 1)
-        weigh(0, 0, y, c_terms, 2, PICKED * P, T)
-        weigh(0, 1, y, c_terms, 2, PICKED * P, T)
-        turn_gates(0, (banks[5], banks[6]))
-        pick(0, 1, y, c_terms, 2, banks[3], 0, PICKED)
-        pick(0, 0, y, c_terms, 2, banks[4], 0, PICKED)
-        scale_picked(weighed, banks[3], 0, 1, 0, PICKED)
-        join_tile3(banks[4])
-        multiply_step1(3, 0, HALF_E, banks[7])
-        multiply_step1(3, HALF_E, E, banks[0])
-        weigh(0, 0, y, c_terms, 3)
-        weigh(0, 1, y, c_terms, 3, 0, 2 * P)
-        weigh(0, 1, y, c_terms, 3, 2 * P, 3 * P)
-        weigh(0, 1, y, c_terms, 3, 3 * P, T)
-        sum_pair0(0, banks[1])
-        sum_pair0(1, banks[2])
-        sum_rest(banks[3])
-        turn_back(0, banks[5], 0, 2)
-        turn_back(0, banks[4], 2, 4)
-        sum_tile2(0, 2, banks[3])
-        sum_tile2(2, 3, banks[5])
-        sum_tile2(3, 4, banks[4])
-        turn_back(1, banks[6], 0, 3)
-        turn_back(1, banks[7], 3, 4)
-        turn_gates(1, (banks[6], banks[7]))
-        gather_pairs(0, 2, 5)
-        gather_pairs(0, 5, 8)
-        gather_pairs(0, 0, 2)
-        gather_pairs(1, 0, 2)
-        gather_pairs(1, 2, 4)
-        interleave(2, 4)
-        quantize(0, 2)
-        gather_pairs(1, 4, 6)
-        interleave(4, 6)
-        quantize(2, 4)
-        gather_pairs(1, 6, 8)
-        interleave(6, 8)
-        quantize(4, 6)
-        quantize(6, 7)
-        quantize(7, 8)
+        gather_pairs(0, DIRECT, DIRECT + STAGED // 2)
+        gather_pairs(0, DIRECT + STAGED // 2, E)
+        gather_pairs(0, 0, DIRECT)
+        gather_pairs(1, 0, DIRECT)
+        for e in range(DIRECT, E, 2):
+            gather_pairs(1, e, e + 2)
+            interleave(e)
+            quantize(e - 2, e)
+        for e in range(SINGLY, E):
+            quantize(e, e + 1)
 
-        z = [held.tile([P, S], F32, name="z%d" % m) for m in range(ROW_TILES)]
+        z = [held.tile([P, S], F32, name="z%d" % m) for m in range(TILES)]
 
-        def multiply_step2(m, e0, e1, bank):
-            for e in range(e0, e1):
-                words, scales = natural(e, m)
-                nc.tensor.matmul_mx(
-                    bank[:, slots(e - e0, e - e0 + 1)],
-                    lhsT=words,
-                    lhsT_scale=scales,
-                    rhs=c_words[:, slots(e, e + 1)].bitcast(FP8X4),
-                    rhs_scale=c_scales[:, slots(e, e + 1)],
-                    start=True,
-                    stop=True,
-                )
+        def make_z(tiles, e0, e1, bank, copy=nc.scalar.copy):
+            width = e1 - e0
+            for i, m in enumerate(tiles):
+                for e in range(e0, e1):
+                    words, scales = columns_in_order(e, m)
+                    nc.tensor.matmul_mx(
+                        bank[:, slots(i * width + e - e0, i * width + e - e0 + 1)],
+                        lhsT=words,
+                        lhsT_scale=scales,
+                        rhs=c_words[:, slots(e, e + 1)].bitcast(FP8X4),
+                        rhs_scale=c_scales[:, slots(e, e + 1)],
+                        start=True,
+                        stop=True,
+                    )
+            for i, m in enumerate(tiles):
+                copy(z[m][:, slots(e0, e1)], bank[:, slots(i * width, (i + 1) * width)])
 
-        def share(m, e0, e1, bank, copy=nc.scalar.copy):
-            multiply_step2(m, e0, e1, bank)
-            copy(z[m][:, slots(e0, e1)], bank[:, slots(0, e1 - e0)])
+        make_z([0], 0, HALF_E, banks[0])
+        make_z([0], HALF_E, SINGLY, banks[1])
+        make_z([0], SINGLY, LAST, banks[2], nc.vector.tensor_copy)
+        make_z([0], LAST, E, banks[6], nc.vector.tensor_copy)
+        make_z([1, 2], 0, DIRECT, banks[3])
+        make_z([1], DIRECT, SINGLY, banks[0])
+        make_z([1, 2], SINGLY, E, banks[5])
+        make_z([2], DIRECT, SINGLY, banks[1])
+        make_z([3], 0, DIRECT, banks[4])
+        make_z([3], DIRECT, SINGLY, banks[2])
+        make_z([3], SINGLY, E, banks[7])
 
-        def two_shares(e0, e1, bank):
-            parts = ((1, bank[:, : 2 * C]), (2, bank[:, 2 * C :]))
-            for m, part in parts:
-                multiply_step2(m, e0, e1, part)
-            for m, part in parts:
-                nc.scalar.copy(z[m][:, slots(e0, e1)], part)
+        out_terms = [[held.tile([P, T], F32, name="out_terms%d%d" % (r, m)) for m in range(TILES)] for r in range(2)]
+        result = held.tile([P, TILES, T], F32, name="result")
+        turned_terms = [held.tile([P, T], F32, name="turned_terms%d" % r) for r in range(2)]
 
-        share(0, 0, HALF_E, banks[0])
-        share(0, HALF_E, 6, banks[1])
-        share(0, 6, LAST, banks[2], nc.vector.tensor_copy)
-        share(0, LAST, E, banks[6], nc.vector.tensor_copy)
-        two_shares(0, 2, banks[3])
-        share(1, 2, 6, banks[0])
-        two_shares(6, E, banks[5])
-        share(2, 2, 6, banks[1])
-        share(3, 0, 2, banks[4])
-        share(3, 2, 6, banks[2])
-        share(3, 6, E, banks[7])
+        def add_and_store(m, j0, j1):
+            tokens = runs(j0, j1)
+            nc.vector.tensor_tensor(result[:, m, tokens], out_terms[0][m][:, tokens], out_terms[1][m][:, tokens], ADD)
+            nc.sync.dma_start(out[run(m), tokens], result[:, m, tokens])
 
-        out_terms = [[held.tile([P, T], F32, name="out_terms%d%d" % (r, m)) for m in range(ROW_TILES)] for r in range(2)]
-        result = held.tile([P, ROW_TILES, T], F32, name="result")
-        out_weighed = [held.tile([P, T], F32, name="out_weighed%d" % r) for r in range(2)]
-
-        def finish_on_vector(m, t0, t1):
-            nc.vector.tensor_tensor(result[:, m, t0:t1], out_terms[0][m][:, t0:t1], out_terms[1][m][:, t0:t1], ADD)
-            nc.sync.dma_start(out[block(m), t0:t1], result[:, m, t0:t1])
-
-        def finish_on_tensor(m, j0, j1, bank_sum, bank_back):
-            tokens = slice(j0 * P, j1 * P)
-            add_turned(bank_sum, [(block(j), out_terms[r][m][:, block(j)]) for r in range(2) for j in range(j0, j1)])
-            turned_sum = held.tile([P, T], F32, name="turned_sum")
-            nc.scalar.copy(turned_sum[:, tokens], bank_sum[:, tokens])
-            for j in range(j0, j1):
-                nc.tensor.transpose(bank_back[:, block(j)], turned_sum[:, block(j)], ident[:])
-            nc.scalar.copy(result[:, m, tokens], bank_back[:, tokens])
-            nc.scalar.dma_start(out[block(m), tokens], result[:, m, tokens])
-
-        def turn_back_sum(m, half, bank):
-            add_turned(bank, [(block(jj), out_weighed[r][:, block(2 * half + jj)]) for r in range(2) for jj in range(2)])
-            tokens = slice(half * HALF_T, (half + 1) * HALF_T)
-            nc.scalar.copy(result[:, m, tokens], bank[:, :HALF_T])
-            nc.scalar.dma_start(out[block(m), tokens], result[:, m, tokens])
-
-        pick(1, 0, z, out_terms, 3, banks[3])
+        pick(1, 0, z, out_terms, 3, banks[3], 0, RUNS)
         pick(1, 1, z, out_terms, 3, banks[4], 0, 2)
-        scale_picked(out_weighed[0], banks[3], 1, 0, 0, 2)
-        pick(1, 1, z, out_terms, 3, banks[6], 2, 4)
-        scale_picked(out_weighed[1], banks[4], 1, 1, 0, 2)
-        scale_picked(out_weighed[0], banks[3], 1, 0, 2, 4)
-        scale_picked(out_weighed[1], banks[6], 1, 1, 2, 4)
-        turn_back_sum(3, 0, banks[5])
-        turn_back_sum(3, 1, banks[0])
+        weigh_turned(turned_terms[0], banks[3], 1, 0, 0, 2)
+        pick(1, 1, z, out_terms, 3, banks[6], 2, RUNS)
+        weigh_turned(turned_terms[1], banks[4], 1, 1, 0, 2)
+        weigh_turned(turned_terms[0], banks[3], 1, 0, 2, RUNS)
+        weigh_turned(turned_terms[1], banks[6], 1, 1, 2, RUNS)
+        for j0, bank in ((0, banks[5]), (2, banks[0])):
+            add_turned(bank, [(run(j), turned_terms[r][:, run(j0 + j)]) for r in range(2) for j in range(2)])
+            nc.scalar.copy(result[:, 3, runs(j0, j0 + 2)], bank[:, :HALF_T])
+            nc.scalar.dma_start(out[run(3), runs(j0, j0 + 2)], result[:, 3, runs(j0, j0 + 2)])
+
         weigh(1, 0, z, out_terms, 0)
         weigh(1, 1, z, out_terms, 0)
         weigh(1, 0, z, out_terms, 1)
-        finish_on_vector(0, 0, HALF_T)
-        finish_on_tensor(0, 2, 4, banks[1], banks[2])
+        add_and_store(0, 0, RUNS)
         weigh(1, 1, z, out_terms, 1)
-        weigh(1, 0, z, out_terms, 2)
-        finish_on_vector(1, 0, T)
-        weigh(1, 1, z, out_terms, 2, 0, 3 * P)
-        weigh(1, 1, z, out_terms, 2, 3 * P, T)
-        finish_on_vector(2, 0, 3 * P)
-        finish_on_vector(2, 3 * P, T)
+        weigh(1, 0, z, out_terms, 2, 0, 2)
+        add_and_store(1, 0, RUNS)
+        weigh(1, 1, z, out_terms, 2, 0, 2)
+        weigh(1, 0, z, out_terms, 2, 2, RUNS)
+        add_and_store(2, 0, 2)
+        weigh(1, 1, z, out_terms, 2, 2, RUNS)
+        add_and_store(2, 2, RUNS)

@@ -16,8 +16,7 @@ FLOPS = 2 * 2 * K * K * S
 
 SINGLY = 6
 LAST = E - 1
-DIRECT = 2
-STAGED = E - DIRECT
+EARLY = 2
 WINDOW = 704
 PICKED = 2
 ZEROED_BY_GPSIMD = 512
@@ -228,7 +227,7 @@ def tile_moe_uni_none_kernel(
                 nc.tensor.transpose(bank[:, run(j)], pair_view[:, run(j)], ident[:])
             nc.scalar.copy(c_pair[u][:, runs(j0, j1)], bank[:, runs(j0, j1)])
 
-        staged = held.tile([P, 2 * STAGED * C], U32, name="staged", align_bytes=64)
+        staged = held.tile([P, 2 * S], U32, name="staged", align_bytes=64)
         grouped = [held.tile([P, 2 * 2 * C], U32, name="grouped%d" % e, align_bytes=64) for e in range(0, E, 2)]
         c_words = held.tile([P, S], U32, name="c_words", align_bytes=64)
         c_scales = held.tile([P, S], U8, name="c_scales", align_bytes=64)
@@ -270,15 +269,12 @@ def tile_moe_uni_none_kernel(
 
         def gather_pairs(u, e0, e1):
             gathered = c_pair[u][:].bitcast(U32).indirect(offs2_sb[:, entries(e0 * C, e1 * C)])
-            if e0 >= DIRECT:
-                nc.vector.tensor_copy(staged[:, slots(u * STAGED + e0 - DIRECT, u * STAGED + e1 - DIRECT)], gathered)
-            else:
-                nc.vector.tensor_copy(grouped[0][:, u::2], gathered)
+            nc.vector.tensor_copy(staged[:, slots(u * E + e0, u * E + e1)], gathered)
 
         def interleave(e0):
             nc.scalar.copy(
                 grouped[e0 // 2][:].rearrange("p (s u) -> p s u", u=2),
-                staged[:].rearrange("p (u s) -> p s u", u=2)[:, slots(e0 - DIRECT, e0 - DIRECT + 2), :],
+                staged[:].rearrange("p (u s) -> p s u", u=2)[:, slots(e0, e0 + 2), :],
             )
 
         def quantize(e0, e1):
@@ -289,11 +285,12 @@ def tile_moe_uni_none_kernel(
                 in_=grouped[e0 // 2][:].bitcast(BF16)[:, slots(PACK * first, PACK * (first + e1 - e0))],
             )
 
-        gather_pairs(0, DIRECT, DIRECT + STAGED // 2)
-        gather_pairs(0, DIRECT + STAGED // 2, E)
-        gather_pairs(0, 0, DIRECT)
-        gather_pairs(1, 0, DIRECT)
-        for e in range(DIRECT, E, 2):
+        gather_pairs(0, 0, 3)
+        gather_pairs(0, 3, SINGLY)
+        gather_pairs(0, SINGLY, E)
+        gather_pairs(1, 0, EARLY)
+        interleave(0)
+        for e in range(EARLY, E, 2):
             gather_pairs(1, e, e + 2)
             interleave(e)
             quantize(e - 2, e)
@@ -323,12 +320,12 @@ def tile_moe_uni_none_kernel(
         make_z([0], HALF_E, SINGLY, banks[1])
         make_z([0], SINGLY, LAST, banks[2], nc.vector.tensor_copy)
         make_z([0], LAST, E, banks[6], nc.vector.tensor_copy)
-        make_z([1, 2], 0, DIRECT, banks[3])
-        make_z([1], DIRECT, SINGLY, banks[0])
+        make_z([1, 2], 0, EARLY, banks[3])
+        make_z([1], EARLY, SINGLY, banks[0])
         make_z([1, 2], SINGLY, E, banks[5])
-        make_z([2], DIRECT, SINGLY, banks[1])
-        make_z([3], 0, DIRECT, banks[4])
-        make_z([3], DIRECT, SINGLY, banks[2])
+        make_z([2], EARLY, SINGLY, banks[1])
+        make_z([3], 0, EARLY, banks[4])
+        make_z([3], EARLY, SINGLY, banks[2])
         make_z([3], SINGLY, E, banks[7])
 
         out_terms = [[held.tile([P, T], F32, name="out_terms%d%d" % (r, m)) for m in range(TILES)] for r in range(2)]

@@ -16,7 +16,7 @@ FLOPS = 2 * 2 * K * K * S
 
 SINGLY = 6
 LAST = E - 1
-EARLY = 2
+SHARED_FROM = (4, 4, 2, 2)
 WINDOW = 704
 PICKED = 2
 ZEROED_BY_GPSIMD = 512
@@ -69,7 +69,7 @@ def tile_moe_uni_none_kernel(
         upper_words = [held.tile([P, HALF_E * P], I32, name="upper_words%d" % g, align_bytes=64) for g in range(2)]
         w_scales_sb = held.tile([P, E * K // 4], I32, name="w_scales_sb", align_bytes=64)
         gates = [held.tile([P, 2, T], F32, name="gate%d_sb" % (step + 1)) for step in range(2)]
-        gate_columns = [held.tile([P, 2, n], F32, name="gate_columns%d" % n) for n in (PICKED, RUNS)]
+        gate_columns = [held.tile([P, 4], F32, name="gate_columns%d" % step) for step in range(2)]
         ident = held.tile([P, P], F32, name="ident")
         banks = [psum.tile([P, RUNS * P], F32, name="bank%d" % b) for b in range(8)]
 
@@ -145,7 +145,7 @@ def tile_moe_uni_none_kernel(
             g, i = divmod(e, HALF_E)
             return pair_words[g][:, u, i, :].bitcast(U8).bitcast(FP4X4), pair_scales[g][:, u, i, :].bitcast(U8)
 
-        y = [held.tile([P, S], F32, name="y%d" % n) for n in range(TILES)]
+        y = [held.tile([P, S], F32, name="y%d" % n, tag="y%d" % n, align_bytes=64) for n in range(TILES)]
 
         def make_y(n, e0, e1, bank, copy=nc.scalar.copy):
             for e in range(e0, e1):
@@ -185,15 +185,15 @@ def tile_moe_uni_none_kernel(
             for j in range(j0, j1):
                 nc.tensor.transpose(bank[:, run(j)], terms[r][n][:, run(j)], ident[:])
 
-        def turn_gates(step, two_banks, count):
-            for r, bank in enumerate(two_banks):
-                for j in range(count):
-                    nc.tensor.transpose(bank[:, run(j)], gates[step][:, r, run(j)], ident[:])
-                nc.scalar.copy(gate_columns[step][:, r, :], bank[:, 0 : count * P : P])
+        def turn_gates(step, bank, j0):
+            for r in range(2):
+                for j in range(2):
+                    nc.tensor.transpose(bank[:, run(2 * r + j)], gates[step][:, r, run(j0 + j)], ident[:])
+            nc.scalar.copy(gate_columns[step][:], bank[:, 0 : RUNS * P : P])
 
         def weigh_turned(dst, bank, step, r, j0, j1):
             for j in range(j0, j1):
-                nc.scalar.activation(dst[:, run(j)], bank[:, run(j)], COPY, scale=gate_columns[step][:, r, j : j + 1])
+                nc.scalar.activation(dst[:, run(j)], bank[:, run(j)], COPY, scale=gate_columns[step][:, 2 * r + j : 2 * r + j + 1])
 
         def add_turned(bank, parts):
             for i, (columns, source) in enumerate(parts):
@@ -227,8 +227,10 @@ def tile_moe_uni_none_kernel(
                 nc.tensor.transpose(bank[:, run(j)], pair_view[:, run(j)], ident[:])
             nc.scalar.copy(c_pair[u][:, runs(j0, j1)], bank[:, runs(j0, j1)])
 
-        staged = held.tile([P, 2 * S], U32, name="staged", align_bytes=64)
-        grouped = [held.tile([P, 2 * 2 * C], U32, name="grouped%d" % e, align_bytes=64) for e in range(0, E, 2)]
+        grouped = [
+            held.tile([P, 2 * 2 * C], U32, name="grouped%d" % e, tag="grouped%d" % e, align_bytes=64)
+            for e in range(0, E, 2)
+        ]
         c_words = held.tile([P, S], U32, name="c_words", align_bytes=64)
         c_scales = held.tile([P, S], U8, name="c_scales", align_bytes=64)
 
@@ -237,7 +239,7 @@ def tile_moe_uni_none_kernel(
             weigh(0, 1, y, c_terms, n)
         weigh(0, 0, y, c_terms, 2, PICKED, RUNS)
         weigh(0, 1, y, c_terms, 2, PICKED, RUNS)
-        turn_gates(0, (banks[5], banks[6]), PICKED)
+        turn_gates(0, banks[5], 0)
         pick(0, 1, y, c_terms, 2, banks[3], 0, PICKED)
         pick(0, 0, y, c_terms, 2, banks[4], 0, PICKED)
         weigh_turned(second_term, banks[3], 0, 1, 0, PICKED)
@@ -245,7 +247,7 @@ def tile_moe_uni_none_kernel(
             nc.vector.scalar_tensor_tensor(
                 c_turned[:, 0, j, 1, :],
                 banks[4][:, run(j)],
-                gate_columns[0][:, 0, j : j + 1],
+                gate_columns[0][:, j : j + 1],
                 second_term[:, run(j)],
                 MULT,
                 ADD,
@@ -263,19 +265,12 @@ def tile_moe_uni_none_kernel(
         turn_back(0, 2, RUNS, banks[4])
         for (j0, j1), b in zip(pieces, (3, 5, 4)):
             sum_upper(1, j0, j1, banks[b])
-        turn_back(1, 0, 3, banks[6])
-        turn_back(1, 3, RUNS, banks[7])
-        turn_gates(1, (banks[6], banks[7]), RUNS)
+        for (j0, j1), b in zip(pieces, (6, 7, 1)):
+            turn_back(1, j0, j1, banks[b])
 
-        def gather_pairs(u, e0, e1):
-            gathered = c_pair[u][:].bitcast(U32).indirect(offs2_sb[:, entries(e0 * C, e1 * C)])
-            nc.vector.tensor_copy(staged[:, slots(u * E + e0, u * E + e1)], gathered)
-
-        def interleave(e0):
-            nc.scalar.copy(
-                grouped[e0 // 2][:].rearrange("p (s u) -> p s u", u=2),
-                staged[:].rearrange("p (u s) -> p s u", u=2)[:, slots(e0, e0 + 2), :],
-            )
+        def gather_pairs(u, e0):
+            gathered = c_pair[u][:].bitcast(U32).indirect(offs2_sb[:, entries(e0 * C, (e0 + 2) * C)])
+            nc.vector.tensor_copy(grouped[e0 // 2][:, u::2], gathered)
 
         def quantize(e0, e1):
             first = e0 % 2
@@ -285,24 +280,32 @@ def tile_moe_uni_none_kernel(
                 in_=grouped[e0 // 2][:].bitcast(BF16)[:, slots(PACK * first, PACK * (first + e1 - e0))],
             )
 
-        gather_pairs(0, 0, 3)
-        gather_pairs(0, 3, SINGLY)
-        gather_pairs(0, SINGLY, E)
-        gather_pairs(1, 0, EARLY)
-        interleave(0)
-        for e in range(EARLY, E, 2):
-            gather_pairs(1, e, e + 2)
-            interleave(e)
-            quantize(e - 2, e)
-        for e in range(SINGLY, E):
-            quantize(e, e + 1)
+        c_single = held.tile([P, 2 * T], BF16, name="c_single", tag="y3", align_bytes=64)
+        nc.gpsimd.tensor_copy(
+            c_single[:].rearrange("p (i t) -> p i t", i=2), c_pair[0][:].bitcast(BF16).rearrange("p (t i) -> p i t", i=2)
+        )
+        for i in range(2):
+            gathered = c_single[:, i * T : (i + 1) * T].indirect(offs2_sb[:, entries(SINGLY * C, S)])
+            nc.scalar.activation(grouped[SINGLY // 2][:].bitcast(BF16)[:, i::PACK], gathered, COPY)
+        turn_gates(1, banks[6], 2)
+
+        for e in range(0, SINGLY, 2):
+            gather_pairs(0, e)
+        gather_pairs(1, 0)
+        gather_pairs(1, 2)
+        quantize(0, 2)
+        quantize(2, HALF_E)
+        gather_pairs(1, HALF_E)
+        gather_pairs(1, SINGLY)
+        quantize(HALF_E, SINGLY)
+        quantize(SINGLY, E)
 
         z = [held.tile([P, S], F32, name="z%d" % m) for m in range(TILES)]
 
         def make_z(tiles, e0, e1, bank, copy=nc.scalar.copy):
             width = e1 - e0
             for i, m in enumerate(tiles):
-                for e in range(e0, e1):
+                for e in range(e0, e1) if e1 < E or m == 0 else reversed(range(e0, e1)):
                     words, scales = columns_in_order(e, m)
                     nc.tensor.matmul_mx(
                         bank[:, slots(i * width + e - e0, i * width + e - e0 + 1)],
@@ -317,47 +320,56 @@ def tile_moe_uni_none_kernel(
                 copy(z[m][:, slots(e0, e1)], bank[:, slots(i * width, (i + 1) * width)])
 
         make_z([0], 0, HALF_E, banks[0])
-        make_z([0], HALF_E, SINGLY, banks[1])
-        make_z([0], SINGLY, LAST, banks[2], nc.vector.tensor_copy)
-        make_z([0], LAST, E, banks[6], nc.vector.tensor_copy)
-        make_z([1, 2], 0, EARLY, banks[3])
-        make_z([1], EARLY, SINGLY, banks[0])
-        make_z([1, 2], SINGLY, E, banks[5])
-        make_z([2], EARLY, SINGLY, banks[1])
-        make_z([3], 0, EARLY, banks[4])
-        make_z([3], EARLY, SINGLY, banks[2])
-        make_z([3], SINGLY, E, banks[7])
+        make_z([0], HALF_E, SINGLY, banks[4], nc.vector.tensor_copy)
+        make_z([0], SINGLY, E, banks[5], nc.vector.tensor_copy)
+        make_z([1], 0, HALF_E, banks[1])
+        for m, b in ((1, 2), (2, 3), (3, 7)):
+            make_z([m], HALF_E, E, banks[b])
+        make_z([2], 0, HALF_E, banks[4])
+        make_z([3], 0, HALF_E, banks[5])
 
         out_terms = [[held.tile([P, T], F32, name="out_terms%d%d" % (r, m)) for m in range(TILES)] for r in range(2)]
         result = held.tile([P, TILES, T], F32, name="result")
-        turned_terms = [held.tile([P, T], F32, name="turned_terms%d" % r) for r in range(2)]
 
-        def add_and_store(m, j0, j1):
-            tokens = runs(j0, j1)
+        def add_and_store(m):
+            tokens = runs(0, SHARED_FROM[m])
             nc.vector.tensor_tensor(result[:, m, tokens], out_terms[0][m][:, tokens], out_terms[1][m][:, tokens], ADD)
             nc.sync.dma_start(out[run(m), tokens], result[:, m, tokens])
 
-        pick(1, 0, z, out_terms, 3, banks[3], 0, RUNS)
-        pick(1, 1, z, out_terms, 3, banks[4], 0, 2)
-        weigh_turned(turned_terms[0], banks[3], 1, 0, 0, 2)
-        pick(1, 1, z, out_terms, 3, banks[6], 2, RUNS)
-        weigh_turned(turned_terms[1], banks[4], 1, 1, 0, 2)
-        weigh_turned(turned_terms[0], banks[3], 1, 0, 2, RUNS)
-        weigh_turned(turned_terms[1], banks[6], 1, 1, 2, RUNS)
-        for j0, bank in ((0, banks[5]), (2, banks[0])):
-            add_turned(bank, [(run(j), turned_terms[r][:, run(j0 + j)]) for r in range(2) for j in range(2)])
-            nc.scalar.copy(result[:, 3, runs(j0, j0 + 2)], bank[:, :HALF_T])
-            nc.scalar.dma_start(out[run(3), runs(j0, j0 + 2)], result[:, 3, runs(j0, j0 + 2)])
+        shared_runs = (3, 2)
+        first_tile = {j: min(m for m in range(TILES) if SHARED_FROM[m] <= j) for j in shared_runs}
+        term_banks = {(0, 3): banks[0], (0, 2): banks[1], (1, 3): banks[2], (1, 2): banks[3]}
+        sum_banks = {3: banks[6], 2: banks[7]}
+        for r in range(2):
+            for m in range(2, TILES):
+                j0 = SHARED_FROM[m]
+                gathered = z[m][:].indirect(pos_sb[2 + r][:, entries(j0 * P, T)])
+                nc.scalar.activation(out_terms[r][m][:, runs(j0, RUNS)], gathered, COPY)
+                for j in range(j0, RUNS):
+                    nc.tensor.transpose(term_banks[r, j][:, run(m)], out_terms[r][m][:, run(j)], ident[:])
+        weighed = {}
+        for r in range(2):
+            for j in shared_runs:
+                rows = runs(first_tile[j], TILES)
+                weighed[r, j] = held.tile([P, T], F32, name="weighed%d%d" % (r, j))
+                scale = gate_columns[1][:, 2 * r + j - 2 : 2 * r + j - 1]
+                nc.scalar.activation(weighed[r, j][:, rows], term_banks[r, j][:, rows], COPY, scale=scale)
+        for j in shared_runs:
+            rows = runs(first_tile[j], TILES)
+            add_turned(
+                sum_banks[j],
+                [(run(m), weighed[r, j][:, run(m)]) for r in range(2) for m in range(first_tile[j], TILES)],
+            )
+            summed = held.tile([P, T], F32, name="summed%d" % j)
+            nc.scalar.copy(summed[:, rows], sum_banks[j][:, rows])
+            nc.scalar.dma_start(
+                out[rows, run(j)].rearrange("(m p) t -> p m t", p=P), summed[:, rows].rearrange("p (m t) -> p m t", t=P)
+            )
 
         weigh(1, 0, z, out_terms, 0)
         weigh(1, 1, z, out_terms, 0)
-        weigh(1, 0, z, out_terms, 1)
-        add_and_store(0, 0, RUNS)
-        weigh(1, 1, z, out_terms, 1)
-        weigh(1, 0, z, out_terms, 2, 0, 2)
-        add_and_store(1, 0, RUNS)
-        weigh(1, 1, z, out_terms, 2, 0, 2)
-        weigh(1, 0, z, out_terms, 2, 2, RUNS)
-        add_and_store(2, 0, 2)
-        weigh(1, 1, z, out_terms, 2, 2, RUNS)
-        add_and_store(2, 2, RUNS)
+        for m in range(1, TILES):
+            weigh(1, 0, z, out_terms, m, 0, SHARED_FROM[m])
+            add_and_store(m - 1)
+            weigh(1, 1, z, out_terms, m, 0, SHARED_FROM[m])
+        add_and_store(TILES - 1)

@@ -231,6 +231,7 @@ def tile_moe_uni_none_kernel(
             held.tile([P, 2 * 2 * C], U32, name="grouped%d" % e, tag="grouped%d" % e, align_bytes=64)
             for e in range(0, E, 2)
         ]
+        staged = held.tile([P, 2 * S], U32, name="staged", align_bytes=64)
         c_words = held.tile([P, S], U32, name="c_words", align_bytes=64)
         c_scales = held.tile([P, S], U8, name="c_scales", align_bytes=64)
 
@@ -268,9 +269,18 @@ def tile_moe_uni_none_kernel(
         for (j0, j1), b in zip(pieces, (6, 7, 1)):
             turn_back(1, j0, j1, banks[b])
 
-        def gather_pairs(u, e0):
-            gathered = c_pair[u][:].bitcast(U32).indirect(offs2_sb[:, entries(e0 * C, (e0 + 2) * C)])
-            nc.vector.tensor_copy(grouped[e0 // 2][:, u::2], gathered)
+        def listed_pairs(u, e0, e1):
+            return c_pair[u][:].bitcast(U32).indirect(offs2_sb[:, entries(e0 * C, e1 * C)])
+
+        def stage(u, e0, e1):
+            nc.vector.tensor_copy(staged[:, slots(u * E + e0, u * E + e1)], listed_pairs(u, e0, e1))
+
+        def interleave(e0, e1):
+            first = e0 % 2
+            nc.scalar.copy(
+                grouped[e0 // 2][:, slots(2 * first, 2 * (first + e1 - e0))].rearrange("p (s u) -> p s u", u=2),
+                staged[:].rearrange("p (u s) -> p s u", u=2)[:, slots(e0, e1), :],
+            )
 
         def quantize(e0, e1):
             first = e0 % 2
@@ -280,25 +290,15 @@ def tile_moe_uni_none_kernel(
                 in_=grouped[e0 // 2][:].bitcast(BF16)[:, slots(PACK * first, PACK * (first + e1 - e0))],
             )
 
-        c_single = held.tile([P, 2 * T], BF16, name="c_single", tag="y3", align_bytes=64)
-        nc.gpsimd.tensor_copy(
-            c_single[:].rearrange("p (i t) -> p i t", i=2), c_pair[0][:].bitcast(BF16).rearrange("p (t i) -> p i t", i=2)
-        )
-        for i in range(2):
-            gathered = c_single[:, i * T : (i + 1) * T].indirect(offs2_sb[:, entries(SINGLY * C, S)])
-            nc.scalar.activation(grouped[SINGLY // 2][:].bitcast(BF16)[:, i::PACK], gathered, COPY)
+        for e0, e1 in ((0, 3), (3, SINGLY), (SINGLY, E)):
+            stage(0, e0, e1)
         turn_gates(1, banks[6], 2)
-
-        for e in range(0, SINGLY, 2):
-            gather_pairs(0, e)
-        gather_pairs(1, 0)
-        gather_pairs(1, 2)
-        quantize(0, 2)
-        quantize(2, HALF_E)
-        gather_pairs(1, HALF_E)
-        gather_pairs(1, SINGLY)
-        quantize(HALF_E, SINGLY)
-        quantize(SINGLY, E)
+        shares = ((0, 2), (2, HALF_E), (HALF_E, SINGLY), (SINGLY, LAST), (LAST, E))
+        for e0, e1 in shares:
+            stage(1, e0, e1)
+            interleave(e0, e1)
+        for e0, e1 in shares:
+            quantize(e0, e1)
 
         z = [held.tile([P, S], F32, name="z%d" % m) for m in range(TILES)]
 
@@ -322,11 +322,9 @@ def tile_moe_uni_none_kernel(
         make_z([0], 0, HALF_E, banks[0])
         make_z([0], HALF_E, SINGLY, banks[4], nc.vector.tensor_copy)
         make_z([0], SINGLY, E, banks[5], nc.vector.tensor_copy)
-        make_z([1], 0, HALF_E, banks[1])
-        for m, b in ((1, 2), (2, 3), (3, 7)):
-            make_z([m], HALF_E, E, banks[b])
-        make_z([2], 0, HALF_E, banks[4])
-        make_z([3], 0, HALF_E, banks[5])
+        for m, upper, lower in ((1, 1, 4), (2, 2, 5), (3, 3, 0)):
+            make_z([m], HALF_E, E, banks[upper])
+            make_z([m], 0, HALF_E, banks[lower])
 
         out_terms = [[held.tile([P, T], F32, name="out_terms%d%d" % (r, m)) for m in range(TILES)] for r in range(2)]
         result = held.tile([P, TILES, T], F32, name="result")
@@ -338,8 +336,8 @@ def tile_moe_uni_none_kernel(
 
         shared_runs = (3, 2)
         first_tile = {j: min(m for m in range(TILES) if SHARED_FROM[m] <= j) for j in shared_runs}
-        term_banks = {(0, 3): banks[0], (0, 2): banks[1], (1, 3): banks[2], (1, 2): banks[3]}
-        sum_banks = {3: banks[6], 2: banks[7]}
+        term_banks = {(0, 3): banks[7], (0, 2): banks[1], (1, 3): banks[4], (1, 2): banks[2]}
+        sum_banks = {3: banks[6], 2: banks[5]}
         for r in range(2):
             for m in range(2, TILES):
                 j0 = SHARED_FROM[m]

@@ -63,7 +63,7 @@ def tile_moe_uni_none_kernel(
         offs2_sb = lists.tile([P, S // PER_COLUMN], U16, name="offs2_sb")
         pos_sb = [lists.tile([P, T // PER_COLUMN], U16, name="pos%d_sb" % (n + 1)) for n in range(4)]
 
-        x_words_sb = held.tile([P, WINDOW], I32, name="x_words_sb", align_bytes=64)
+        x_words_sb = held.tile([P, WINDOW], I32, name="x_words_sb", tag="words_then_pairs", align_bytes=64)
         x_scales_sb = held.tile([P, WINDOW // 4], I32, name="x_scales_sb", tag="scales_then_words", align_bytes=64)
         lower_words = held.tile([P, E * P], I32, name="lower_words", align_bytes=64)
         upper_words = [held.tile([P, HALF_E * P], I32, name="upper_words%d" % g, align_bytes=64) for g in range(2)]
@@ -123,13 +123,16 @@ def tile_moe_uni_none_kernel(
             gather_words(late_words[:, slots(e0 - HALF_E, e1 - HALF_E)], e0, e1)
         slot_words = [early_words, late_words]
 
-        pair_words = [held.tile([P, 2, HALF_E, P // 2], U32, name="pair_words%d" % g, align_bytes=64) for g in range(2)]
+        pair_words = [
+            held.tile([P, 2, HALF_E, P // 2], U32, name="pair_words%d" % g, tag=tag, align_bytes=64)
+            for g, tag in enumerate(("pair_words0", "words_then_pairs"))
+        ]
         pair_scales = [held.tile([P, 2, HALF_E, P // 2], U16, name="pair_scales%d" % g, align_bytes=64) for g in range(2)]
         w_scale_bytes = w_scales_sb[:].bitcast(U8)
 
-        def sort_words(g):
-            pairs = upper_words[g][:].bitcast(U32).rearrange("p (i q u) -> p u i q", i=HALF_E, u=2)
-            nc.gpsimd.tensor_copy(pair_words[g][:], pairs)
+        def sort_words(g, copy, dtype):
+            pairs = upper_words[g][:].bitcast(dtype).rearrange("p (i q u) -> p u i q", i=HALF_E, u=2)
+            copy(pair_words[g][:].bitcast(dtype), pairs)
 
         def sort_scales(g):
             pairs = w_scales_sb[:].bitcast(U16).rearrange("p (g i h q u) -> p g h u i q", g=2, i=HALF_E, h=2, u=2)
@@ -162,14 +165,14 @@ def tile_moe_uni_none_kernel(
                 )
             copy(y[n][:, slots(e0, e1)], bank[:, slots(0, e1 - e0)])
 
-        sort_words(0)
         sort_scales(0)
         sort_scales(1)
-        sort_words(1)
+        sort_words(0, nc.scalar.copy, U32)
         make_y(0, 0, HALF_E, banks[0])
         make_y(1, 0, HALF_E, banks[3])
         make_y(0, HALF_E, SINGLY, banks[1])
         make_y(0, SINGLY, LAST, banks[2], nc.vector.tensor_copy)
+        sort_words(1, nc.vector.tensor_copy, I32)
         make_y(0, LAST, E, banks[7], nc.vector.tensor_copy)
         make_y(1, HALF_E, E, banks[4])
         make_y(2, 0, HALF_E, banks[5])

@@ -207,8 +207,10 @@ def tile_moe_uni_none_kernel(
 
         c_terms = [[held.tile([P, T], F32, name="c_terms%d%d" % (r, n)) for n in range(TILES)] for r in range(2)]
         c_turned = held.tile([P, 2, RUNS, 2, P], BF16, name="c_turned")
-        c_pair = [held.tile([P, T], F32, name="c_pair%d" % u) for u in range(2)]
+        c_pair = [held.tile([P, width], F32, name="c_pair%d" % u) for u, width in enumerate((WINDOW, T))]
         second_term = held.tile([P, T], F32, name="second_term")
+
+        nc.gpsimd.memset(c_pair[0][:, T:], 0.0)
 
         def sum_lower(j0, bank):
             parts = [
@@ -293,8 +295,8 @@ def tile_moe_uni_none_kernel(
                 in_=grouped[e0 // 2][:].bitcast(BF16)[:, slots(PACK * first, PACK * (first + e1 - e0))],
             )
 
-        for e0, e1 in ((0, 3), (3, SINGLY), (SINGLY, E)):
-            stage(0, e0, e1)
+        for e0 in (0, HALF_E):
+            stage(0, e0, e0 + HALF_E)
         turn_gates(1, banks[6], 2)
         shares = ((0, 2), (2, HALF_E), (HALF_E, SINGLY), (SINGLY, LAST), (LAST, E))
         for e0, e1 in shares:
@@ -369,8 +371,11 @@ def tile_moe_uni_none_kernel(
 
         weigh(1, 0, z, out_terms, 0)
         weigh(1, 1, z, out_terms, 0)
-        for m in range(1, TILES):
+        for m in range(1, TILES - 1):
             weigh(1, 0, z, out_terms, m, 0, SHARED_FROM[m])
             add_and_store(m - 1)
             weigh(1, 1, z, out_terms, m, 0, SHARED_FROM[m])
+        for r in range(2):
+            weigh(1, r, z, out_terms, TILES - 1, 0, SHARED_FROM[TILES - 1])
+        add_and_store(TILES - 2)
         add_and_store(TILES - 1)

@@ -212,14 +212,11 @@ def tile_moe_uni_none_kernel(
 
         nc.gpsimd.memset(c_pair[0][:, T:], 0.0)
 
-        def sum_lower(j0, bank):
-            parts = [
-                (run(2 * j + n), c_terms[r][n][:, run(j0 + j)]) for n in range(2) for r in range(2) for j in range(2)
-            ]
-            add_turned(bank, parts)
+        def sum_lower(n, bank):
+            add_turned(bank, [(run(j), c_terms[r][n][:, run(j)]) for r in range(2) for j in range(RUNS)])
             nc.scalar.copy(
-                c_turned[:, :, j0 : j0 + 2, 0, :].rearrange("a u j (q i) -> a u j q i", i=2),
-                bank[:].rearrange("a (j q u i) -> a u j q i", j=2, u=2, i=2),
+                c_turned[:, :, :, 0, n * P // 2 : (n + 1) * P // 2].rearrange("a u j (q i) -> a u j q i", i=2),
+                bank[:].rearrange("a (j q u i) -> a u j q i", j=RUNS, u=2, i=2),
             )
 
         def sum_upper(u, j0, j1, bank):
@@ -232,11 +229,12 @@ def tile_moe_uni_none_kernel(
                 nc.tensor.transpose(bank[:, run(j)], pair_view[:, run(j)], ident[:])
             nc.scalar.copy(c_pair[u][:, runs(j0, j1)], bank[:, runs(j0, j1)])
 
-        grouped = [
-            held.tile([P, 2 * 2 * C], U32, name="grouped%d" % e, tag="grouped%d" % e, align_bytes=64)
-            for e in range(0, E, 2)
+        reused = (E + SINGLY) * C
+        staged_then_grouped = held.tile([P, reused + 2 * 2 * C], U32, name="staged_then_grouped", align_bytes=64)
+        staged = staged_then_grouped[:, : 2 * S]
+        grouped = [staged_then_grouped[:, reused:]] + [
+            held.tile([P, 2 * 2 * C], U32, name="grouped%d" % e, align_bytes=64)[:] for e in range(2, E, 2)
         ]
-        staged = held.tile([P, 2 * S], U32, name="staged", align_bytes=64)
         c_words = held.tile([P, S], U32, name="c_words", align_bytes=64)
         c_scales = held.tile([P, S], U8, name="c_scales", align_bytes=64)
 
@@ -265,7 +263,7 @@ def tile_moe_uni_none_kernel(
         for j0, j1 in pieces:
             weigh(0, 1, y, c_terms, 3, j0, j1)
         sum_lower(0, banks[1])
-        sum_lower(2, banks[2])
+        sum_lower(1, banks[2])
         sum_upper(0, PICKED, RUNS, banks[3])
         turn_back(0, 0, 2, banks[5])
         turn_back(0, 2, RUNS, banks[4])
@@ -284,7 +282,7 @@ def tile_moe_uni_none_kernel(
             first = e0 % 2
             nc.scalar.copy(
                 grouped[e0 // 2][:, slots(2 * first, 2 * (first + e1 - e0))].rearrange("p (s u) -> p s u", u=2),
-                staged[:].rearrange("p (u s) -> p s u", u=2)[:, slots(e0, e1), :],
+                staged.rearrange("p (u s) -> p s u", u=2)[:, slots(e0, e1), :],
             )
 
         def quantize(e0, e1):
@@ -292,17 +290,22 @@ def tile_moe_uni_none_kernel(
             nc.vector.quantize_mx(
                 out=c_words[:, slots(e0, e1)].bitcast(FP8X4),
                 scales=c_scales[:, slots(e0, e1)],
-                in_=grouped[e0 // 2][:].bitcast(BF16)[:, slots(PACK * first, PACK * (first + e1 - e0))],
+                in_=grouped[e0 // 2].bitcast(BF16)[:, slots(PACK * first, PACK * (first + e1 - e0))],
             )
 
         for e0 in (0, HALF_E):
             stage(0, e0, e0 + HALF_E)
         turn_gates(1, banks[6], 2)
         shares = ((0, 2), (2, HALF_E), (HALF_E, SINGLY), (SINGLY, LAST), (LAST, E))
-        for e0, e1 in shares:
+        for e0, e1 in shares[:3]:
             stage(1, e0, e1)
             interleave(e0, e1)
-        for e0, e1 in shares:
+        for e0, e1 in shares[:2]:
+            quantize(e0, e1)
+        for e0, e1 in shares[3:]:
+            stage(1, e0, e1)
+            interleave(e0, e1)
+        for e0, e1 in shares[2:]:
             quantize(e0, e1)
 
         z = [held.tile([P, S], F32, name="z%d" % m) for m in range(TILES)]
@@ -327,9 +330,13 @@ def tile_moe_uni_none_kernel(
         make_z([0], 0, HALF_E, banks[0])
         make_z([0], HALF_E, SINGLY, banks[4], nc.vector.tensor_copy)
         make_z([0], SINGLY, E, banks[5], nc.vector.tensor_copy)
-        for m, upper, lower in ((1, 1, 4), (2, 2, 5), (3, 3, 0)):
-            make_z([m], HALF_E, E, banks[upper])
-            make_z([m], 0, HALF_E, banks[lower])
+        make_z([1], 0, 2, banks[7])
+        make_z([1], HALF_E, E, banks[1])
+        make_z([1], 2, HALF_E, banks[4])
+        make_z([2], HALF_E, E, banks[2])
+        make_z([2], 0, HALF_E, banks[5])
+        make_z([3], HALF_E, E, banks[3])
+        make_z([3], 0, HALF_E, banks[1])
 
         out_terms = [[held.tile([P, T], F32, name="out_terms%d%d" % (r, m)) for m in range(TILES)] for r in range(2)]
         result = held.tile([P, TILES, T], F32, name="result")
@@ -341,7 +348,7 @@ def tile_moe_uni_none_kernel(
 
         shared_runs = (3, 2)
         first_tile = {j: min(m for m in range(TILES) if SHARED_FROM[m] <= j) for j in shared_runs}
-        term_banks = {(0, 3): banks[7], (0, 2): banks[1], (1, 3): banks[4], (1, 2): banks[2]}
+        term_banks = {(0, 3): banks[0], (0, 2): banks[7], (1, 3): banks[4], (1, 2): banks[2]}
         sum_banks = {3: banks[6], 2: banks[5]}
         for r in range(2):
             for m in range(2, TILES):

from contextlib import ExitStack

import concourse.mybir as mybir
from concourse.masks import make_identity

K, T, E, C = 512, 512, 8, 128
S = E * C
P = 128
PACK = 4
TILES = K // P
PER_COLUMN = 16
SCALE_ROWS = K // 32
HALF_E, HALF_T = E // 2, T // 2
RUNS = T // P
FLOPS = 2 * 2 * K * K * S

SINGLY = 6
LAST = E - 1
SHARED_FROM = (4, 4, 2, 2)
WINDOW = 704
PICKED = 2
ZEROED_BY_GPSIMD = 512

F32 = mybir.dt.float32
BF16 = mybir.dt.bfloat16
I32 = mybir.dt.int32
U32 = mybir.dt.uint32
U16 = mybir.dt.uint16
U8 = mybir.dt.uint8
FP8X4 = mybir.dt.float8_e4m3fn_x4
FP4X4 = mybir.dt.float4_e2m1fn_x4
MULT = mybir.AluOpType.mult
ADD = mybir.AluOpType.add
COPY = mybir.ActivationFunctionType.Copy


def entries(first, last):
    return slice(first // PER_COLUMN, last // PER_COLUMN)


def slots(e0, e1):
    return slice(e0 * C, e1 * C)


def runs(j0, j1):
    return slice(j0 * P, j1 * P)


def run(j):
    return runs(j, j + 1)


def tile_moe_uni_none_kernel(
    tc, x_words, x_scales, w_words, w_scales, gate1, gate2, offs, pos1, pos2, offs2, pos3, pos4, out
):
    nc = tc.nc
    with ExitStack() as ctx:
        lists = ctx.enter_context(tc.tile_pool(name="lists", bufs=1))
        held = ctx.enter_context(tc.tile_pool(name="held", bufs=1))
        psum = ctx.enter_context(tc.psum_pool(name="psum", bufs=1))

        offs_sb = lists.tile([P, S // PER_COLUMN], U16, name="offs_sb")
        offs2_sb = lists.tile([P, S // PER_COLUMN], U16, name="offs2_sb")
        pos_sb = [lists.tile([P, T // PER_COLUMN], U16, name="pos%d_sb" % (n + 1)) for n in range(4)]

        x_words_sb = held.tile([P, WINDOW], I32, name="x_words_sb", tag="words_then_pairs", align_bytes=64)
        x_scales_sb = held.tile([P, WINDOW // 4], I32, name="x_scales_sb", tag="scales_then_words", align_bytes=64)
        lower_words = held.tile([P, E * P], I32, name="lower_words", align_bytes=64)
        upper_words = [held.tile([P, HALF_E * P], I32, name="upper_words%d" % g, align_bytes=64) for g in range(2)]
        w_scales_sb = held.tile([P, E * K // 4], I32, name="w_scales_sb", align_bytes=64)
        gates = [held.tile([P, 2, T], F32, name="gate%d_sb" % (step + 1)) for step in range(2)]
        gate_columns = [held.tile([P, 4], F32, name="gate_columns%d" % step) for step in range(2)]
        ident = held.tile([P, P], F32, name="ident")
        banks = [psum.tile([P, RUNS * P], F32, name="bank%d" % b) for b in range(8)]

        nc.gpsimd.memset(x_scales_sb[:], 0)
        nc.gpsimd.memset(x_words_sb[:, T:], 0)
        nc.gpsimd.memset(w_scales_sb[:, :ZEROED_BY_GPSIMD], 0)
        nc.vector.memset(w_scales_sb[:, ZEROED_BY_GPSIMD:], 0)
        ident_bf16 = held.tile([P, P], BF16, name="ident_bf16")
        make_identity(nc, ident_bf16[:])
        nc.scalar.activation(ident[:], ident_bf16[:], COPY)

        def load_words(dst, e0, e1, h):
            nc.sync.dma_start(
                dst[:].rearrange("p (e n) -> p e n", e=e1 - e0),
                w_words[e0:e1, 0, :, h * K : (h + 1) * K].rearrange("e p n -> p e n").bitcast(I32),
            )

        nc.sync.dma_start(x_words_sb[:, :T], x_words[0].rearrange("p t d -> p (t d)").bitcast(I32))
        nc.sync.dma_start(offs_sb[:], offs)
        for r in range(4):
            nc.sync.dma_start(x_scales_sb[r:P:32, : T // 4], x_scales[0, r:SCALE_ROWS:4, :].bitcast(I32))
        for r in range(4):
            nc.sync.dma_start(
                w_scales_sb[r:P:32, :].rearrange("q (e n) -> q e n", e=E),
                w_scales[:, 0, r:SCALE_ROWS:4, :].rearrange("e q n -> q e n").bitcast(I32),
            )
        load_words(lower_words, 0, E, 0)
        load_words(upper_words[0], 0, HALF_E, 1)
        load_words(upper_words[1], HALF_E, E, 1)
        nc.sync.dma_start(pos_sb[0][:], pos1)
        nc.sync.dma_start(pos_sb[1][:], pos2)
        nc.sync.dma_start(gates[0][:], gate1.rearrange("r p t -> p r t"))
        nc.sync.dma_start(offs2_sb[:], offs2)
        nc.sync.dma_start(pos_sb[2][:], pos3)
        nc.sync.dma_start(pos_sb[3][:], pos4)
        nc.sync.dma_start(gates[1][:], gate2.rearrange("r p t -> p r t"))

        early_words = held.tile([P, HALF_E * C], U32, name="early_words", align_bytes=64)
        slot_scales = [held.tile([P, HALF_E * C], U8, name="slot_scales%d" % g, align_bytes=64) for g in range(2)]

        def gather_words(dst, e0, e1):
            window = x_words_sb[:].bitcast(U32)
            nc.vector.tensor_copy(dst, window.indirect(offs_sb[:, entries(e0 * C, e1 * C)]))

        gather_words(early_words[:], 0, HALF_E)
        for g in range(2):
            listed = offs_sb[:, entries(g * HALF_E * C, (g + 1) * HALF_E * C)]
            nc.vector.tensor_copy(slot_scales[g][:], x_scales_sb[:].bitcast(U8).indirect(listed))
        late_words = held.tile([P, HALF_E * C], U32, name="late_words", tag="scales_then_words", align_bytes=64)
        for e0, e1 in ((HALF_E, SINGLY), (SINGLY, LAST), (LAST, E)):
            gather_words(late_words[:, slots(e0 - HALF_E, e1 - HALF_E)], e0, e1)
        slot_words = [early_words, late_words]

        pair_words = [
            held.tile([P, 2, HALF_E, P // 2], U32, name="pair_words%d" % g, tag=tag, align_bytes=64)
            for g, tag in enumerate(("pair_words0", "words_then_pairs"))
        ]
        pair_scales = [held.tile([P, 2, HALF_E, P // 2], U16, name="pair_scales%d" % g, align_bytes=64) for g in range(2)]
        w_scale_bytes = w_scales_sb[:].bitcast(U8)

        def sort_words(g, copy, dtype):
            pairs = upper_words[g][:].bitcast(dtype).rearrange("p (i q u) -> p u i q", i=HALF_E, u=2)
            copy(pair_words[g][:].bitcast(dtype), pairs)

        def sort_scales(g):
            pairs = w_scales_sb[:].bitcast(U16).rearrange("p (g i h q u) -> p g h u i q", g=2, i=HALF_E, h=2, u=2)
            nc.scalar.copy(pair_scales[g][:], pairs[:, g, 1])

        def columns_in_order(e, m):
            tile, i = (lower_words, e) if m < 2 else (upper_words[e // HALF_E], e % HALF_E)
            column = (2 * i + m % 2) * P
            words = tile[:].bitcast(U8)[:, 2 * column : 2 * (column + P)]
            return words.bitcast(FP4X4), w_scale_bytes[:, e * K + m * P : e * K + (m + 1) * P]

        def columns_sorted(e, u):
            g, i = divmod(e, HALF_E)
            return pair_words[g][:, u, i, :].bitcast(U8).bitcast(FP4X4), pair_scales[g][:, u, i, :].bitcast(U8)

        y = [held.tile([P, S], F32, name="y%d" % n, tag="y%d" % n, align_bytes=64) for n in range(TILES)]

        def make_y(n, e0, e1, bank, copy=nc.scalar.copy):
            for e in range(e0, e1):
                words, scales = columns_in_order(e, n) if n < 2 else columns_sorted(e, n - 2)
                g, i = divmod(e, HALF_E)
                nc.tensor.matmul_mx(
                    bank[:, slots(e - e0, e - e0 + 1)],
                    lhsT=words,
                    lhsT_scale=scales,
                    rhs=slot_words[g][:, slots(i, i + 1)].bitcast(FP8X4),
                    rhs_scale=slot_scales[g][:, slots(i, i + 1)],
                    start=True,
                    stop=True,
                )
            copy(y[n][:, slots(e0, e1)], bank[:, slots(0, e1 - e0)])

        sort_scales(0)
        sort_scales(1)
        sort_words(0, nc.scalar.copy, U32)
        make_y(0, 0, HALF_E, banks[0])
        make_y(1, 0, HALF_E, banks[3])
        make_y(0, HALF_E, SINGLY, banks[1])
        make_y(0, SINGLY, LAST, banks[2], nc.vector.tensor_copy)
        sort_words(1, nc.vector.tensor_copy, I32)
        make_y(0, LAST, E, banks[7], nc.vector.tensor_copy)
        make_y(1, HALF_E, E, banks[4])
        make_y(2, 0, HALF_E, banks[5])
        make_y(2, HALF_E, E, banks[6])

        def weigh(step, r, rows, terms, n, j0=0, j1=RUNS):
            gathered = rows[n][:].indirect(pos_sb[2 * step + r][:, entries(j0 * P, j1 * P)])
            nc.vector.tensor_tensor(terms[r][n][:, runs(j0, j1)], gathered, gates[step][:, r, runs(j0, j1)], MULT)

        def pick(step, r, rows, terms, n, bank, j0, j1):
            gathered = rows[n][:].indirect(pos_sb[2 * step + r][:, entries(j0 * P, j1 * P)])
            nc.scalar.activation(terms[r][n][:, runs(j0, j1)], gathered, COPY)
            for j in range(j0, j1):
                nc.tensor.transpose(bank[:, run(j)], terms[r][n][:, run(j)], ident[:])

        def turn_gates(step, bank, j0):
            for r in range(2):
                for j in range(2):
                    nc.tensor.transpose(bank[:, run(2 * r + j)], gates[step][:, r, run(j0 + j)], ident[:])
            nc.scalar.copy(gate_columns[step][:], bank[:, 0 : RUNS * P : P])

        def weigh_turned(dst, bank, step, r, j0, j1):
            for j in range(j0, j1):
                nc.scalar.activation(dst[:, run(j)], bank[:, run(j)], COPY, scale=gate_columns[step][:, 2 * r + j : 2 * r + j + 1])

        def add_turned(bank, parts):
            for i, (columns, source) in enumerate(parts):
                first, final = i == 0, i == len(parts) - 1
                nc.tensor.matmul(
                    bank[:, columns], lhsT=source, rhs=ident[:], start=first, stop=final, is_transpose=True
                )

        c_terms = [[held.tile([P, T], F32, name="c_terms%d%d" % (r, n)) for n in range(TILES)] for r in range(2)]
        c_turned = held.tile([P, 2, RUNS, 2, P], BF16, name="c_turned")
        c_pair = [held.tile([P, width], F32, name="c_pair%d" % u) for u, width in enumerate((WINDOW, T))]
        second_term = held.tile([P, T], F32, name="second_term")

        nc.gpsimd.memset(c_pair[0][:, T:], 0.0)

        def sum_lower(n, bank):
            add_turned(bank, [(run(j), c_terms[r][n][:, run(j)]) for r in range(2) for j in range(RUNS)])
            nc.scalar.copy(
                c_turned[:, :, :, 0, n * P // 2 : (n + 1) * P // 2].rearrange("a u j (q i) -> a u j q i", i=2),
                bank[:].rearrange("a (j q u i) -> a u j q i", j=RUNS, u=2, i=2),
            )

        def sum_upper(u, j0, j1, bank):
            add_turned(bank, [(run(j), c_terms[r][2 + u][:, run(j)]) for r in range(2) for j in range(j0, j1)])
            nc.scalar.copy(c_turned[:, u, j0:j1, 1, :], bank[:, runs(j0, j1)].rearrange("a (j q) -> a j q", j=j1 - j0))

        def turn_back(u, j0, j1, bank):
            pair_view = c_turned[:, u].rearrange("a j h q -> a (j h q)").bitcast(F32)
            for j in range(j0, j1):
                nc.tensor.transpose(bank[:, run(j)], pair_view[:, run(j)], ident[:])
            nc.scalar.copy(c_pair[u][:, runs(j0, j1)], bank[:, runs(j0, j1)])

        reused = (E + SINGLY) * C
        staged_then_grouped = held.tile([P, reused + 2 * 2 * C], U32, name="staged_then_grouped", align_bytes=64)
        staged = staged_then_grouped[:, : 2 * S]
        grouped = [staged_then_grouped[:, reused:]] + [
            held.tile([P, 2 * 2 * C], U32, name="grouped%d" % e, align_bytes=64)[:] for e in range(2, E, 2)
        ]
        c_words = held.tile([P, S], U32, name="c_words", align_bytes=64)
        c_scales = held.tile([P, S], U8, name="c_scales", align_bytes=64)

        for n in range(2):
            weigh(0, 0, y, c_terms, n)
            weigh(0, 1, y, c_terms, n)
        weigh(0, 0, y, c_terms, 2, PICKED, RUNS)
        weigh(0, 1, y, c_terms, 2, PICKED, RUNS)
        turn_gates(0, banks[5], 0)
        pick(0, 1, y, c_terms, 2, banks[3], 0, PICKED)
        pick(0, 0, y, c_terms, 2, banks[4], 0, PICKED)
        weigh_turned(second_term, banks[3], 0, 1, 0, PICKED)
        for j in range(PICKED):
            nc.vector.scalar_tensor_tensor(
                c_turned[:, 0, j, 1, :],
                banks[4][:, run(j)],
                gate_columns[0][:, j : j + 1],
                second_term[:, run(j)],
                MULT,
                ADD,
            )
        make_y(3, 0, HALF_E, banks[7])
        make_y(3, HALF_E, E, banks[0])
        pieces = ((0, 2), (2, 3), (3, RUNS))
        weigh(0, 0, y, c_terms, 3)
        for j0, j1 in pieces:
            weigh(0, 1, y, c_terms, 3, j0, j1)
        sum_lower(0, banks[1])
        sum_lower(1, banks[2])
        sum_upper(0, PICKED, RUNS, banks[3])
        turn_back(0, 0, 2, banks[5])
        turn_back(0, 2, RUNS, banks[4])
        for (j0, j1), b in zip(pieces, (3, 5, 4)):
            sum_upper(1, j0, j1, banks[b])
        for (j0, j1), b in zip(pieces, (6, 7, 1)):
            turn_back(1, j0, j1, banks[b])

        def listed_pairs(u, e0, e1):
            return c_pair[u][:].bitcast(U32).indirect(offs2_sb[:, entries(e0 * C, e1 * C)])

        def stage(u, e0, e1):
            nc.vector.tensor_copy(staged[:, slots(u * E + e0, u * E + e1)], listed_pairs(u, e0, e1))

        def interleave(e0, e1):
            first = e0 % 2
            nc.scalar.copy(
                grouped[e0 // 2][:, slots(2 * first, 2 * (first + e1 - e0))].rearrange("p (s u) -> p s u", u=2),
                staged.rearrange("p (u s) -> p s u", u=2)[:, slots(e0, e1), :],
            )

        def quantize(e0, e1):
            first = e0 % 2
            nc.vector.quantize_mx(
                out=c_words[:, slots(e0, e1)].bitcast(FP8X4),
                scales=c_scales[:, slots(e0, e1)],
                in_=grouped[e0 // 2].bitcast(BF16)[:, slots(PACK * first, PACK * (first + e1 - e0))],
            )

        for e0 in (0, HALF_E):
            stage(0, e0, e0 + HALF_E)
        turn_gates(1, banks[6], 2)
        shares = ((0, 2), (2, HALF_E), (HALF_E, SINGLY), (SINGLY, LAST), (LAST, E))
        for e0, e1 in shares[:3]:
            stage(1, e0, e1)
            interleave(e0, e1)
        for e0, e1 in shares[:2]:
            quantize(e0, e1)
        for e0, e1 in shares[3:]:
            stage(1, e0, e1)
            interleave(e0, e1)
        for e0, e1 in shares[2:]:
            quantize(e0, e1)

        z = [held.tile([P, S], F32, name="z%d" % m) for m in range(TILES)]

        def make_z(tiles, e0, e1, bank, copy=nc.scalar.copy):
            width = e1 - e0
            for i, m in enumerate(tiles):
                for e in range(e0, e1) if e1 < E or m == 0 else reversed(range(e0, e1)):
                    words, scales = columns_in_order(e, m)
                    nc.tensor.matmul_mx(
                        bank[:, slots(i * width + e - e0, i * width + e - e0 + 1)],
                        lhsT=words,
                        lhsT_scale=scales,
                        rhs=c_words[:, slots(e, e + 1)].bitcast(FP8X4),
                        rhs_scale=c_scales[:, slots(e, e + 1)],
                        start=True,
                        stop=True,
                    )
            for i, m in enumerate(tiles):
                copy(z[m][:, slots(e0, e1)], bank[:, slots(i * width, (i + 1) * width)])

        make_z([0], 0, HALF_E, banks[0])
        make_z([0], HALF_E, SINGLY, banks[4], nc.vector.tensor_copy)
        make_z([0], SINGLY, E, banks[5], nc.vector.tensor_copy)
        make_z([1], 0, 2, banks[7])
        make_z([1], HALF_E, E, banks[1])
        make_z([1], 2, HALF_E, banks[4])
        make_z([2], HALF_E, E, banks[2])
        make_z([2], 0, HALF_E, banks[5])
        make_z([3], HALF_E, E, banks[3])
        make_z([3], 0, HALF_E, banks[1])

        out_terms = [[held.tile([P, T], F32, name="out_terms%d%d" % (r, m)) for m in range(TILES)] for r in range(2)]
        result = held.tile([P, TILES, T], F32, name="result")

        def add_and_store(m):
            tokens = runs(0, SHARED_FROM[m])
            nc.vector.tensor_tensor(result[:, m, tokens], out_terms[0][m][:, tokens], out_terms[1][m][:, tokens], ADD)
            nc.sync.dma_start(out[run(m), tokens], result[:, m, tokens])

        shared_runs = (3, 2)
        first_tile = {j: min(m for m in range(TILES) if SHARED_FROM[m] <= j) for j in shared_runs}
        term_banks = {(0, 3): banks[0], (0, 2): banks[7], (1, 3): banks[4], (1, 2): banks[2]}
        sum_banks = {3: banks[6], 2: banks[5]}
        for r in range(2):
            for m in range(2, TILES):
                j0 = SHARED_FROM[m]
                gathered = z[m][:].indirect(pos_sb[2 + r][:, entries(j0 * P, T)])
                nc.scalar.activation(out_terms[r][m][:, runs(j0, RUNS)], gathered, COPY)
                for j in range(j0, RUNS):
                    nc.tensor.transpose(term_banks[r, j][:, run(m)], out_terms[r][m][:, run(j)], ident[:])
        weighed = {}
        for r in range(2):
            for j in shared_runs:
                rows = runs(first_tile[j], TILES)
                weighed[r, j] = held.tile([P, T], F32, name="weighed%d%d" % (r, j))
                scale = gate_columns[1][:, 2 * r + j - 2 : 2 * r + j - 1]
                nc.scalar.activation(weighed[r, j][:, rows], term_banks[r, j][:, rows], COPY, scale=scale)
        for j in shared_runs:
            rows = runs(first_tile[j], TILES)
            add_turned(
                sum_banks[j],
                [(run(m), weighed[r, j][:, run(m)]) for r in range(2) for m in range(first_tile[j], TILES)],
            )
            summed = held.tile([P, T], F32, name="summed%d" % j)
            nc.scalar.copy(summed[:, rows], sum_banks[j][:, rows])
            nc.scalar.dma_start(
                out[rows, run(j)].rearrange("(m p) t -> p m t", p=P), summed[:, rows].rearrange("p (m t) -> p m t", t=P)
            )

        weigh(1, 0, z, out_terms, 0)
        weigh(1, 1, z, out_terms, 0)
        for m in range(1, TILES - 1):
            weigh(1, 0, z, out_terms, m, 0, SHARED_FROM[m])
            add_and_store(m - 1)
            weigh(1, 1, z, out_terms, m, 0, SHARED_FROM[m])
        for r in range(2):
            weigh(1, r, z, out_terms, TILES - 1, 0, SHARED_FROM[TILES - 1])
        add_and_store(TILES - 2)
        add_and_store(TILES - 1)
